import numpy as np
import ml_dtypes


def mxq(x, axis, fmt="e4m3"):
    dtype, down = {"e4m3": (ml_dtypes.float8_e4m3fn, 7), "e5m2": (ml_dtypes.float8_e5m2, 14)}[fmt]
    v = np.moveaxis(np.asarray(x, np.float32).astype(ml_dtypes.bfloat16).astype(np.float64), axis, -1)
    blocks = v.reshape(v.shape[:-1] + (-1, 32))
    amax = np.abs(blocks).max(-1, keepdims=True)
    byte = np.maximum(np.where(amax > 0, np.frexp(amax)[1] - 1 + 127, 0) - down, 1)
    scale = np.exp2(byte - 127.0)
    codes = (blocks / scale).astype(np.float32).astype(dtype).astype(np.float64)
    return np.moveaxis((codes * scale).reshape(v.shape), -1, axis)


WIDE = False


def mx_kscale(k):
    if not WIDE:
        return np.ones(k)
    levels = np.array([10, -10, 5, -5, 0])
    if k % 512:
        return np.exp2(np.random.permutation(np.resize(levels, k // 32))).repeat(32)
    a = np.empty((k // 512, 16))
    for p in range(k // 512):
        a[p, :8] = np.random.permutation(np.resize(levels, 8))
        for g in range(8):
            far = levels[np.abs(levels - a[p, g]) >= 10]
            a[p, g + 8] = far[np.random.randint(len(far))]
    return np.exp2(a.ravel()).repeat(32)


def f64(x):
    return np.asarray(x).astype(np.float64)


def striped(idx):
    return np.tile(idx.reshape(-1, 16).T, (8, 1)).astype(np.uint16)


def unstriped(offs):
    return offs[:16].T.reshape(-1).astype(np.int64)


def relu(v):
    return np.maximum(v, 0.0)


K, T, S, H, N, U, V = 1024, 2048, 1024, 512, 256, 1024, 512


def setup_inputs():
    n = np.random.standard_normal
    s = mx_kscale(K)[:, None]
    u = mx_kscale(H)
    return {
        "xT": (n((K, T)) * s).astype(np.float32),
        "w1": (n((K, H)) / np.sqrt(K) / s * u).astype(np.float32),
        "w2": (n((K, H)) / np.sqrt(K) / s * u).astype(np.float32),
        "w3": (n((H, N)) / np.sqrt(H) / u[:, None]).astype(np.float32),
        "offs": striped(np.random.permutation(T)[:S]),
        "near": striped(np.random.permutation(U)[:V]),
        "far": striped(np.random.permutation(U)[:V]),
    }


def reference(xT, w1, w2, w3, offs, near, far):
    xq = mxq(f64(xT)[:, unstriped(offs)], 0, "e4m3")
    a = np.zeros((H, S))
    a[:, unstriped(near)] = relu(mxq(f64(w1), 0, "e4m3").T @ xq[:, :V])
    e = np.zeros((H, S))
    e[:, unstriped(far)] = relu(mxq(f64(w2), 0, "e4m3").T @ xq[:, V:2 * V])
    z = np.maximum(a, e)
    return mxq(f64(w3), 0, "e4m3").T @ mxq(z, 0, "e4m3")

@@ -1,0 +1,214 @@
+from contextlib import ExitStack
+
+import concourse.mybir as mybir
+
+K, T, S, H, N, V = 1024, 2048, 1024, 512, 256, 512
+FLOPS = 2 * K * H * V * 2 + 2 * H * N * S
+
+F32 = mybir.dt.float32
+BF16 = mybir.dt.bfloat16
+I32 = mybir.dt.int32
+U32 = mybir.dt.uint32
+U16 = mybir.dt.uint16
+U8 = mybir.dt.uint8
+FP8X4 = mybir.dt.float8_e4m3fn_x4
+COPY = mybir.ActivationFunctionType.Copy
+RELU = mybir.ActivationFunctionType.Relu
+MAX = mybir.AluOpType.max
+
+P = 128
+PACK = 4
+K_PASS = P * PACK
+PASSES = K // K_PASS
+X_CHUNKS = ((512, 512, 512, 512), (512, 512, 512, 256, 256))
+SCALAR_COLS = {512: 320, 256: 96}
+CELLS = 256
+
+
+def tile_picked_bev_max_e_kernel(tc, xT, w1, w2, w3, offs, near, far, out):
+    nc = tc.nc
+    with ExitStack() as ctx:
+        keep = ctx.enter_context(tc.tile_pool(name="keep", bufs=1))
+        stage = ctx.enter_context(tc.tile_pool(name="stage", bufs=3))
+        psum = ctx.enter_context(tc.psum_pool(name="psum", bufs=2))
+
+        offs_sb = keep.tile([P, S // 16], U16, name="offs_sb")
+        near_sb = keep.tile([P, V // 16], U16, name="near_sb")
+        far_sb = keep.tile([P, V // 16], U16, name="far_sb")
+        lists = (near_sb, far_sb)
+
+        def load(src, g, c0, width, tag):
+            raw = keep.tile([P, PACK, width], F32, name=tag, tag=tag, align_bytes=64)
+            rows = src[g * K_PASS:(g + 1) * K_PASS, c0:c0 + width]
+            nc.sync.dma_start(out=raw[:], in_=rows.rearrange("(p j) w -> p j w", j=PACK))
+            return raw
+
+        def weave_views(grouped, raw, a, b):
+            dst = grouped[:, a:b, :].rearrange("p (c i) j -> p c j i", i=4)
+            src = raw[:, :, a:b].rearrange("p j (c i) -> p c j i", i=4)
+            return dst, src
+
+        x_scales = keep.tile([P, T], U8, name="x_scales", align_bytes=64)
+        nc.vector.memset(x_scales[:].bitcast(I32), 0)
+        windows = [[keep.tile([P, S], F32, name="win%d%d" % (s, t), tag="win%d%d" % (s, t)) for t in range(PACK)] for s in range(2)]
+        for s in range(2):
+            for t in range(PACK):
+                (nc.vector, nc.gpsimd)[s].memset(windows[s][t][:], 0.0)
+
+        x_codes = [keep.tile([P, T], U32, name="x_codes%d" % g, align_bytes=64) for g in range(PASSES)]
+        got_words = [[None, None], [None, None]]
+        got_bytes = [None, None]
+
+        def gather_words(g, s, tag):
+            got = keep.tile([P, V], U32, name="got_words%d%d" % (g, s), tag=tag, align_bytes=64)
+            nc.vector.tensor_copy(got[:], x_codes[g][:].indirect(offs_sb[:, 32 * s:32 * (s + 1)]))
+            got_words[g][s] = got
+
+        def gather_bytes(s, tag):
+            got = keep.tile([P, V], U8, name="got_bytes%d" % s, tag=tag, align_bytes=64)
+            nc.vector.tensor_copy(got[:], x_scales[:].indirect(offs_sb[:, 32 * s:32 * (s + 1)]))
+            got_bytes[s] = got
+
+        for g in range(PASSES):
+            c0 = 0
+            for i, width in enumerate(X_CHUNKS[g]):
+                raw = load(xT, g, c0, width, "x_raw%d%d" % (g, i))
+                if g == 0 and i == 2:
+                    nc.sync.dma_start(offs_sb[:], offs)
+                grouped = stage.tile([P, width, PACK], BF16, name="x_grouped", tag="x_grouped", align_bytes=64)
+                a = SCALAR_COLS[width]
+                dst, src = weave_views(grouped, raw, 0, a)
+                nc.scalar.activation(dst, src, COPY)
+                dst, src = weave_views(grouped, raw, a, width)
+                nc.vector.tensor_copy(dst, src)
+                nc.vector.quantize_mx(
+                    out=x_codes[g][:, c0:c0 + width].bitcast(FP8X4),
+                    scales=x_scales[4 * g:P, c0:c0 + width],
+                    in_=grouped[:].rearrange("p w j -> p (w j)"),
+                )
+                c0 += width
+            if g == 0:
+                gather_words(0, 0, "got_words00")
+                gather_words(0, 1, "got_words01")
+        gather_words(1, 0, "got_words10")
+        gather_bytes(0, "got_bytes0")
+
+        def deal(grouped, raw, m0, count):
+            dst = grouped[:].rearrange("p (t m j) -> p m j t", t=PACK, j=PACK)[:, m0:m0 + count]
+            src = raw[:].rearrange("p j (m t) -> p m j t", t=PACK)
+            nc.scalar.activation(dst, src, COPY)
+
+        w_codes = {}
+        w_scales = {}
+
+        def quantize_weights(s, g, grouped, t0, t1, tag):
+            width = P * (t1 - t0)
+            codes = keep.tile([P, width], U32, name="w_codes%d%d%d" % (s, g, t0), tag=tag, align_bytes=64)
+            scales = keep.tile([P, width], U8, name="w_scales%d%d%d" % (s, g, t0), align_bytes=64)
+            nc.vector.quantize_mx(out=codes[:].bitcast(FP8X4), scales=scales[:],
+                                  in_=grouped[:, t0 * K_PASS:t1 * K_PASS])
+            for t in range(t0, t1):
+                w_codes[s, g, t] = codes[:, (t - t0) * P:(t - t0 + 1) * P]
+                w_scales[s, g, t] = scales[:, (t - t0) * P:(t - t0 + 1) * P]
+
+        def layer(s, t):
+            acc = psum.tile([P, V], F32, name="acc", tag="acc%d" % s, bufs=(2, 4)[s])
+            for g in range(PASSES):
+                nc.tensor.matmul_mx(
+                    out=acc[:],
+                    lhsT=w_codes[s, g, t].bitcast(FP8X4), lhsT_scale=w_scales[s, g, t],
+                    rhs=got_words[g][s][:].bitcast(FP8X4), rhs_scale=got_bytes[s][4 * g:P, :],
+                    start=(g == 0), stop=(g == PASSES - 1),
+                )
+            return acc
+
+        def put(s, t, acc, packed):
+            nc.scalar.activation(packed[:, :], acc[:], RELU)
+            nc.vector.tensor_copy(windows[s][t][:].indirect(lists[s][:]), packed[:, :])
+
+        w1_grouped = [keep.tile([P, PACK * K_PASS], BF16, name="w1_grouped%d" % g, tag="w1_grouped%d" % g, align_bytes=64) for g in range(PASSES)]
+        for g in range(PASSES):
+            for half in range(2):
+                raw = load(w1, g, 256 * half, 256, "w1_raw%d%d" % (g, half))
+                deal(w1_grouped[g], raw, 64 * half, 64)
+        nc.sync.dma_start(near_sb[:], near)
+        nc.sync.dma_start(far_sb[:], far)
+        quantize_weights(0, 0, w1_grouped[0], 0, PACK, "w1p0")
+        gather_words(1, 1, "w1_grouped0")
+        for t in range(PACK):
+            quantize_weights(0, 1, w1_grouped[1], t, t + 1, "w1p1t%d" % t)
+        gather_bytes(1, "w1_grouped1")
+        accs = [layer(0, t) for t in range(2)]
+        early = keep.tile([P, 2, V], F32, name="early", tag="x_raw00", align_bytes=64)
+        put(0, 0, accs[0], early[:, 0, :])
+        put(0, 1, accs[1], early[:, 1, :])
+        accs = accs + [layer(0, t) for t in range(2, PACK)]
+
+        for g in range(PASSES):
+            raw = load(w2, g, 0, H, "w2_raw%d" % g)
+            grouped = keep.tile([P, PACK * K_PASS], BF16, name="w2_grouped%d" % g,
+                                tag=("w1p1t2", "w1p1t3")[g], align_bytes=64)
+            deal(grouped, raw, 0, P)
+            quantize_weights(1, g, grouped, 0, PACK, "w2p%d" % g)
+        late = keep.tile([P, 2, V], F32, name="late", tag="w2_raw1", align_bytes=64)
+        put(0, 2, accs[2], late[:, 0, :])
+        put(0, 3, accs[3], late[:, 1, :])
+        far_packed = keep.tile([P, PACK, V], F32, name="far_packed", tag="x_raw01", align_bytes=64)
+        for t in range(PACK):
+            put(1, t, layer(1, t), far_packed[:, t, :])
+
+        raw = load(w3, 0, 0, N, "w3_raw")
+        w3_grouped = keep.tile([P, N, PACK], BF16, name="w3_grouped", tag="w2_raw0", align_bytes=64)
+        dst, src = weave_views(w3_grouped, raw, 0, N)
+        nc.scalar.activation(dst, src, COPY)
+        w3_codes = keep.tile([P, N], U32, name="w3_codes", align_bytes=64)
+        w3_scales = keep.tile([P, N], U8, name="w3_scales", align_bytes=64)
+        nc.vector.quantize_mx(out=w3_codes[:].bitcast(FP8X4), scales=w3_scales[:],
+                              in_=w3_grouped[:].rearrange("p w j -> p (w j)"))
+
+        near_pairs = keep.tile([P, 2, S, 2], BF16, name="near_pairs", tag="w1_grouped0", align_bytes=64)
+        for t in range(PACK):
+            nc.scalar.activation(near_pairs[:, t // 2, :, t % 2], windows[0][t][:], COPY)
+        chunks = S // CELLS
+        far_all = keep.tile([P, chunks, 2, CELLS, 2], BF16, name="far_pairs", tag="win03")
+        far_pairs = [far_all[:, c] for c in range(chunks)]
+        for t in range(PACK):
+            for c in range(chunks):
+                nc.scalar.activation(far_pairs[c][:, t // 2, :, t % 2],
+                                     windows[1][t][:, c * CELLS:(c + 1) * CELLS], COPY)
+
+        out_view = out.rearrange("(h p) r -> p h r", p=P)
+        z_all = keep.tile([P, chunks, CELLS, 2, 2], BF16, name="z_all", tag="x_raw02", align_bytes=64)
+        res_all = keep.tile([P, chunks, 2, CELLS], F32, name="res_all", tag="x_raw03", align_bytes=64)
+        for c in range(chunks):
+            cells = slice(c * CELLS, (c + 1) * CELLS)
+            z = z_all[:, c]
+            res = res_all[:, c]
+            nc.vector.tensor_tensor(z, far_pairs[c].rearrange("p u r e -> p r u e"),
+                                    near_pairs[:, :, cells, :].rearrange("p u r e -> p r u e"), MAX)
+            z_codes = keep.tile([P, CELLS], U32, name="z_codes%d" % c, align_bytes=64)
+            z_scales = keep.tile([P, CELLS], U8, name="z_scales%d" % c, align_bytes=64)
+            nc.vector.quantize_mx(out=z_codes[:].bitcast(FP8X4), scales=z_scales[:],
+                                  in_=z.rearrange("p r u e -> p (r u e)"))
+            last = c == chunks - 1
+            if last:
+                banks = [psum.tile([P, V], F32, name="acc", tag="acc0", bufs=2) for h in range(2)]
+                parts = [banks[h][:, 0:CELLS] for h in range(2)]
+            else:
+                bank = psum.tile([P, V], F32, name="acc", tag="acc_out", bufs=2)
+                parts = [bank[:, h * CELLS:(h + 1) * CELLS] for h in range(2)]
+            for h in range(2):
+                nc.tensor.matmul_mx(
+                    out=parts[h],
+                    lhsT=w3_codes[:, h * P:(h + 1) * P].bitcast(FP8X4), lhsT_scale=w3_scales[:, h * P:(h + 1) * P],
+                    rhs=z_codes[:].bitcast(FP8X4), rhs_scale=z_scales[:],
+                    start=True, stop=True,
+                )
+            if last:
+                nc.scalar.activation(res[:, 0, :], parts[0], COPY)
+                nc.vector.tensor_copy(res[:, 1, :], parts[1])
+                nc.scalar.dma_start(out=out_view[:, 0, cells], in_=res[:, 0, :])
+                nc.sync.dma_start(out=out_view[:, 1, cells], in_=res[:, 1, :])
+            else:
+                nc.scalar.activation(res.rearrange("p h r -> p (h r)"), bank[:], COPY)
+                nc.sync.dma_start(out=out_view[:, :, cells], in_=res)

@@ -20,9 +20,9 @@ P = 128
 PACK = 4
 K_PASS = P * PACK
 PASSES = K // K_PASS
-X_CHUNKS = ((512, 512, 512, 512), (512, 512, 512, 256, 256))
-SCALAR_COLS = {512: 320, 256: 96}
-CELLS = 256
+X_CHUNKS = (((512, 320), (512, 320), (512, 256), (512, 64)),
+            ((512, 512), (512, 320), (512, 256), (256, 192), (256, 192)))
+CELL_CHUNKS = (128, 256, 256, 256, 128)
 
 
 def tile_picked_bev_max_e_kernel(tc, xT, w1, w2, w3, offs, near, far, out):
@@ -71,16 +71,16 @@ def tile_picked_bev_max_e_kernel(tc, xT, w1, w2, w3, offs, near, far, out):
 
         for g in range(PASSES):
             c0 = 0
-            for i, width in enumerate(X_CHUNKS[g]):
+            for i, (width, a) in enumerate(X_CHUNKS[g]):
                 raw = load(xT, g, c0, width, "x_raw%d%d" % (g, i))
                 if g == 0 and i == 2:
                     nc.sync.dma_start(offs_sb[:], offs)
                 grouped = stage.tile([P, width, PACK], BF16, name="x_grouped", tag="x_grouped", align_bytes=64)
-                a = SCALAR_COLS[width]
                 dst, src = weave_views(grouped, raw, 0, a)
                 nc.scalar.activation(dst, src, COPY)
-                dst, src = weave_views(grouped, raw, a, width)
-                nc.vector.tensor_copy(dst, src)
+                if a < width:
+                    dst, src = weave_views(grouped, raw, a, width)
+                    nc.vector.tensor_copy(dst, src)
                 nc.vector.quantize_mx(
                     out=x_codes[g][:, c0:c0 + width].bitcast(FP8X4),
                     scales=x_scales[4 * g:P, c0:c0 + width],
@@ -139,20 +139,20 @@ def tile_picked_bev_max_e_kernel(tc, xT, w1, w2, w3, offs, near, far, out):
             quantize_weights(0, 1, w1_grouped[1], t, t + 1, "w1p1t%d" % t)
         gather_bytes(1, "w1_grouped1")
         accs = [layer(0, t) for t in range(2)]
-        early = keep.tile([P, 2, V], F32, name="early", tag="x_raw00", align_bytes=64)
+        early = keep.tile([P, 3, V], F32, name="early", tag="x_raw00", align_bytes=64)
         put(0, 0, accs[0], early[:, 0, :])
         put(0, 1, accs[1], early[:, 1, :])
         accs = accs + [layer(0, t) for t in range(2, PACK)]
+        put(0, 2, accs[2], early[:, 2, :])
 
         for g in range(PASSES):
             raw = load(w2, g, 0, H, "w2_raw%d" % g)
             grouped = keep.tile([P, PACK * K_PASS], BF16, name="w2_grouped%d" % g,
-                                tag=("w1p1t2", "w1p1t3")[g], align_bytes=64)
+                                tag=("w1p1t3", "w2_raw0")[g], align_bytes=64)
             deal(grouped, raw, 0, P)
             quantize_weights(1, g, grouped, 0, PACK, "w2p%d" % g)
-        late = keep.tile([P, 2, V], F32, name="late", tag="w2_raw1", align_bytes=64)
-        put(0, 2, accs[2], late[:, 0, :])
-        put(0, 3, accs[3], late[:, 1, :])
+        late = keep.tile([P, V], F32, name="late", tag="w2_raw1", align_bytes=64)
+        put(0, 3, accs[3], late)
         far_packed = keep.tile([P, PACK, V], F32, name="far_packed", tag="x_raw01", align_bytes=64)
         for t in range(PACK):
             put(1, t, layer(1, t), far_packed[:, t, :])
@@ -161,7 +161,7 @@ def tile_picked_bev_max_e_kernel(tc, xT, w1, w2, w3, offs, near, far, out):
         w3_grouped = keep.tile([P, N, PACK], BF16, name="w3_grouped", tag="w2_raw0", align_bytes=64)
         dst, src = weave_views(w3_grouped, raw, 0, N)
         nc.scalar.activation(dst, src, COPY)
-        w3_codes = keep.tile([P, N], U32, name="w3_codes", align_bytes=64)
+        w3_codes = keep.tile([P, N], U32, name="w3_codes", tag="x_raw01", align_bytes=64)
         w3_scales = keep.tile([P, N], U8, name="w3_scales", align_bytes=64)
         nc.vector.quantize_mx(out=w3_codes[:].bitcast(FP8X4), scales=w3_scales[:],
                               in_=w3_grouped[:].rearrange("p w j -> p (w j)"))
@@ -169,34 +169,34 @@ def tile_picked_bev_max_e_kernel(tc, xT, w1, w2, w3, offs, near, far, out):
         near_pairs = keep.tile([P, 2, S, 2], BF16, name="near_pairs", tag="w1_grouped0", align_bytes=64)
         for t in range(PACK):
             nc.scalar.activation(near_pairs[:, t // 2, :, t % 2], windows[0][t][:], COPY)
-        chunks = S // CELLS
-        far_all = keep.tile([P, chunks, 2, CELLS, 2], BF16, name="far_pairs", tag="win03")
-        far_pairs = [far_all[:, c] for c in range(chunks)]
+        starts = [sum(CELL_CHUNKS[:c]) for c in range(len(CELL_CHUNKS))]
+        far_all = keep.tile([P, PACK * S], BF16, name="far_pairs", tag="win03")
+        far_pairs = [far_all[:, PACK * r0:PACK * (r0 + n)].rearrange("p (u r e) -> p u r e", u=2, e=2)
+                     for r0, n in zip(starts, CELL_CHUNKS)]
         for t in range(PACK):
-            for c in range(chunks):
-                nc.scalar.activation(far_pairs[c][:, t // 2, :, t % 2],
-                                     windows[1][t][:, c * CELLS:(c + 1) * CELLS], COPY)
+            for c, (r0, n) in enumerate(zip(starts, CELL_CHUNKS)):
+                nc.scalar.activation(far_pairs[c][:, t // 2, :, t % 2], windows[1][t][:, r0:r0 + n], COPY)
 
         out_view = out.rearrange("(h p) r -> p h r", p=P)
-        z_all = keep.tile([P, chunks, CELLS, 2, 2], BF16, name="z_all", tag="x_raw02", align_bytes=64)
-        res_all = keep.tile([P, chunks, 2, CELLS], F32, name="res_all", tag="x_raw03", align_bytes=64)
-        for c in range(chunks):
-            cells = slice(c * CELLS, (c + 1) * CELLS)
-            z = z_all[:, c]
-            res = res_all[:, c]
-            nc.vector.tensor_tensor(z, far_pairs[c].rearrange("p u r e -> p r u e"),
+        z_all = keep.tile([P, PACK * S], BF16, name="z_all", tag="x_raw02", align_bytes=64)
+        res_all = keep.tile([P, 2 * S], F32, name="res_all", tag="x_raw03", align_bytes=64)
+        for c, (r0, n) in enumerate(zip(starts, CELL_CHUNKS)):
+            cells = slice(r0, r0 + n)
+            z = z_all[:, PACK * r0:PACK * (r0 + n)]
+            res = res_all[:, 2 * r0:2 * (r0 + n)]
+            nc.vector.tensor_tensor(z.rearrange("p (r u e) -> p r u e", u=2, e=2),
+                                    far_pairs[c].rearrange("p u r e -> p r u e"),
                                     near_pairs[:, :, cells, :].rearrange("p u r e -> p r u e"), MAX)
-            z_codes = keep.tile([P, CELLS], U32, name="z_codes%d" % c, align_bytes=64)
-            z_scales = keep.tile([P, CELLS], U8, name="z_scales%d" % c, align_bytes=64)
-            nc.vector.quantize_mx(out=z_codes[:].bitcast(FP8X4), scales=z_scales[:],
-                                  in_=z.rearrange("p r u e -> p (r u e)"))
-            last = c == chunks - 1
+            z_codes = keep.tile([P, n], U32, name="z_codes%d" % c, align_bytes=64)
+            z_scales = keep.tile([P, n], U8, name="z_scales%d" % c, align_bytes=64)
+            nc.vector.quantize_mx(out=z_codes[:].bitcast(FP8X4), scales=z_scales[:], in_=z)
+            last = c == len(CELL_CHUNKS) - 1
             if last:
                 banks = [psum.tile([P, V], F32, name="acc", tag="acc0", bufs=2) for h in range(2)]
-                parts = [banks[h][:, 0:CELLS] for h in range(2)]
+                parts = [banks[h][:, 0:n] for h in range(2)]
             else:
                 bank = psum.tile([P, V], F32, name="acc", tag="acc_out", bufs=2)
-                parts = [bank[:, h * CELLS:(h + 1) * CELLS] for h in range(2)]
+                parts = [bank[:, h * n:(h + 1) * n] for h in range(2)]
             for h in range(2):
                 nc.tensor.matmul_mx(
                     out=parts[h],
@@ -205,10 +205,10 @@ def tile_picked_bev_max_e_kernel(tc, xT, w1, w2, w3, offs, near, far, out):
                     start=True, stop=True,
                 )
             if last:
-                nc.scalar.activation(res[:, 0, :], parts[0], COPY)
-                nc.vector.tensor_copy(res[:, 1, :], parts[1])
-                nc.scalar.dma_start(out=out_view[:, 0, cells], in_=res[:, 0, :])
-                nc.sync.dma_start(out=out_view[:, 1, cells], in_=res[:, 1, :])
+                nc.scalar.activation(res[:, 0:n], parts[0], COPY)
+                nc.vector.tensor_copy(res[:, n:2 * n], parts[1])
+                nc.scalar.dma_start(out=out_view[:, 0, cells], in_=res[:, 0:n])
+                nc.sync.dma_start(out=out_view[:, 1, cells], in_=res[:, n:2 * n])
             else:
-                nc.scalar.activation(res.rearrange("p h r -> p (h r)"), bank[:], COPY)
-                nc.sync.dma_start(out=out_view[:, :, cells], in_=res)
+                nc.scalar.activation(res, bank[:, 0:2 * n], COPY)
+                nc.sync.dma_start(out=out_view[:, :, cells], in_=res.rearrange("p (h r) -> p h r", h=2))

@@ -20,9 +20,9 @@ P = 128
 PACK = 4
 K_PASS = P * PACK
 PASSES = K // K_PASS
-X_CHUNKS = (((512, 320), (512, 320), (512, 256), (512, 64)),
-            ((512, 512), (512, 320), (512, 256), (256, 192), (256, 192)))
-CELL_CHUNKS = (128, 256, 256, 256, 128)
+X_LOADS = ((((512, 320),), ((512, 320),), ((512, 320),), ((512, 256),)),
+           (((512, 512),), ((512, 256),), ((256, 192),), ((256, 192),), ((256, 192),), ((128, 0),), ((128, 128),)))
+CELL_CHUNKS = (128, 256, 256, 128, 128, 128)
 
 
 def tile_picked_bev_max_e_kernel(tc, xT, w1, w2, w3, offs, near, far, out):
@@ -43,9 +43,9 @@ def tile_picked_bev_max_e_kernel(tc, xT, w1, w2, w3, offs, near, far, out):
             nc.sync.dma_start(out=raw[:], in_=rows.rearrange("(p j) w -> p j w", j=PACK))
             return raw
 
-        def weave_views(grouped, raw, a, b):
+        def weave_views(grouped, raw, r0, a, b):
             dst = grouped[:, a:b, :].rearrange("p (c i) j -> p c j i", i=4)
-            src = raw[:, :, a:b].rearrange("p j (c i) -> p c j i", i=4)
+            src = raw[:, :, r0 + a:r0 + b].rearrange("p j (c i) -> p c j i", i=4)
             return dst, src
 
         x_scales = keep.tile([P, T], U8, name="x_scales", align_bytes=64)
@@ -71,45 +71,49 @@ def tile_picked_bev_max_e_kernel(tc, xT, w1, w2, w3, offs, near, far, out):
 
         for g in range(PASSES):
             c0 = 0
-            for i, (width, a) in enumerate(X_CHUNKS[g]):
-                raw = load(xT, g, c0, width, "x_raw%d%d" % (g, i))
+            for i, steps in enumerate(X_LOADS[g]):
+                raw = load(xT, g, c0, sum(w for w, a in steps), "x_raw%d%d" % (g, i))
                 if g == 0 and i == 2:
                     nc.sync.dma_start(offs_sb[:], offs)
-                grouped = stage.tile([P, width, PACK], BF16, name="x_grouped", tag="x_grouped", align_bytes=64)
-                dst, src = weave_views(grouped, raw, 0, a)
-                nc.scalar.activation(dst, src, COPY)
-                if a < width:
-                    dst, src = weave_views(grouped, raw, a, width)
-                    nc.vector.tensor_copy(dst, src)
-                nc.vector.quantize_mx(
-                    out=x_codes[g][:, c0:c0 + width].bitcast(FP8X4),
-                    scales=x_scales[4 * g:P, c0:c0 + width],
-                    in_=grouped[:].rearrange("p w j -> p (w j)"),
-                )
-                c0 += width
+                r0 = 0
+                for width, a in steps:
+                    grouped = stage.tile([P, width, PACK], BF16, name="x_grouped", tag="x_grouped", align_bytes=64)
+                    if a > 0:
+                        dst, src = weave_views(grouped, raw, r0, 0, a)
+                        nc.scalar.activation(dst, src, COPY)
+                    if a < width:
+                        dst, src = weave_views(grouped, raw, r0, a, width)
+                        nc.vector.tensor_copy(dst, src)
+                    nc.vector.quantize_mx(
+                        out=x_codes[g][:, c0:c0 + width].bitcast(FP8X4),
+                        scales=x_scales[4 * g:P, c0:c0 + width],
+                        in_=grouped[:].rearrange("p w j -> p (w j)"),
+                    )
+                    c0 += width
+                    r0 += width
             if g == 0:
                 gather_words(0, 0, "got_words00")
                 gather_words(0, 1, "got_words01")
         gather_words(1, 0, "got_words10")
         gather_bytes(0, "got_bytes0")
 
-        def deal(grouped, raw, m0, count):
-            dst = grouped[:].rearrange("p (t m j) -> p m j t", t=PACK, j=PACK)[:, m0:m0 + count]
-            src = raw[:].rearrange("p j (m t) -> p m j t", t=PACK)
+        def deal(grouped, raw, t):
+            dst = grouped.rearrange("p (c i j) -> p c j i", i=4, j=PACK)
+            src = raw[:].rearrange("p j (c t i) -> p t c j i", t=PACK, i=4)[:, t]
             nc.scalar.activation(dst, src, COPY)
 
         w_codes = {}
         w_scales = {}
 
-        def quantize_weights(s, g, grouped, t0, t1, tag):
-            width = P * (t1 - t0)
-            codes = keep.tile([P, width], U32, name="w_codes%d%d%d" % (s, g, t0), tag=tag, align_bytes=64)
-            scales = keep.tile([P, width], U8, name="w_scales%d%d%d" % (s, g, t0), align_bytes=64)
-            nc.vector.quantize_mx(out=codes[:].bitcast(FP8X4), scales=scales[:],
-                                  in_=grouped[:, t0 * K_PASS:t1 * K_PASS])
-            for t in range(t0, t1):
-                w_codes[s, g, t] = codes[:, (t - t0) * P:(t - t0 + 1) * P]
-                w_scales[s, g, t] = scales[:, (t - t0) * P:(t - t0 + 1) * P]
+        def quantize_weights(s, parts, grouped, tag):
+            width = P * len(parts)
+            name = "%d%d%d" % ((s,) + parts[0])
+            codes = keep.tile([P, width], U32, name="w_codes" + name, tag=tag, align_bytes=64)
+            scales = keep.tile([P, width], U8, name="w_scales" + name, tag="w_scales" + name, align_bytes=64)
+            nc.vector.quantize_mx(out=codes[:].bitcast(FP8X4), scales=scales[:], in_=grouped)
+            for n, (g, t) in enumerate(parts):
+                w_codes[s, g, t] = codes[:, n * P:(n + 1) * P]
+                w_scales[s, g, t] = scales[:, n * P:(n + 1) * P]
 
         def layer(s, t):
             acc = psum.tile([P, V], F32, name="acc", tag="acc%d" % s, bufs=(2, 4)[s])
@@ -126,76 +130,103 @@ def tile_picked_bev_max_e_kernel(tc, xT, w1, w2, w3, offs, near, far, out):
             nc.scalar.activation(packed[:, :], acc[:], RELU)
             nc.vector.tensor_copy(windows[s][t][:].indirect(lists[s][:]), packed[:, :])
 
-        w1_grouped = [keep.tile([P, PACK * K_PASS], BF16, name="w1_grouped%d" % g, tag="w1_grouped%d" % g, align_bytes=64) for g in range(PASSES)]
-        for g in range(PASSES):
-            for half in range(2):
-                raw = load(w1, g, 256 * half, 256, "w1_raw%d%d" % (g, half))
-                deal(w1_grouped[g], raw, 64 * half, 64)
+        w1_raw = [load(w1, g, 0, H, "w1_raw%d" % g) for g in range(PASSES)]
         nc.sync.dma_start(near_sb[:], near)
         nc.sync.dma_start(far_sb[:], far)
-        quantize_weights(0, 0, w1_grouped[0], 0, PACK, "w1p0")
-        gather_words(1, 1, "w1_grouped0")
-        for t in range(PACK):
-            quantize_weights(0, 1, w1_grouped[1], t, t + 1, "w1p1t%d" % t)
-        gather_bytes(1, "w1_grouped1")
-        accs = [layer(0, t) for t in range(2)]
+
+        def near_weights(parts, tag=None):
+            name = "w1_grouped%d%d" % parts[0]
+            grouped = keep.tile([P, len(parts) * K_PASS], BF16, name=name, tag=tag or name, align_bytes=64)
+            for n, (g, t) in enumerate(parts):
+                deal(grouped[:, n * K_PASS:(n + 1) * K_PASS], w1_raw[g], t)
+            quantize_weights(0, parts, grouped[:], "w1p%dt%d" % parts[0])
+
+        near_weights([(0, 0)])
+        gather_words(1, 1, "w1_grouped00")
+        near_weights([(1, 0)])
+        gather_bytes(1, "w1_grouped10")
+        near_weights([(0, 1), (1, 1)])
+        near_weights([(0, 2), (1, 2)])
         early = keep.tile([P, 3, V], F32, name="early", tag="x_raw00", align_bytes=64)
-        put(0, 0, accs[0], early[:, 0, :])
-        put(0, 1, accs[1], early[:, 1, :])
-        accs = accs + [layer(0, t) for t in range(2, PACK)]
-        put(0, 2, accs[2], early[:, 2, :])
+        put(0, 0, layer(0, 0), early[:, 0, :])
+        near_weights([(0, 3), (1, 3)], "w1p1t0")
+        put(0, 1, layer(0, 1), early[:, 1, :])
+        put(0, 2, layer(0, 2), early[:, 2, :])
+        last_near = layer(0, 3)
 
         for g in range(PASSES):
             raw = load(w2, g, 0, H, "w2_raw%d" % g)
             grouped = keep.tile([P, PACK * K_PASS], BF16, name="w2_grouped%d" % g,
-                                tag=("w1p1t3", "w2_raw0")[g], align_bytes=64)
-            deal(grouped, raw, 0, P)
-            quantize_weights(1, g, grouped, 0, PACK, "w2p%d" % g)
+                                tag=("w_scales010", "w2_grouped1")[g], align_bytes=64)
+            for t in range(PACK):
+                deal(grouped[:, t * K_PASS:(t + 1) * K_PASS], raw, t)
+            quantize_weights(1, [(g, t) for t in range(PACK)], grouped[:], "w2p%d" % g)
         late = keep.tile([P, V], F32, name="late", tag="w2_raw1", align_bytes=64)
-        put(0, 3, accs[3], late)
-        far_packed = keep.tile([P, PACK, V], F32, name="far_packed", tag="x_raw01", align_bytes=64)
+        put(0, 3, last_near, late)
+        near_pairs = keep.tile([P, 2, S, 2], BF16, name="near_pairs", tag="w2_raw0", align_bytes=64)
+        for t in range(2):
+            nc.scalar.activation(near_pairs[:, t // 2, :, t % 2], windows[0][t][:], COPY)
+        far_packed = keep.tile([P, PACK, V], F32, name="far_packed", tag="x_raw10", align_bytes=64)
         for t in range(PACK):
             put(1, t, layer(1, t), far_packed[:, t, :])
 
-        raw = load(w3, 0, 0, N, "w3_raw")
-        w3_grouped = keep.tile([P, N, PACK], BF16, name="w3_grouped", tag="w2_raw0", align_bytes=64)
-        dst, src = weave_views(w3_grouped, raw, 0, N)
+        raw = keep.tile([P, PACK, N], F32, name="w3_raw", align_bytes=64)
+        w3_rows = w3.rearrange("(c t i) n -> i c t n", t=PACK, i=4)
+        for i in range(4):
+            nc.sync.dma_start(out=raw[i:P:4], in_=w3_rows[i])
+        w3_grouped = keep.tile([P, N, PACK], BF16, name="w3_grouped", tag="w2_grouped1", align_bytes=64)
+        dst, src = weave_views(w3_grouped, raw, 0, 0, N)
         nc.scalar.activation(dst, src, COPY)
-        w3_codes = keep.tile([P, N], U32, name="w3_codes", tag="x_raw01", align_bytes=64)
+        w3_codes = keep.tile([P, N], U32, name="w3_codes", tag="x_raw10", align_bytes=64)
         w3_scales = keep.tile([P, N], U8, name="w3_scales", align_bytes=64)
         nc.vector.quantize_mx(out=w3_codes[:].bitcast(FP8X4), scales=w3_scales[:],
                               in_=w3_grouped[:].rearrange("p w j -> p (w j)"))
 
-        near_pairs = keep.tile([P, 2, S, 2], BF16, name="near_pairs", tag="w1_grouped0", align_bytes=64)
-        for t in range(PACK):
+        for t in range(2, PACK):
             nc.scalar.activation(near_pairs[:, t // 2, :, t % 2], windows[0][t][:], COPY)
         starts = [sum(CELL_CHUNKS[:c]) for c in range(len(CELL_CHUNKS))]
         far_all = keep.tile([P, PACK * S], BF16, name="far_pairs", tag="win03")
         far_pairs = [far_all[:, PACK * r0:PACK * (r0 + n)].rearrange("p (u r e) -> p u r e", u=2, e=2)
                      for r0, n in zip(starts, CELL_CHUNKS)]
-        for t in range(PACK):
-            for c, (r0, n) in enumerate(zip(starts, CELL_CHUNKS)):
-                nc.scalar.activation(far_pairs[c][:, t // 2, :, t % 2], windows[1][t][:, r0:r0 + n], COPY)
+        for t in range(PACK - 1):
+            for r0, r1, n in ((0, 128, 128), (128, 640, 256), (640, S, 128)):
+                dst = far_all[:, PACK * r0:PACK * r1].rearrange("p (c u r e) -> p c u r e", u=2, r=n, e=2)
+                nc.scalar.activation(dst[:, :, t // 2, :, t % 2],
+                                     windows[1][t][:, r0:r1].rearrange("p (c r) -> p c r", r=n), COPY)
+        for c, (r0, n) in enumerate(zip(starts, CELL_CHUNKS)):
+            nc.scalar.activation(far_pairs[c][:, 1, :, 1], windows[1][3][:, r0:r0 + n], COPY)
 
         out_view = out.rearrange("(h p) r -> p h r", p=P)
-        z_all = keep.tile([P, PACK * S], BF16, name="z_all", tag="x_raw02", align_bytes=64)
-        res_all = keep.tile([P, 2 * S], F32, name="res_all", tag="x_raw03", align_bytes=64)
-        for c, (r0, n) in enumerate(zip(starts, CELL_CHUNKS)):
+        z_all = keep.tile([P, PACK * S], BF16, name="z_all", tag="x_raw01", align_bytes=64)
+        res_all = keep.tile([P, 2 * S], F32, name="res_all", tag="x_raw11", align_bytes=64)
+
+        emptied = []
+
+        def join(c):
+            r0, n = starts[c], CELL_CHUNKS[c]
+            z = z_all[:, PACK * r0:PACK * (r0 + n)]
+            nc.vector.tensor_tensor(z.rearrange("p (r u e) -> p r u e", u=2, e=2),
+                                    far_pairs[c].rearrange("p u r e -> p r u e"),
+                                    near_pairs[:, :, r0:r0 + n, :].rearrange("p u r e -> p r u e"), MAX)
+
+        def finish(c):
+            r0, n = starts[c], CELL_CHUNKS[c]
             cells = slice(r0, r0 + n)
             z = z_all[:, PACK * r0:PACK * (r0 + n)]
             res = res_all[:, 2 * r0:2 * (r0 + n)]
-            nc.vector.tensor_tensor(z.rearrange("p (r u e) -> p r u e", u=2, e=2),
-                                    far_pairs[c].rearrange("p u r e -> p r u e"),
-                                    near_pairs[:, :, cells, :].rearrange("p u r e -> p r u e"), MAX)
             z_codes = keep.tile([P, n], U32, name="z_codes%d" % c, align_bytes=64)
             z_scales = keep.tile([P, n], U8, name="z_scales%d" % c, align_bytes=64)
             nc.vector.quantize_mx(out=z_codes[:].bitcast(FP8X4), scales=z_scales[:], in_=z)
             last = c == len(CELL_CHUNKS) - 1
             if last:
+                for held, held_bank, held_cells in emptied:
+                    nc.vector.tensor_copy(held, held_bank[:, 0:2 * n])
+                    nc.sync.dma_start(out=out_view[:, :, held_cells], in_=held.rearrange("p (h r) -> p h r", h=2))
+            if last:
                 banks = [psum.tile([P, V], F32, name="acc", tag="acc0", bufs=2) for h in range(2)]
                 parts = [banks[h][:, 0:n] for h in range(2)]
             else:
-                bank = psum.tile([P, V], F32, name="acc", tag="acc_out", bufs=2)
+                bank = psum.tile([P, V], F32, name="acc", tag=("acc_out", "acc1")[c >= 2], bufs=(2, 4)[c >= 2])
                 parts = [bank[:, h * n:(h + 1) * n] for h in range(2)]
             for h in range(2):
                 nc.tensor.matmul_mx(
@@ -207,8 +238,15 @@ def tile_picked_bev_max_e_kernel(tc, xT, w1, w2, w3, offs, near, far, out):
             if last:
                 nc.scalar.activation(res[:, 0:n], parts[0], COPY)
                 nc.vector.tensor_copy(res[:, n:2 * n], parts[1])
-                nc.scalar.dma_start(out=out_view[:, 0, cells], in_=res[:, 0:n])
-                nc.sync.dma_start(out=out_view[:, 1, cells], in_=res[:, n:2 * n])
+            elif c == len(CELL_CHUNKS) - 3:
+                emptied.append((res, bank, cells))
+                return
             else:
                 nc.scalar.activation(res, bank[:, 0:2 * n], COPY)
-                nc.sync.dma_start(out=out_view[:, :, cells], in_=res.rearrange("p (h r) -> p h r", h=2))
+            nc.sync.dma_start(out=out_view[:, :, cells], in_=res.rearrange("p (h r) -> p h r", h=2))
+
+        join(0)
+        for c in range(1, len(CELL_CHUNKS)):
+            join(c)
+            finish(c - 1)
+        finish(len(CELL_CHUNKS) - 1)

@@ -20,8 +20,8 @@ P = 128
 PACK = 4
 K_PASS = P * PACK
 PASSES = K // K_PASS
-X_LOADS = ((((512, 320),), ((512, 320),), ((512, 320),), ((512, 256),)),
-           (((512, 512),), ((512, 256),), ((256, 192),), ((256, 192),), ((256, 192),), ((128, 0),), ((128, 128),)))
+X_LOADS = ((((512, 320), (512, 320)), ((512, 320),), ((512, 256),)),
+           (((512, 256), (512, 320)), ((512, 256),), ((256, 128),), ((256, 160),)))
 CELL_CHUNKS = (128, 256, 256, 128, 128, 128)
 
 
@@ -73,7 +73,7 @@ def tile_picked_bev_max_e_kernel(tc, xT, w1, w2, w3, offs, near, far, out):
             c0 = 0
             for i, steps in enumerate(X_LOADS[g]):
                 raw = load(xT, g, c0, sum(w for w, a in steps), "x_raw%d%d" % (g, i))
-                if g == 0 and i == 2:
+                if g == 0 and i == 1:
                     nc.sync.dma_start(offs_sb[:], offs)
                 r0 = 0
                 for width, a in steps:

@@ -22,7 +22,7 @@ K_PASS = P * PACK
 PASSES = K // K_PASS
 X_LOADS = ((((512, 320), (512, 320)), ((512, 320),), ((512, 256),)),
            (((512, 256), (512, 320)), ((512, 256),), ((256, 128),), ((256, 160),)))
-CELL_CHUNKS = (128, 256, 256, 128, 128, 128)
+CELL_CHUNKS = (128, 128, 256, 256, 128, 128)
 
 
 def tile_picked_bev_max_e_kernel(tc, xT, w1, w2, w3, offs, near, far, out):
@@ -62,7 +62,7 @@ def tile_picked_bev_max_e_kernel(tc, xT, w1, w2, w3, offs, near, far, out):
         def gather_words(g, s, tag):
             got = keep.tile([P, V], U32, name="got_words%d%d" % (g, s), tag=tag, align_bytes=64)
             nc.vector.tensor_copy(got[:], x_codes[g][:].indirect(offs_sb[:, 32 * s:32 * (s + 1)]))
-            got_words[g][s] = got
+            got_words[g][s] = got[:]
 
         def gather_bytes(s, tag):
             got = keep.tile([P, V], U8, name="got_bytes%d" % s, tag=tag, align_bytes=64)
@@ -92,8 +92,9 @@ def tile_picked_bev_max_e_kernel(tc, xT, w1, w2, w3, offs, near, far, out):
                     c0 += width
                     r0 += width
             if g == 0:
-                gather_words(0, 0, "got_words00")
-                gather_words(0, 1, "got_words01")
+                both = keep.tile([P, S], U32, name="got_words0", align_bytes=64)
+                nc.vector.tensor_copy(both[:], x_codes[0][:].indirect(offs_sb[:]))
+                got_words[0] = [both[:, 0:V], both[:, V:S]]
         gather_words(1, 0, "got_words10")
         gather_bytes(0, "got_bytes0")
 
@@ -121,7 +122,7 @@ def tile_picked_bev_max_e_kernel(tc, xT, w1, w2, w3, offs, near, far, out):
                 nc.tensor.matmul_mx(
                     out=acc[:],
                     lhsT=w_codes[s, g, t].bitcast(FP8X4), lhsT_scale=w_scales[s, g, t],
-                    rhs=got_words[g][s][:].bitcast(FP8X4), rhs_scale=got_bytes[s][4 * g:P, :],
+                    rhs=got_words[g][s].bitcast(FP8X4), rhs_scale=got_bytes[s][4 * g:P, :],
                     start=(g == 0), stop=(g == PASSES - 1),
                 )
             return acc
@@ -154,13 +155,12 @@ def tile_picked_bev_max_e_kernel(tc, xT, w1, w2, w3, offs, near, far, out):
         put(0, 2, layer(0, 2), early[:, 2, :])
         last_near = layer(0, 3)
 
-        for g in range(PASSES):
-            raw = load(w2, g, 0, H, "w2_raw%d" % g)
-            grouped = keep.tile([P, PACK * K_PASS], BF16, name="w2_grouped%d" % g,
-                                tag=("w_scales010", "w2_grouped1")[g], align_bytes=64)
-            for t in range(PACK):
-                deal(grouped[:, t * K_PASS:(t + 1) * K_PASS], raw, t)
-            quantize_weights(1, [(g, t) for t in range(PACK)], grouped[:], "w2p%d" % g)
+        w2_grouped = keep.tile([P, PASSES * PACK * K_PASS], BF16, name="w2_grouped", tag="w_scales010", align_bytes=64)
+        parts = [(g, t) for g in range(PASSES) for t in range(PACK)]
+        w2_raw = [load(w2, g, 0, H, "w2_raw%d" % g) for g in range(PASSES)]
+        for n, (g, t) in enumerate(parts):
+            deal(w2_grouped[:, n * K_PASS:(n + 1) * K_PASS], w2_raw[g], t)
+        quantize_weights(1, parts, w2_grouped[:], "w2_codes")
         late = keep.tile([P, V], F32, name="late", tag="w2_raw1", align_bytes=64)
         put(0, 3, last_near, late)
         near_pairs = keep.tile([P, 2, S, 2], BF16, name="near_pairs", tag="w2_raw0", align_bytes=64)
@@ -174,7 +174,7 @@ def tile_picked_bev_max_e_kernel(tc, xT, w1, w2, w3, offs, near, far, out):
         w3_rows = w3.rearrange("(c t i) n -> i c t n", t=PACK, i=4)
         for i in range(4):
             nc.sync.dma_start(out=raw[i:P:4], in_=w3_rows[i])
-        w3_grouped = keep.tile([P, N, PACK], BF16, name="w3_grouped", tag="w2_grouped1", align_bytes=64)
+        w3_grouped = keep.tile([P, N, PACK], BF16, name="w3_grouped", tag="w_scales010", align_bytes=64)
         dst, src = weave_views(w3_grouped, raw, 0, 0, N)
         nc.scalar.activation(dst, src, COPY)
         w3_codes = keep.tile([P, N], U32, name="w3_codes", tag="x_raw10", align_bytes=64)
@@ -189,7 +189,7 @@ def tile_picked_bev_max_e_kernel(tc, xT, w1, w2, w3, offs, near, far, out):
         far_pairs = [far_all[:, PACK * r0:PACK * (r0 + n)].rearrange("p (u r e) -> p u r e", u=2, e=2)
                      for r0, n in zip(starts, CELL_CHUNKS)]
         for t in range(PACK - 1):
-            for r0, r1, n in ((0, 128, 128), (128, 640, 256), (640, S, 128)):
+            for r0, r1, n in ((0, 256, 128), (256, 768, 256), (768, S, 128)):
                 dst = far_all[:, PACK * r0:PACK * r1].rearrange("p (c u r e) -> p c u r e", u=2, r=n, e=2)
                 nc.scalar.activation(dst[:, :, t // 2, :, t % 2],
                                      windows[1][t][:, r0:r1].rearrange("p (c r) -> p c r", r=n), COPY)
@@ -238,7 +238,7 @@ def tile_picked_bev_max_e_kernel(tc, xT, w1, w2, w3, offs, near, far, out):
             if last:
                 nc.scalar.activation(res[:, 0:n], parts[0], COPY)
                 nc.vector.tensor_copy(res[:, n:2 * n], parts[1])
-            elif c == len(CELL_CHUNKS) - 3:
+            elif c == len(CELL_CHUNKS) - 2:
                 emptied.append((res, bank, cells))
                 return
             else:

@@ -163,6 +163,13 @@ def tile_picked_bev_max_e_kernel(tc, xT, w1, w2, w3, offs, near, far, out):
         quantize_weights(1, parts, w2_grouped[:], "w2_codes")
         late = keep.tile([P, V], F32, name="late", tag="w2_raw1", align_bytes=64)
         put(0, 3, last_near, late)
+        raw = keep.tile([P, PACK, N], F32, name="w3_raw", align_bytes=64)
+        w3_rows = w3.rearrange("(c t i) n -> i c t n", t=PACK, i=4)
+        for i in range(4):
+            nc.sync.dma_start(out=raw[i:P:4], in_=w3_rows[i])
+        w3_grouped = keep.tile([P, N, PACK], BF16, name="w3_grouped", tag="w1p0t3", align_bytes=64)
+        dst, src = weave_views(w3_grouped, raw, 0, 0, N)
+        nc.scalar.activation(dst, src, COPY)
         near_pairs = keep.tile([P, 2, S, 2], BF16, name="near_pairs", tag="w2_raw0", align_bytes=64)
         for t in range(2):
             nc.scalar.activation(near_pairs[:, t // 2, :, t % 2], windows[0][t][:], COPY)
@@ -170,13 +177,6 @@ def tile_picked_bev_max_e_kernel(tc, xT, w1, w2, w3, offs, near, far, out):
         for t in range(PACK):
             put(1, t, layer(1, t), far_packed[:, t, :])
 
-        raw = keep.tile([P, PACK, N], F32, name="w3_raw", align_bytes=64)
-        w3_rows = w3.rearrange("(c t i) n -> i c t n", t=PACK, i=4)
-        for i in range(4):
-            nc.sync.dma_start(out=raw[i:P:4], in_=w3_rows[i])
-        w3_grouped = keep.tile([P, N, PACK], BF16, name="w3_grouped", tag="w_scales010", align_bytes=64)
-        dst, src = weave_views(w3_grouped, raw, 0, 0, N)
-        nc.scalar.activation(dst, src, COPY)
         w3_codes = keep.tile([P, N], U32, name="w3_codes", tag="x_raw10", align_bytes=64)
         w3_scales = keep.tile([P, N], U8, name="w3_scales", align_bytes=64)
         nc.vector.quantize_mx(out=w3_codes[:].bitcast(FP8X4), scales=w3_scales[:],

@@ -18,11 +18,17 @@ MAX = mybir.AluOpType.max
 
 P = 128
 PACK = 4
+RUN = 4
 K_PASS = P * PACK
 PASSES = K // K_PASS
-X_LOADS = ((((512, 320), (512, 320)), ((512, 320),), ((512, 256),)),
-           (((512, 256), (512, 320)), ((512, 256),), ((256, 128),), ((256, 160),)))
-CELL_CHUNKS = (128, 128, 256, 256, 128, 128)
+LIST_COLS = V // 16
+NEAR, FAR = 0, 1
+X_LOADS = ((1024, 512, 512), (1024, 512, 256, 256))
+X_STEP = 512
+SHARE_EVEN, SHARE_MORE = 4, 5
+CELLS = 128
+STEPS = S // CELLS
+LAST_PIECES = (1, 2, 4, STEPS)
 
 
 def tile_picked_bev_max_e_kernel(tc, xT, w1, w2, w3, offs, near, far, out):
@@ -33,85 +39,88 @@ def tile_picked_bev_max_e_kernel(tc, xT, w1, w2, w3, offs, near, far, out):
         psum = ctx.enter_context(tc.psum_pool(name="psum", bufs=2))
 
         offs_sb = keep.tile([P, S // 16], U16, name="offs_sb")
-        near_sb = keep.tile([P, V // 16], U16, name="near_sb")
-        far_sb = keep.tile([P, V // 16], U16, name="far_sb")
-        lists = (near_sb, far_sb)
+        near_sb = keep.tile([P, LIST_COLS], U16, name="near_sb")
+        far_sb = keep.tile([P, LIST_COLS], U16, name="far_sb")
+        cell_lists = (near_sb, far_sb)
 
-        def load(src, g, c0, width, tag):
+        def load_pass(src, g, c0, width, tag):
             raw = keep.tile([P, PACK, width], F32, name=tag, tag=tag, align_bytes=64)
             rows = src[g * K_PASS:(g + 1) * K_PASS, c0:c0 + width]
             nc.sync.dma_start(out=raw[:], in_=rows.rearrange("(p j) w -> p j w", j=PACK))
             return raw
 
         def weave_views(grouped, raw, r0, a, b):
-            dst = grouped[:, a:b, :].rearrange("p (c i) j -> p c j i", i=4)
-            src = raw[:, :, r0 + a:r0 + b].rearrange("p j (c i) -> p c j i", i=4)
+            dst = grouped[:, a:b, :].rearrange("p (c e) j -> p c j e", e=RUN)
+            src = raw[:, :, r0 + a:r0 + b].rearrange("p j (c e) -> p c j e", e=RUN)
             return dst, src
 
         x_scales = keep.tile([P, T], U8, name="x_scales", align_bytes=64)
         nc.vector.memset(x_scales[:].bitcast(I32), 0)
-        windows = [[keep.tile([P, S], F32, name="win%d%d" % (s, t), tag="win%d%d" % (s, t)) for t in range(PACK)] for s in range(2)]
-        for s in range(2):
+        windows = [[keep.tile([P, S], F32, name="win%d%d" % (s, t), tag="win%d%d" % (s, t)) for t in range(PACK)]
+                   for s in (NEAR, FAR)]
+        for s in (NEAR, FAR):
             for t in range(PACK):
                 (nc.vector, nc.gpsimd)[s].memset(windows[s][t][:], 0.0)
 
         x_codes = [keep.tile([P, T], U32, name="x_codes%d" % g, align_bytes=64) for g in range(PASSES)]
-        got_words = [[None, None], [None, None]]
-        got_bytes = [None, None]
+        got_words = {}
+        got_bytes = {}
 
         def gather_words(g, s, tag):
             got = keep.tile([P, V], U32, name="got_words%d%d" % (g, s), tag=tag, align_bytes=64)
-            nc.vector.tensor_copy(got[:], x_codes[g][:].indirect(offs_sb[:, 32 * s:32 * (s + 1)]))
-            got_words[g][s] = got[:]
+            nc.vector.tensor_copy(got[:], x_codes[g][:].indirect(offs_sb[:, LIST_COLS * s:LIST_COLS * (s + 1)]))
+            got_words[g, s] = got[:]
 
         def gather_bytes(s, tag):
             got = keep.tile([P, V], U8, name="got_bytes%d" % s, tag=tag, align_bytes=64)
-            nc.vector.tensor_copy(got[:], x_scales[:].indirect(offs_sb[:, 32 * s:32 * (s + 1)]))
+            nc.vector.tensor_copy(got[:], x_scales[:].indirect(offs_sb[:, LIST_COLS * s:LIST_COLS * (s + 1)]))
             got_bytes[s] = got
 
         for g in range(PASSES):
             c0 = 0
-            for i, steps in enumerate(X_LOADS[g]):
-                raw = load(xT, g, c0, sum(w for w, a in steps), "x_raw%d%d" % (g, i))
-                if g == 0 and i == 1:
+            for index, loaded in enumerate(X_LOADS[g]):
+                raw = load_pass(xT, g, c0, loaded, "x_raw%d%d" % (g, index))
+                if (g, index) == (0, 1):
                     nc.sync.dma_start(offs_sb[:], offs)
-                r0 = 0
-                for width, a in steps:
+                width = min(loaded, X_STEP)
+                for r0 in range(0, loaded, width):
+                    very_last = g == PASSES - 1 and c0 + loaded == T
+                    split = width * (SHARE_MORE if r0 > 0 or very_last else SHARE_EVEN) // 8
                     grouped = stage.tile([P, width, PACK], BF16, name="x_grouped", tag="x_grouped", align_bytes=64)
-                    if a > 0:
-                        dst, src = weave_views(grouped, raw, r0, 0, a)
-                        nc.scalar.activation(dst, src, COPY)
-                    if a < width:
-                        dst, src = weave_views(grouped, raw, r0, a, width)
-                        nc.vector.tensor_copy(dst, src)
+                    dst, src = weave_views(grouped, raw, r0, 0, split)
+                    nc.scalar.activation(dst, src, COPY)
+                    dst, src = weave_views(grouped, raw, r0, split, width)
+                    nc.vector.tensor_copy(dst, src)
                     nc.vector.quantize_mx(
-                        out=x_codes[g][:, c0:c0 + width].bitcast(FP8X4),
-                        scales=x_scales[4 * g:P, c0:c0 + width],
+                        out=x_codes[g][:, c0 + r0:c0 + r0 + width].bitcast(FP8X4),
+                        scales=x_scales[4 * g:P, c0 + r0:c0 + r0 + width],
                         in_=grouped[:].rearrange("p w j -> p (w j)"),
                     )
-                    c0 += width
-                    r0 += width
+                c0 += loaded
             if g == 0:
                 both = keep.tile([P, S], U32, name="got_words0", align_bytes=64)
                 nc.vector.tensor_copy(both[:], x_codes[0][:].indirect(offs_sb[:]))
-                got_words[0] = [both[:, 0:V], both[:, V:S]]
-        gather_words(1, 0, "got_words10")
-        gather_bytes(0, "got_bytes0")
+                got_words[0, NEAR] = both[:, 0:V]
+                got_words[0, FAR] = both[:, V:S]
+        gather_words(1, NEAR, "got_words10")
+        gather_bytes(NEAR, "got_bytes0")
 
         def deal(grouped, raw, t):
-            dst = grouped.rearrange("p (c i j) -> p c j i", i=4, j=PACK)
-            src = raw[:].rearrange("p j (c t i) -> p t c j i", t=PACK, i=4)[:, t]
+            dst = grouped.rearrange("p (c e j) -> p c j e", e=RUN, j=PACK)
+            src = raw[:].rearrange("p j (c t e) -> p t c j e", t=PACK, e=RUN)[:, t]
             nc.scalar.activation(dst, src, COPY)
 
         w_codes = {}
         w_scales = {}
 
-        def quantize_weights(s, parts, grouped, tag):
-            width = P * len(parts)
+        def prepare_weights(s, raws, parts, tag):
             name = "%d%d%d" % ((s,) + parts[0])
-            codes = keep.tile([P, width], U32, name="w_codes" + name, tag=tag, align_bytes=64)
-            scales = keep.tile([P, width], U8, name="w_scales" + name, tag="w_scales" + name, align_bytes=64)
-            nc.vector.quantize_mx(out=codes[:].bitcast(FP8X4), scales=scales[:], in_=grouped)
+            grouped = keep.tile([P, len(parts) * K_PASS], BF16, name="w_grouped" + name, tag=tag, align_bytes=64)
+            for n, (g, t) in enumerate(parts):
+                deal(grouped[:, n * K_PASS:(n + 1) * K_PASS], raws[g], t)
+            codes = keep.tile([P, len(parts) * P], U32, name="w_codes" + name, tag="w_codes" + name, align_bytes=64)
+            scales = keep.tile([P, len(parts) * P], U8, name="w_scales" + name, tag="w_scales" + name, align_bytes=64)
+            nc.vector.quantize_mx(out=codes[:].bitcast(FP8X4), scales=scales[:], in_=grouped[:])
             for n, (g, t) in enumerate(parts):
                 w_codes[s, g, t] = codes[:, n * P:(n + 1) * P]
                 w_scales[s, g, t] = scales[:, n * P:(n + 1) * P]
@@ -122,131 +131,113 @@ def tile_picked_bev_max_e_kernel(tc, xT, w1, w2, w3, offs, near, far, out):
                 nc.tensor.matmul_mx(
                     out=acc[:],
                     lhsT=w_codes[s, g, t].bitcast(FP8X4), lhsT_scale=w_scales[s, g, t],
-                    rhs=got_words[g][s].bitcast(FP8X4), rhs_scale=got_bytes[s][4 * g:P, :],
+                    rhs=got_words[g, s].bitcast(FP8X4), rhs_scale=got_bytes[s][4 * g:P, :],
                     start=(g == 0), stop=(g == PASSES - 1),
                 )
             return acc
 
         def put(s, t, acc, packed):
-            nc.scalar.activation(packed[:, :], acc[:], RELU)
-            nc.vector.tensor_copy(windows[s][t][:].indirect(lists[s][:]), packed[:, :])
+            nc.scalar.activation(packed, acc[:], RELU)
+            nc.vector.tensor_copy(windows[s][t][:].indirect(cell_lists[s][:]), packed)
 
-        w1_raw = [load(w1, g, 0, H, "w1_raw%d" % g) for g in range(PASSES)]
+        w1_raw = [load_pass(w1, g, 0, H, "w1_raw%d" % g) for g in range(PASSES)]
         nc.sync.dma_start(near_sb[:], near)
         nc.sync.dma_start(far_sb[:], far)
 
-        def near_weights(parts, tag=None):
-            name = "w1_grouped%d%d" % parts[0]
-            grouped = keep.tile([P, len(parts) * K_PASS], BF16, name=name, tag=tag or name, align_bytes=64)
-            for n, (g, t) in enumerate(parts):
-                deal(grouped[:, n * K_PASS:(n + 1) * K_PASS], w1_raw[g], t)
-            quantize_weights(0, parts, grouped[:], "w1p%dt%d" % parts[0])
+        prepare_weights(NEAR, w1_raw, [(0, 0)], "w1_grouped00")
+        gather_words(1, FAR, "w1_grouped00")
+        prepare_weights(NEAR, w1_raw, [(1, 0)], "w1_grouped10")
+        gather_bytes(FAR, "w1_grouped10")
+        prepare_weights(NEAR, w1_raw, [(0, 1), (1, 1)], "w1_grouped01")
+        prepare_weights(NEAR, w1_raw, [(0, 2), (1, 2)], "w1_grouped02")
+        near_packed = keep.tile([P, PACK - 1, V], F32, name="near_packed", tag="x_raw00", align_bytes=64)
+        put(NEAR, 0, layer(NEAR, 0), near_packed[:, 0, :])
+        prepare_weights(NEAR, w1_raw, [(0, 3), (1, 3)], "w_codes010")
+        put(NEAR, 1, layer(NEAR, 1), near_packed[:, 1, :])
+        put(NEAR, 2, layer(NEAR, 2), near_packed[:, 2, :])
+        last_near = layer(NEAR, 3)
 
-        near_weights([(0, 0)])
-        gather_words(1, 1, "w1_grouped00")
-        near_weights([(1, 0)])
-        gather_bytes(1, "w1_grouped10")
-        near_weights([(0, 1), (1, 1)])
-        near_weights([(0, 2), (1, 2)])
-        early = keep.tile([P, 3, V], F32, name="early", tag="x_raw00", align_bytes=64)
-        put(0, 0, layer(0, 0), early[:, 0, :])
-        near_weights([(0, 3), (1, 3)], "w1p1t0")
-        put(0, 1, layer(0, 1), early[:, 1, :])
-        put(0, 2, layer(0, 2), early[:, 2, :])
-        last_near = layer(0, 3)
+        w2_raw = [load_pass(w2, g, 0, H, "w2_raw%d" % g) for g in range(PASSES)]
+        prepare_weights(FAR, w2_raw, [(g, t) for g in range(PASSES) for t in range(PACK)], "w_scales010")
+        late_packed = keep.tile([P, V], F32, name="late_packed", tag="w2_raw1", align_bytes=64)
+        put(NEAR, 3, last_near, late_packed[:])
 
-        w2_grouped = keep.tile([P, PASSES * PACK * K_PASS], BF16, name="w2_grouped", tag="w_scales010", align_bytes=64)
-        parts = [(g, t) for g in range(PASSES) for t in range(PACK)]
-        w2_raw = [load(w2, g, 0, H, "w2_raw%d" % g) for g in range(PASSES)]
-        for n, (g, t) in enumerate(parts):
-            deal(w2_grouped[:, n * K_PASS:(n + 1) * K_PASS], w2_raw[g], t)
-        quantize_weights(1, parts, w2_grouped[:], "w2_codes")
-        late = keep.tile([P, V], F32, name="late", tag="w2_raw1", align_bytes=64)
-        put(0, 3, last_near, late)
-        raw = keep.tile([P, PACK, N], F32, name="w3_raw", align_bytes=64)
-        w3_rows = w3.rearrange("(c t i) n -> i c t n", t=PACK, i=4)
-        for i in range(4):
-            nc.sync.dma_start(out=raw[i:P:4], in_=w3_rows[i])
-        w3_grouped = keep.tile([P, N, PACK], BF16, name="w3_grouped", tag="w1p0t3", align_bytes=64)
-        dst, src = weave_views(w3_grouped, raw, 0, 0, N)
+        w3_raw = keep.tile([P, PACK, N], F32, name="w3_raw", align_bytes=64)
+        w3_rows = w3.rearrange("(c t e) n -> e c t n", t=PACK, e=RUN)
+        for e in range(RUN):
+            nc.sync.dma_start(out=w3_raw[e:P:RUN], in_=w3_rows[e])
+        w3_grouped = keep.tile([P, N, PACK], BF16, name="w3_grouped", tag="w_codes003", align_bytes=64)
+        dst, src = weave_views(w3_grouped, w3_raw, 0, 0, N)
         nc.scalar.activation(dst, src, COPY)
+
         near_pairs = keep.tile([P, 2, S, 2], BF16, name="near_pairs", tag="w2_raw0", align_bytes=64)
-        for t in range(2):
-            nc.scalar.activation(near_pairs[:, t // 2, :, t % 2], windows[0][t][:], COPY)
+
+        def round_near(t):
+            nc.scalar.activation(near_pairs[:, t // 2, :, t % 2], windows[NEAR][t][:], COPY)
+
+        round_near(0)
+        round_near(1)
         far_packed = keep.tile([P, PACK, V], F32, name="far_packed", tag="x_raw10", align_bytes=64)
         for t in range(PACK):
-            put(1, t, layer(1, t), far_packed[:, t, :])
+            put(FAR, t, layer(FAR, t), far_packed[:, t, :])
 
         w3_codes = keep.tile([P, N], U32, name="w3_codes", tag="x_raw10", align_bytes=64)
         w3_scales = keep.tile([P, N], U8, name="w3_scales", align_bytes=64)
         nc.vector.quantize_mx(out=w3_codes[:].bitcast(FP8X4), scales=w3_scales[:],
                               in_=w3_grouped[:].rearrange("p w j -> p (w j)"))
 
-        for t in range(2, PACK):
-            nc.scalar.activation(near_pairs[:, t // 2, :, t % 2], windows[0][t][:], COPY)
-        starts = [sum(CELL_CHUNKS[:c]) for c in range(len(CELL_CHUNKS))]
-        far_all = keep.tile([P, PACK * S], BF16, name="far_pairs", tag="win03")
-        far_pairs = [far_all[:, PACK * r0:PACK * (r0 + n)].rearrange("p (u r e) -> p u r e", u=2, e=2)
-                     for r0, n in zip(starts, CELL_CHUNKS)]
+        round_near(2)
+        round_near(3)
+        far_flat = keep.tile([P, PACK * S], BF16, name="far_pairs", tag="win03")
+        far_pairs = far_flat[:].rearrange("p (c u r v) -> p c u r v", u=2, r=CELLS, v=2)
+
+        def round_far(t, c0, c1):
+            src = windows[FAR][t][:, c0 * CELLS:c1 * CELLS].rearrange("p (c r) -> p c r", r=CELLS)
+            nc.scalar.activation(far_pairs[:, c0:c1, t // 2, :, t % 2], src, COPY)
+
         for t in range(PACK - 1):
-            for r0, r1, n in ((0, 256, 128), (256, 768, 256), (768, S, 128)):
-                dst = far_all[:, PACK * r0:PACK * r1].rearrange("p (c u r e) -> p c u r e", u=2, r=n, e=2)
-                nc.scalar.activation(dst[:, :, t // 2, :, t % 2],
-                                     windows[1][t][:, r0:r1].rearrange("p (c r) -> p c r", r=n), COPY)
-        for c, (r0, n) in enumerate(zip(starts, CELL_CHUNKS)):
-            nc.scalar.activation(far_pairs[c][:, 1, :, 1], windows[1][3][:, r0:r0 + n], COPY)
+            round_far(t, 0, STEPS)
+        for c0, c1 in zip((0,) + LAST_PIECES, LAST_PIECES):
+            round_far(PACK - 1, c0, c1)
 
         out_view = out.rearrange("(h p) r -> p h r", p=P)
-        z_all = keep.tile([P, PACK * S], BF16, name="z_all", tag="x_raw01", align_bytes=64)
-        res_all = keep.tile([P, 2 * S], F32, name="res_all", tag="x_raw11", align_bytes=64)
-
-        emptied = []
+        z_all = keep.tile([P, STEPS * CELLS * PACK], BF16, name="z_all", tag="x_raw01", align_bytes=64)
+        res_all = keep.tile([P, STEPS * 2 * CELLS], F32, name="res_all", tag="x_raw11", align_bytes=64)
 
         def join(c):
-            r0, n = starts[c], CELL_CHUNKS[c]
-            z = z_all[:, PACK * r0:PACK * (r0 + n)]
-            nc.vector.tensor_tensor(z.rearrange("p (r u e) -> p r u e", u=2, e=2),
-                                    far_pairs[c].rearrange("p u r e -> p r u e"),
-                                    near_pairs[:, :, r0:r0 + n, :].rearrange("p u r e -> p r u e"), MAX)
+            z = z_all[:, c * CELLS * PACK:(c + 1) * CELLS * PACK]
+            nc.vector.tensor_tensor(z.rearrange("p (r u v) -> p r u v", u=2, v=2),
+                                    far_pairs[:, c].rearrange("p u r v -> p r u v"),
+                                    near_pairs[:, :, c * CELLS:(c + 1) * CELLS, :].rearrange("p u r v -> p r u v"), MAX)
 
         def finish(c):
-            r0, n = starts[c], CELL_CHUNKS[c]
-            cells = slice(r0, r0 + n)
-            z = z_all[:, PACK * r0:PACK * (r0 + n)]
-            res = res_all[:, 2 * r0:2 * (r0 + n)]
-            z_codes = keep.tile([P, n], U32, name="z_codes%d" % c, align_bytes=64)
-            z_scales = keep.tile([P, n], U8, name="z_scales%d" % c, align_bytes=64)
-            nc.vector.quantize_mx(out=z_codes[:].bitcast(FP8X4), scales=z_scales[:], in_=z)
-            last = c == len(CELL_CHUNKS) - 1
+            z_codes = keep.tile([P, CELLS], U32, name="z_codes%d" % c, align_bytes=64)
+            z_scales = keep.tile([P, CELLS], U8, name="z_scales%d" % c, align_bytes=64)
+            nc.vector.quantize_mx(out=z_codes[:].bitcast(FP8X4), scales=z_scales[:],
+                                  in_=z_all[:, c * CELLS * PACK:(c + 1) * CELLS * PACK])
+            last = c == STEPS - 1
             if last:
-                for held, held_bank, held_cells in emptied:
-                    nc.vector.tensor_copy(held, held_bank[:, 0:2 * n])
-                    nc.sync.dma_start(out=out_view[:, :, held_cells], in_=held.rearrange("p (h r) -> p h r", h=2))
-            if last:
-                banks = [psum.tile([P, V], F32, name="acc", tag="acc0", bufs=2) for h in range(2)]
-                parts = [banks[h][:, 0:n] for h in range(2)]
+                halves = [psum.tile([P, V], F32, name="acc", tag="acc0", bufs=2)[:, 0:CELLS] for h in range(2)]
             else:
-                bank = psum.tile([P, V], F32, name="acc", tag=("acc_out", "acc1")[c >= 2], bufs=(2, 4)[c >= 2])
-                parts = [bank[:, h * n:(h + 1) * n] for h in range(2)]
+                bank = psum.tile([P, V], F32, name="acc", tag="acc1", bufs=4)
+                halves = [bank[:, h * CELLS:(h + 1) * CELLS] for h in range(2)]
             for h in range(2):
                 nc.tensor.matmul_mx(
-                    out=parts[h],
+                    out=halves[h],
                     lhsT=w3_codes[:, h * P:(h + 1) * P].bitcast(FP8X4), lhsT_scale=w3_scales[:, h * P:(h + 1) * P],
                     rhs=z_codes[:].bitcast(FP8X4), rhs_scale=z_scales[:],
                     start=True, stop=True,
                 )
+            res = res_all[:, c * 2 * CELLS:(c + 1) * 2 * CELLS]
             if last:
-                nc.scalar.activation(res[:, 0:n], parts[0], COPY)
-                nc.vector.tensor_copy(res[:, n:2 * n], parts[1])
-            elif c == len(CELL_CHUNKS) - 2:
-                emptied.append((res, bank, cells))
-                return
+                nc.scalar.activation(res[:, 0:CELLS], halves[0], COPY)
+                nc.vector.tensor_copy(res[:, CELLS:2 * CELLS], halves[1])
             else:
-                nc.scalar.activation(res, bank[:, 0:2 * n], COPY)
-            nc.sync.dma_start(out=out_view[:, :, cells], in_=res.rearrange("p (h r) -> p h r", h=2))
+                nc.scalar.activation(res, bank[:, 0:2 * CELLS], COPY)
+            nc.sync.dma_start(out=out_view[:, :, c * CELLS:(c + 1) * CELLS], in_=res.rearrange("p (h r) -> p h r", h=2))
 
         join(0)
-        for c in range(1, len(CELL_CHUNKS)):
+        for c in range(1, STEPS):
             join(c)
             finish(c - 1)
-        finish(len(CELL_CHUNKS) - 1)
+        finish(STEPS - 1)

@@ -23,9 +23,8 @@ K_PASS = P * PACK
 PASSES = K // K_PASS
 LIST_COLS = V // 16
 NEAR, FAR = 0, 1
-X_LOADS = ((1024, 512, 512), (1024, 512, 256, 256))
-X_STEP = 512
-SHARE_EVEN, SHARE_MORE = 4, 5
+X_LOADS = (((1024, 16), (1024, 6)), ((1024, 16), (1024, 6)), ((512, 16), (1024, 9), (512, 7)), ((1024, 16), (512, 0), (256, 16), (256, 0)))
+HALF = H // 2
 CELLS = 128
 STEPS = S // CELLS
 LAST_PIECES = (1, 2, 4, STEPS)
@@ -35,7 +34,6 @@ def tile_picked_bev_max_e_kernel(tc, xT, w1, w2, w3, offs, near, far, out):
     nc = tc.nc
     with ExitStack() as ctx:
         keep = ctx.enter_context(tc.tile_pool(name="keep", bufs=1))
-        stage = ctx.enter_context(tc.tile_pool(name="stage", bufs=3))
         psum = ctx.enter_context(tc.psum_pool(name="psum", bufs=2))
 
         offs_sb = keep.tile([P, S // 16], U16, name="offs_sb")
@@ -54,73 +52,92 @@ def tile_picked_bev_max_e_kernel(tc, xT, w1, w2, w3, offs, near, far, out):
             src = raw[:, :, r0 + a:r0 + b].rearrange("p j (c e) -> p c j e", e=RUN)
             return dst, src
 
-        x_scales = keep.tile([P, T], U8, name="x_scales", align_bytes=64)
-        nc.vector.memset(x_scales[:].bitcast(I32), 0)
         windows = [[keep.tile([P, S], F32, name="win%d%d" % (s, t), tag="win%d%d" % (s, t)) for t in range(PACK)]
                    for s in (NEAR, FAR)]
         for s in (NEAR, FAR):
             for t in range(PACK):
                 (nc.vector, nc.gpsimd)[s].memset(windows[s][t][:], 0.0)
 
-        x_codes = [keep.tile([P, T], U32, name="x_codes%d" % g, align_bytes=64) for g in range(PASSES)]
-        got_words = {}
-        got_bytes = {}
+        x_in = {}
+        got = [keep.tile([P, 2, S + g * V], U32, name="got%d" % g, align_bytes=64) for g in range(PASSES)]
+        x_codes = {}
+        x_scales = {}
 
-        def gather_words(g, s, tag):
-            got = keep.tile([P, V], U32, name="got_words%d%d" % (g, s), tag=tag, align_bytes=64)
-            nc.vector.tensor_copy(got[:], x_codes[g][:].indirect(offs_sb[:, LIST_COLS * s:LIST_COLS * (s + 1)]))
-            got_words[g, s] = got[:]
+        def gather(g, u, first, last, window):
+            nc.vector.tensor_copy(got[g][:, u, first * V:(last + 1) * V],
+                                  window.indirect(offs_sb[:, LIST_COLS * first:LIST_COLS * (last + 1)]))
 
-        def gather_bytes(s, tag):
-            got = keep.tile([P, V], U8, name="got_bytes%d" % s, tag=tag, align_bytes=64)
-            nc.vector.tensor_copy(got[:], x_scales[:].indirect(offs_sb[:, LIST_COLS * s:LIST_COLS * (s + 1)]))
-            got_bytes[s] = got
+        def weave(g, s, tag, copy, place=None):
+            if place is None:
+                place = keep.tile([P, V * PACK], BF16, name="x_in%d%d" % (g, s), tag=tag, align_bytes=64)[:]
+            x_in[g, s] = place
+            copy(place.bitcast(U32).rearrange("p (n u) -> p n u", u=2), got[g][:, :, s * V:(s + 1) * V].rearrange("p u n -> p n u"))
+
+        def quantise_picked(g, s, codes_tag=None):
+            codes = keep.tile([P, V], U32, name="x_codes%d%d" % (g, s), tag=codes_tag or "x_codes%d%d" % (g, s), align_bytes=64)
+            scales = keep.tile([P, V], U8, name="x_scales%d%d" % (g, s), align_bytes=64)
+            nc.vector.quantize_mx(out=codes[:].bitcast(FP8X4), scales=scales[:], in_=x_in[g, s])
+            x_codes[g, s] = codes
+            x_scales[g, s] = scales
 
         for g in range(PASSES):
-            c0 = 0
-            for index, loaded in enumerate(X_LOADS[g]):
-                raw = load_pass(xT, g, c0, loaded, "x_raw%d%d" % (g, index))
-                if (g, index) == (0, 1):
-                    nc.sync.dma_start(offs_sb[:], offs)
-                width = min(loaded, X_STEP)
-                for r0 in range(0, loaded, width):
-                    very_last = g == PASSES - 1 and c0 + loaded == T
-                    split = width * (SHARE_MORE if r0 > 0 or very_last else SHARE_EVEN) // 8
-                    grouped = stage.tile([P, width, PACK], BF16, name="x_grouped", tag="x_grouped", align_bytes=64)
-                    dst, src = weave_views(grouped, raw, r0, 0, split)
-                    nc.scalar.activation(dst, src, COPY)
-                    dst, src = weave_views(grouped, raw, r0, split, width)
-                    nc.vector.tensor_copy(dst, src)
-                    nc.vector.quantize_mx(
-                        out=x_codes[g][:, c0 + r0:c0 + r0 + width].bitcast(FP8X4),
-                        scales=x_scales[4 * g:P, c0 + r0:c0 + r0 + width],
-                        in_=grouped[:].rearrange("p w j -> p (w j)"),
-                    )
-                c0 += loaded
-            if g == 0:
-                both = keep.tile([P, S], U32, name="got_words0", align_bytes=64)
-                nc.vector.tensor_copy(both[:], x_codes[0][:].indirect(offs_sb[:]))
-                got_words[0, NEAR] = both[:, 0:V]
-                got_words[0, FAR] = both[:, V:S]
-        gather_words(1, NEAR, "got_words10")
-        gather_bytes(NEAR, "got_bytes0")
+            rows = xT[g * K_PASS:(g + 1) * K_PASS, :].rearrange("(p j) w -> p j w", j=PACK)
+            for u in range(2):
+                pairs = keep.tile([P, T, 2], BF16, name="pairs%d%d" % (g, u), tag="pairs%d" % ((2 * g + u) % 3), align_bytes=64)
+                c0 = 0
+                for index, (width, share) in enumerate(X_LOADS[2 * g + u]):
+                    tag = "x_raw%d%d%d" % (g, u, index)
+                    raw = keep.tile([P, 2, width], F32, name=tag, tag=tag, align_bytes=64)
+                    nc.sync.dma_start(out=raw[:], in_=rows[:, 2 * u:2 * u + 2, c0:c0 + width])
+                    if (g, u, index) == (0, 0, 0):
+                        nc.sync.dma_start(offs_sb[:], offs)
+                    split = width * share // 16
+                    both = raw[:].rearrange("p v w -> p w v")
+                    if split > 0:
+                        nc.scalar.activation(pairs[:, c0:c0 + split, :], both[:, 0:split, :], COPY)
+                    if split < width:
+                        nc.vector.tensor_copy(pairs[:, c0 + split:c0 + width, :], both[:, split:width, :])
+                    c0 += width
+                    if (g, u, index) == (1, 0, 0):
+                        weave(0, NEAR, tag, nc.scalar.copy)
+                    if (g, u, index) == (1, 0, 1):
+                        quantise_picked(0, NEAR)
+                window = pairs[:].rearrange("p w v -> p (w v)").bitcast(U32)
+                if u == 0:
+                    gather(g, u, NEAR, FAR, window)
+                else:
+                    gather(g, u, NEAR, NEAR, window)
+                    if g == 0:
+                        gather(g, u, FAR, FAR, window)
+                if (g, u) == (1, 0):
+                    weave(0, FAR, "x_raw102", nc.scalar.copy)
+                    quantise_picked(0, FAR)
 
         def deal(grouped, raw, t):
             dst = grouped.rearrange("p (c e j) -> p c j e", e=RUN, j=PACK)
             src = raw[:].rearrange("p j (c t e) -> p t c j e", t=PACK, e=RUN)[:, t]
             nc.scalar.activation(dst, src, COPY)
 
+        def deal_near(grouped, raw, v):
+            dst = grouped.rearrange("p (u c e j) -> p u c j e", u=2, e=RUN, j=PACK)
+            src = raw[:].rearrange("p j (c u v e) -> p v u c j e", u=2, v=2, e=RUN)[:, v]
+            nc.scalar.copy(dst, src)
+
         w_codes = {}
         w_scales = {}
 
-        def prepare_weights(s, raws, parts, tag):
+        def prepare_weights(s, raws, parts, tag, grouped=None):
             name = "%d%d%d" % ((s,) + parts[0])
-            grouped = keep.tile([P, len(parts) * K_PASS], BF16, name="w_grouped" + name, tag=tag, align_bytes=64)
+            if grouped is None:
+                grouped = keep.tile([P, len(parts) * K_PASS], BF16, name="w_grouped" + name, tag=tag, align_bytes=64)[:]
             for n, (g, t) in enumerate(parts):
-                deal(grouped[:, n * K_PASS:(n + 1) * K_PASS], raws[g], t)
+                if s == NEAR:
+                    deal_near(grouped[:, n * K_PASS:(n + 1) * K_PASS], raws[g], t % 2)
+                else:
+                    deal(grouped[:, n * K_PASS:(n + 1) * K_PASS], raws[g], t)
             codes = keep.tile([P, len(parts) * P], U32, name="w_codes" + name, tag="w_codes" + name, align_bytes=64)
             scales = keep.tile([P, len(parts) * P], U8, name="w_scales" + name, tag="w_scales" + name, align_bytes=64)
-            nc.vector.quantize_mx(out=codes[:].bitcast(FP8X4), scales=scales[:], in_=grouped[:])
+            nc.vector.quantize_mx(out=codes[:].bitcast(FP8X4), scales=scales[:], in_=grouped)
             for n, (g, t) in enumerate(parts):
                 w_codes[s, g, t] = codes[:, n * P:(n + 1) * P]
                 w_scales[s, g, t] = scales[:, n * P:(n + 1) * P]
@@ -131,7 +148,7 @@ def tile_picked_bev_max_e_kernel(tc, xT, w1, w2, w3, offs, near, far, out):
                 nc.tensor.matmul_mx(
                     out=acc[:],
                     lhsT=w_codes[s, g, t].bitcast(FP8X4), lhsT_scale=w_scales[s, g, t],
-                    rhs=got_words[g, s].bitcast(FP8X4), rhs_scale=got_bytes[s][4 * g:P, :],
+                    rhs=x_codes[g, s][:].bitcast(FP8X4), rhs_scale=x_scales[g, s][:],
                     start=(g == 0), stop=(g == PASSES - 1),
                 )
             return acc
@@ -140,25 +157,31 @@ def tile_picked_bev_max_e_kernel(tc, xT, w1, w2, w3, offs, near, far, out):
             nc.scalar.activation(packed, acc[:], RELU)
             nc.vector.tensor_copy(windows[s][t][:].indirect(cell_lists[s][:]), packed)
 
-        w1_raw = [load_pass(w1, g, 0, H, "w1_raw%d" % g) for g in range(PASSES)]
+        w1_low = [load_pass(w1, g, 0, HALF, "w1_low%d" % g) for g in range(PASSES)]
         nc.sync.dma_start(near_sb[:], near)
+        w1_high = [load_pass(w1, g, HALF, HALF, "w1_high%d" % g) for g in range(PASSES)]
         nc.sync.dma_start(far_sb[:], far)
 
-        prepare_weights(NEAR, w1_raw, [(0, 0)], "w1_grouped00")
-        gather_words(1, FAR, "w1_grouped00")
-        prepare_weights(NEAR, w1_raw, [(1, 0)], "w1_grouped10")
-        gather_bytes(FAR, "w1_grouped10")
-        prepare_weights(NEAR, w1_raw, [(0, 1), (1, 1)], "w1_grouped01")
-        prepare_weights(NEAR, w1_raw, [(0, 2), (1, 2)], "w1_grouped02")
-        near_packed = keep.tile([P, PACK - 1, V], F32, name="near_packed", tag="x_raw00", align_bytes=64)
-        put(NEAR, 0, layer(NEAR, 0), near_packed[:, 0, :])
-        prepare_weights(NEAR, w1_raw, [(0, 3), (1, 3)], "w_codes010")
-        put(NEAR, 1, layer(NEAR, 1), near_packed[:, 1, :])
-        put(NEAR, 2, layer(NEAR, 2), near_packed[:, 2, :])
+        turns = got[1][:, 1, V:].bitcast(BF16)
+        prepare_weights(NEAR, w1_low, [(0, 0)], None, turns[:, 0:K_PASS])
+        weave(1, NEAR, None, nc.vector.tensor_copy, turns)
+        prepare_weights(NEAR, w1_low, [(1, 0)], "w1_grouped2")
+        quantise_picked(1, NEAR, "w1_grouped2")
+        gather(1, 1, FAR, FAR, window)
+        prepare_weights(NEAR, w1_low, [(0, 1), (1, 1)], "w1_grouped1")
+        weave(1, FAR, "w1_low1", nc.scalar.copy)
+        quantise_picked(1, FAR)
+        packed0 = keep.tile([P, V], F32, name="packed0", tag="x_raw010", align_bytes=64)
+        put(NEAR, 0, layer(NEAR, 0), packed0[:])
+        prepare_weights(NEAR, w1_high, [(0, 2), (1, 2), (0, 3), (1, 3)], "w_codes010")
+        packed1 = keep.tile([P, V], F32, name="packed1", tag="w1_high1", align_bytes=64)
+        put(NEAR, 1, layer(NEAR, 1), packed1[:])
+        packed2 = keep.tile([P, V], F32, name="packed2", tag="x_raw011", align_bytes=64)
+        put(NEAR, 2, layer(NEAR, 2), packed2[:])
         last_near = layer(NEAR, 3)
 
         w2_raw = [load_pass(w2, g, 0, H, "w2_raw%d" % g) for g in range(PASSES)]
-        prepare_weights(FAR, w2_raw, [(g, t) for g in range(PASSES) for t in range(PACK)], "w_scales010")
+        prepare_weights(FAR, w2_raw, [(g, t) for g in range(PASSES) for t in range(PACK)], "w_scales001")
         late_packed = keep.tile([P, V], F32, name="late_packed", tag="w2_raw1", align_bytes=64)
         put(NEAR, 3, last_near, late_packed[:])
 
@@ -166,22 +189,28 @@ def tile_picked_bev_max_e_kernel(tc, xT, w1, w2, w3, offs, near, far, out):
         w3_rows = w3.rearrange("(c t e) n -> e c t n", t=PACK, e=RUN)
         for e in range(RUN):
             nc.sync.dma_start(out=w3_raw[e:P:RUN], in_=w3_rows[e])
-        w3_grouped = keep.tile([P, N, PACK], BF16, name="w3_grouped", tag="w_codes003", align_bytes=64)
+        w3_grouped = keep.tile([P, N, PACK], BF16, name="w3_grouped", tag="w_codes002", align_bytes=64)
         dst, src = weave_views(w3_grouped, w3_raw, 0, 0, N)
         nc.scalar.activation(dst, src, COPY)
 
-        near_pairs = keep.tile([P, 2, S, 2], BF16, name="near_pairs", tag="w2_raw0", align_bytes=64)
+        near_pairs = keep.tile([P, 2, S, 2], BF16, name="near_pairs", tag="pairs0", align_bytes=64)
+        near_halves = [keep.tile([P, S, 2], BF16, name="near_half%d" % h, tag=("w2_raw0", "w_codes100")[h], align_bytes=64)
+                       for h in range(2)]
 
         def round_near(t):
-            nc.scalar.activation(near_pairs[:, t // 2, :, t % 2], windows[NEAR][t][:], COPY)
+            h = t // 2
+            nc.scalar.activation(near_halves[h][:, :, t % 2], windows[NEAR][t][:], COPY)
+            if t % 2 == 1:
+                for u in range(2):
+                    nc.sync.dma_start(out=near_pairs[64 * h:64 * (h + 1), u], in_=near_halves[h][64 * u:64 * (u + 1)])
 
         round_near(0)
         round_near(1)
-        far_packed = keep.tile([P, PACK, V], F32, name="far_packed", tag="x_raw10", align_bytes=64)
+        far_packed = keep.tile([P, PACK, V], F32, name="far_packed", tag="x_raw101", align_bytes=64)
         for t in range(PACK):
             put(FAR, t, layer(FAR, t), far_packed[:, t, :])
 
-        w3_codes = keep.tile([P, N], U32, name="w3_codes", tag="x_raw10", align_bytes=64)
+        w3_codes = keep.tile([P, N], U32, name="w3_codes", tag="x_raw101", align_bytes=64)
         w3_scales = keep.tile([P, N], U8, name="w3_scales", align_bytes=64)
         nc.vector.quantize_mx(out=w3_codes[:].bitcast(FP8X4), scales=w3_scales[:],
                               in_=w3_grouped[:].rearrange("p w j -> p (w j)"))
@@ -201,8 +230,8 @@ def tile_picked_bev_max_e_kernel(tc, xT, w1, w2, w3, offs, near, far, out):
             round_far(PACK - 1, c0, c1)
 
         out_view = out.rearrange("(h p) r -> p h r", p=P)
-        z_all = keep.tile([P, STEPS * CELLS * PACK], BF16, name="z_all", tag="x_raw01", align_bytes=64)
-        res_all = keep.tile([P, STEPS * 2 * CELLS], F32, name="res_all", tag="x_raw11", align_bytes=64)
+        z_all = keep.tile([P, STEPS * CELLS * PACK], BF16, name="z_all", tag="x_raw001", align_bytes=64)
+        res_all = keep.tile([P, STEPS * 2 * CELLS], F32, name="res_all", tag="x_raw110", align_bytes=64)
 
         def join(c):
             z = z_all[:, c * CELLS * PACK:(c + 1) * CELLS * PACK]

@@ -47,11 +47,6 @@ def tile_picked_bev_max_e_kernel(tc, xT, w1, w2, w3, offs, near, far, out):
             nc.sync.dma_start(out=raw[:], in_=rows.rearrange("(p j) w -> p j w", j=PACK))
             return raw
 
-        def weave_views(grouped, raw, r0, a, b):
-            dst = grouped[:, a:b, :].rearrange("p (c e) j -> p c j e", e=RUN)
-            src = raw[:, :, r0 + a:r0 + b].rearrange("p j (c e) -> p c j e", e=RUN)
-            return dst, src
-
         windows = [[keep.tile([P, S], F32, name="win%d%d" % (s, t), tag="win%d%d" % (s, t)) for t in range(PACK)]
                    for s in (NEAR, FAR)]
         for s in (NEAR, FAR):
@@ -113,28 +108,16 @@ def tile_picked_bev_max_e_kernel(tc, xT, w1, w2, w3, offs, near, far, out):
                     weave(0, FAR, "x_raw102", nc.scalar.copy)
                     quantise_picked(0, FAR)
 
-        def deal(grouped, raw, t):
-            dst = grouped.rearrange("p (c e j) -> p c j e", e=RUN, j=PACK)
-            src = raw[:].rearrange("p j (c t e) -> p t c j e", t=PACK, e=RUN)[:, t]
-            nc.scalar.activation(dst, src, COPY)
-
-        def deal_near(grouped, raw, v):
-            dst = grouped.rearrange("p (u c e j) -> p u c j e", u=2, e=RUN, j=PACK)
-            src = raw[:].rearrange("p j (c u v e) -> p v u c j e", u=2, v=2, e=RUN)[:, v]
-            nc.scalar.copy(dst, src)
-
         w_codes = {}
         w_scales = {}
 
-        def prepare_weights(s, raws, parts, tag, grouped=None):
+        def deal(grouped, raw):
+            dst = grouped.rearrange("p (n c e j) -> p n c j e", n=PACK, e=RUN, j=PACK)
+            src = raw[:].rearrange("p j (c n e) -> p n c j e", n=PACK, e=RUN)
+            nc.scalar.copy(dst, src)
+
+        def quantise_weights(s, parts, grouped):
             name = "%d%d%d" % ((s,) + parts[0])
-            if grouped is None:
-                grouped = keep.tile([P, len(parts) * K_PASS], BF16, name="w_grouped" + name, tag=tag, align_bytes=64)[:]
-            for n, (g, t) in enumerate(parts):
-                if s == NEAR:
-                    deal_near(grouped[:, n * K_PASS:(n + 1) * K_PASS], raws[g], t % 2)
-                else:
-                    deal(grouped[:, n * K_PASS:(n + 1) * K_PASS], raws[g], t)
             codes = keep.tile([P, len(parts) * P], U32, name="w_codes" + name, tag="w_codes" + name, align_bytes=64)
             scales = keep.tile([P, len(parts) * P], U8, name="w_scales" + name, tag="w_scales" + name, align_bytes=64)
             nc.vector.quantize_mx(out=codes[:].bitcast(FP8X4), scales=scales[:], in_=grouped)
@@ -163,25 +146,48 @@ def tile_picked_bev_max_e_kernel(tc, xT, w1, w2, w3, offs, near, far, out):
         nc.sync.dma_start(far_sb[:], far)
 
         turns = got[1][:, 1, V:].bitcast(BF16)
-        prepare_weights(NEAR, w1_low, [(0, 0)], None, turns[:, 0:K_PASS])
+        deal(turns[:, 0:2 * K_PASS], w1_low[0])
+        quantise_weights(NEAR, [(0, 0), (0, 1)], turns[:, 0:2 * K_PASS])
         weave(1, NEAR, None, nc.vector.tensor_copy, turns)
-        prepare_weights(NEAR, w1_low, [(1, 0)], "w1_grouped2")
-        quantise_picked(1, NEAR, "w1_grouped2")
+        quantise_picked(1, NEAR)
+        low_grouped = keep.tile([P, 2 * K_PASS], BF16, name="low_grouped", tag="low_grouped", align_bytes=64)
+        deal(low_grouped[:], w1_low[1])
+        quantise_weights(NEAR, [(1, 0), (1, 1)], low_grouped[:])
         gather(1, 1, FAR, FAR, window)
-        prepare_weights(NEAR, w1_low, [(0, 1), (1, 1)], "w1_grouped1")
-        weave(1, FAR, "w1_low1", nc.scalar.copy)
-        quantise_picked(1, FAR)
+        high_grouped = keep.tile([P, 2 * K_PASS], BF16, name="high_grouped0", align_bytes=64)
+        deal(high_grouped[:], w1_high[0])
+        quantise_weights(NEAR, [(0, 2), (0, 3)], high_grouped[:])
+        near_pairs = keep.tile([P, 2, S, 2], BF16, name="near_pairs", tag="pairs0", align_bytes=64)
+        near_halves = {}
+
+        def round_near(t):
+            h = t // 2
+            if t == 2:
+                near_halves[h] = keep.tile([P, S, 2], BF16, name="near_half%d" % h, tag="w_codes100", align_bytes=64)[:]
+            nc.scalar.activation(near_halves[h][:, :, t % 2], windows[NEAR][t][:], COPY)
+            if t % 2 == 1:
+                for u in range(2):
+                    nc.sync.dma_start(out=near_pairs[64 * h:64 * (h + 1), u], in_=near_halves[h][64 * u:64 * (u + 1)])
+
         packed0 = keep.tile([P, V], F32, name="packed0", tag="x_raw010", align_bytes=64)
         put(NEAR, 0, layer(NEAR, 0), packed0[:])
-        prepare_weights(NEAR, w1_high, [(0, 2), (1, 2), (0, 3), (1, 3)], "w_codes010")
+        high_grouped = keep.tile([P, 2 * K_PASS], BF16, name="high_grouped1", tag="w_codes010", align_bytes=64)
+        deal(high_grouped[:], w1_high[1])
+        quantise_weights(NEAR, [(1, 2), (1, 3)], high_grouped[:])
         packed1 = keep.tile([P, V], F32, name="packed1", tag="w1_high1", align_bytes=64)
         put(NEAR, 1, layer(NEAR, 1), packed1[:])
-        packed2 = keep.tile([P, V], F32, name="packed2", tag="x_raw011", align_bytes=64)
-        put(NEAR, 2, layer(NEAR, 2), packed2[:])
-        last_near = layer(NEAR, 3)
-
+        weave(1, FAR, "w_scales010", nc.scalar.copy)
+        quantise_picked(1, FAR)
         w2_raw = [load_pass(w2, g, 0, H, "w2_raw%d" % g) for g in range(PASSES)]
-        prepare_weights(FAR, w2_raw, [(g, t) for g in range(PASSES) for t in range(PACK)], "w_scales001")
+        w2_parts = [(g, t) for g in range(PASSES) for t in (0, 2, 1, 3)]
+        w2_grouped = keep.tile([P, len(w2_parts) * K_PASS], BF16, name="w2_grouped", tag="pairs1", align_bytes=64)
+        deal(w2_grouped[:, 0:PACK * K_PASS], w2_raw[0])
+        after_w2 = keep.tile([P, V + S], F32, name="after_w2", tag="w2_raw0", align_bytes=64)
+        near_halves[0] = after_w2[:, V:].bitcast(BF16).rearrange("p (r v) -> p r v", v=2)
+        put(NEAR, 2, layer(NEAR, 2), after_w2[:, 0:V])
+        last_near = layer(NEAR, 3)
+        deal(w2_grouped[:, PACK * K_PASS:], w2_raw[1])
+        quantise_weights(FAR, w2_parts, w2_grouped[:])
         late_packed = keep.tile([P, V], F32, name="late_packed", tag="w2_raw1", align_bytes=64)
         put(NEAR, 3, last_near, late_packed[:])
 
@@ -189,26 +195,15 @@ def tile_picked_bev_max_e_kernel(tc, xT, w1, w2, w3, offs, near, far, out):
         w3_rows = w3.rearrange("(c t e) n -> e c t n", t=PACK, e=RUN)
         for e in range(RUN):
             nc.sync.dma_start(out=w3_raw[e:P:RUN], in_=w3_rows[e])
-        w3_grouped = keep.tile([P, N, PACK], BF16, name="w3_grouped", tag="w_codes002", align_bytes=64)
-        dst, src = weave_views(w3_grouped, w3_raw, 0, 0, N)
-        nc.scalar.activation(dst, src, COPY)
-
-        near_pairs = keep.tile([P, 2, S, 2], BF16, name="near_pairs", tag="pairs0", align_bytes=64)
-        near_halves = [keep.tile([P, S, 2], BF16, name="near_half%d" % h, tag=("w2_raw0", "w_codes100")[h], align_bytes=64)
-                       for h in range(2)]
-
-        def round_near(t):
-            h = t // 2
-            nc.scalar.activation(near_halves[h][:, :, t % 2], windows[NEAR][t][:], COPY)
-            if t % 2 == 1:
-                for u in range(2):
-                    nc.sync.dma_start(out=near_pairs[64 * h:64 * (h + 1), u], in_=near_halves[h][64 * u:64 * (u + 1)])
-
         round_near(0)
         round_near(1)
         far_packed = keep.tile([P, PACK, V], F32, name="far_packed", tag="x_raw101", align_bytes=64)
         for t in range(PACK):
             put(FAR, t, layer(FAR, t), far_packed[:, t, :])
+
+        w3_grouped = keep.tile([P, N, PACK], BF16, name="w3_grouped", tag="w_scales100", align_bytes=64)
+        nc.scalar.copy(w3_grouped[:].rearrange("p (c e) (u v) -> p c u v e", e=RUN, u=2),
+                       w3_raw[:].rearrange("p (v u) (c e) -> p c u v e", e=RUN, u=2))
 
         w3_codes = keep.tile([P, N], U32, name="w3_codes", tag="x_raw101", align_bytes=64)
         w3_scales = keep.tile([P, N], U8, name="w3_scales", align_bytes=64)

@@ -23,7 +23,7 @@ K_PASS = P * PACK
 PASSES = K // K_PASS
 LIST_COLS = V // 16
 NEAR, FAR = 0, 1
-X_LOADS = (((1024, 16), (1024, 6)), ((1024, 16), (1024, 6)), ((512, 16), (1024, 9), (512, 7)), ((1024, 16), (512, 0), (256, 16), (256, 0)))
+X_LOADS = (((1024, 16), (1024, 6)), ((1024, 16), (512, 0), (512, 5)), ((512, 16), (1024, 5), (512, 6)), ((1024, 16), (512, 12), (512, 2)))
 HALF = H // 2
 CELLS = 128
 STEPS = S // CELLS
@@ -54,7 +54,7 @@ def tile_picked_bev_max_e_kernel(tc, xT, w1, w2, w3, offs, near, far, out):
                 (nc.vector, nc.gpsimd)[s].memset(windows[s][t][:], 0.0)
 
         x_in = {}
-        got = [keep.tile([P, 2, S + g * V], U32, name="got%d" % g, align_bytes=64) for g in range(PASSES)]
+        got = [keep.tile([P, 2, S], U32, name="got%d" % g, align_bytes=64) for g in range(PASSES)]
         x_codes = {}
         x_scales = {}
 
@@ -62,11 +62,11 @@ def tile_picked_bev_max_e_kernel(tc, xT, w1, w2, w3, offs, near, far, out):
             nc.vector.tensor_copy(got[g][:, u, first * V:(last + 1) * V],
                                   window.indirect(offs_sb[:, LIST_COLS * first:LIST_COLS * (last + 1)]))
 
-        def weave(g, s, tag, copy, place=None):
-            if place is None:
-                place = keep.tile([P, V * PACK], BF16, name="x_in%d%d" % (g, s), tag=tag, align_bytes=64)[:]
+        def weave(g, s, tag, copy):
+            place = keep.tile([P, V * PACK], BF16, name="x_in%d%d" % (g, s), tag=tag, align_bytes=64)[:]
             x_in[g, s] = place
-            copy(place.bitcast(U32).rearrange("p (n u) -> p n u", u=2), got[g][:, :, s * V:(s + 1) * V].rearrange("p u n -> p n u"))
+            copy(place.bitcast(U32).rearrange("p (c e u) -> p c u e", e=RUN, u=2),
+                 got[g][:, :, s * V:(s + 1) * V].rearrange("p u (c e) -> p c u e", e=RUN))
 
         def quantise_picked(g, s, codes_tag=None):
             codes = keep.tile([P, V], U32, name="x_codes%d%d" % (g, s), tag=codes_tag or "x_codes%d%d" % (g, s), align_bytes=64)
@@ -87,16 +87,15 @@ def tile_picked_bev_max_e_kernel(tc, xT, w1, w2, w3, offs, near, far, out):
                     if (g, u, index) == (0, 0, 0):
                         nc.sync.dma_start(offs_sb[:], offs)
                     split = width * share // 16
-                    both = raw[:].rearrange("p v w -> p w v")
+                    src = raw[:].rearrange("p v (c e) -> p c v e", e=RUN)
+                    dst = pairs[:, c0:c0 + width, :].rearrange("p (c e) v -> p c v e", e=RUN)
                     if split > 0:
-                        nc.scalar.activation(pairs[:, c0:c0 + split, :], both[:, 0:split, :], COPY)
+                        nc.scalar.activation(dst[:, 0:split // RUN], src[:, 0:split // RUN], COPY)
                     if split < width:
-                        nc.vector.tensor_copy(pairs[:, c0 + split:c0 + width, :], both[:, split:width, :])
+                        nc.vector.tensor_copy(dst[:, split // RUN:], src[:, split // RUN:])
                     c0 += width
                     if (g, u, index) == (1, 0, 0):
                         weave(0, NEAR, tag, nc.scalar.copy)
-                    if (g, u, index) == (1, 0, 1):
-                        quantise_picked(0, NEAR)
                 window = pairs[:].rearrange("p w v -> p (w v)").bitcast(U32)
                 if u == 0:
                     gather(g, u, NEAR, FAR, window)
@@ -105,6 +104,7 @@ def tile_picked_bev_max_e_kernel(tc, xT, w1, w2, w3, offs, near, far, out):
                     if g == 0:
                         gather(g, u, FAR, FAR, window)
                 if (g, u) == (1, 0):
+                    quantise_picked(0, NEAR, "pairs2")
                     weave(0, FAR, "x_raw102", nc.scalar.copy)
                     quantise_picked(0, FAR)
 
@@ -145,14 +145,14 @@ def tile_picked_bev_max_e_kernel(tc, xT, w1, w2, w3, offs, near, far, out):
         w1_high = [load_pass(w1, g, HALF, HALF, "w1_high%d" % g) for g in range(PASSES)]
         nc.sync.dma_start(far_sb[:], far)
 
-        turns = got[1][:, 1, V:].bitcast(BF16)
-        deal(turns[:, 0:2 * K_PASS], w1_low[0])
-        quantise_weights(NEAR, [(0, 0), (0, 1)], turns[:, 0:2 * K_PASS])
-        weave(1, NEAR, None, nc.vector.tensor_copy, turns)
-        quantise_picked(1, NEAR)
-        low_grouped = keep.tile([P, 2 * K_PASS], BF16, name="low_grouped", tag="low_grouped", align_bytes=64)
-        deal(low_grouped[:], w1_low[1])
-        quantise_weights(NEAR, [(1, 0), (1, 1)], low_grouped[:])
+        weave(1, NEAR, "x_in10", nc.vector.tensor_copy)
+        first_grouped = keep.tile([P, 2 * K_PASS], BF16, name="first_grouped", tag="first_grouped", align_bytes=64)
+        deal(first_grouped[:], w1_low[0])
+        quantise_weights(NEAR, [(0, 0), (0, 1)], first_grouped[:])
+        quantise_picked(1, NEAR, "first_grouped")
+        low_grouped = got[1][:, 1, V:].bitcast(BF16)
+        deal(low_grouped, w1_low[1])
+        quantise_weights(NEAR, [(1, 0), (1, 1)], low_grouped)
         gather(1, 1, FAR, FAR, window)
         high_grouped = keep.tile([P, 2 * K_PASS], BF16, name="high_grouped0", align_bytes=64)
         deal(high_grouped[:], w1_high[0])

@@ -7,7 +7,6 @@ FLOPS = 2 * K * H * V * 2 + 2 * H * N * S
 
 F32 = mybir.dt.float32
 BF16 = mybir.dt.bfloat16
-I32 = mybir.dt.int32
 U32 = mybir.dt.uint32
 U16 = mybir.dt.uint16
 U8 = mybir.dt.uint8
@@ -23,8 +22,13 @@ K_PASS = P * PACK
 PASSES = K // K_PASS
 LIST_COLS = V // 16
 NEAR, FAR = 0, 1
-X_LOADS = (((1024, 16), (1024, 6)), ((1024, 16), (512, 0), (512, 5)), ((512, 16), (1024, 5), (512, 6)), ((1024, 16), (512, 12), (512, 2)))
 HALF = H // 2
+ALL, NONE = 16, 0
+SHARE_LAST, SHARE_WIDE, SHARE_END = 6, 7, 8
+X_LOADS = (((1024, ALL), (1024, SHARE_LAST)),
+           ((1024, ALL), (512, NONE), (512, SHARE_LAST)),
+           ((512, ALL), (1024, SHARE_WIDE), (512, SHARE_LAST)),
+           ((1024, ALL), (512, NONE), (512, SHARE_END)))
 CELLS = 128
 STEPS = S // CELLS
 LAST_PIECES = (1, 2, 4, STEPS)
@@ -53,60 +57,74 @@ def tile_picked_bev_max_e_kernel(tc, xT, w1, w2, w3, offs, near, far, out):
             for t in range(PACK):
                 (nc.vector, nc.gpsimd)[s].memset(windows[s][t][:], 0.0)
 
-        x_in = {}
         got = [keep.tile([P, 2, S], U32, name="got%d" % g, align_bytes=64) for g in range(PASSES)]
+        x_woven = {}
         x_codes = {}
         x_scales = {}
 
-        def gather(g, u, first, last, window):
+        def load_and_round(g, u, index, pairs):
+            loads = X_LOADS[2 * g + u]
+            c0 = sum(width for width, share in loads[:index])
+            width, share = loads[index]
+            tag = "x_raw%d%d%d" % (g, u, index)
+            raw = keep.tile([P, 2, width], F32, name=tag, tag=tag, align_bytes=64)
+            rows = xT[g * K_PASS:(g + 1) * K_PASS, :].rearrange("(p j) w -> p j w", j=PACK)
+            nc.sync.dma_start(out=raw[:], in_=rows[:, 2 * u:2 * u + 2, c0:c0 + width])
+            split = width * share // ALL // RUN
+            src = raw[:].rearrange("p v (c e) -> p c v e", e=RUN)
+            dst = pairs[:, c0:c0 + width, :].rearrange("p (c e) v -> p c v e", e=RUN)
+            if share != NONE:
+                nc.scalar.activation(dst[:, 0:split], src[:, 0:split], COPY)
+            if share != ALL:
+                nc.vector.tensor_copy(dst[:, split:], src[:, split:])
+
+        def gather(g, u, first, last, pairs):
+            window = pairs[:].rearrange("p w v -> p (w v)").bitcast(U32)
             nc.vector.tensor_copy(got[g][:, u, first * V:(last + 1) * V],
                                   window.indirect(offs_sb[:, LIST_COLS * first:LIST_COLS * (last + 1)]))
 
         def weave(g, s, tag, copy):
-            place = keep.tile([P, V * PACK], BF16, name="x_in%d%d" % (g, s), tag=tag, align_bytes=64)[:]
-            x_in[g, s] = place
-            copy(place.bitcast(U32).rearrange("p (c e u) -> p c u e", e=RUN, u=2),
+            woven = keep.tile([P, V * PACK], BF16, name="x_woven%d%d" % (g, s), tag=tag, align_bytes=64)
+            copy(woven[:].bitcast(U32).rearrange("p (c e u) -> p c u e", e=RUN, u=2),
                  got[g][:, :, s * V:(s + 1) * V].rearrange("p u (c e) -> p c u e", e=RUN))
+            x_woven[g, s] = woven
 
-        def quantise_picked(g, s, codes_tag=None):
-            codes = keep.tile([P, V], U32, name="x_codes%d%d" % (g, s), tag=codes_tag or "x_codes%d%d" % (g, s), align_bytes=64)
+        def quantise_picked(g, s, codes_tag):
+            codes = keep.tile([P, V], U32, name="x_codes%d%d" % (g, s), tag=codes_tag, align_bytes=64)
             scales = keep.tile([P, V], U8, name="x_scales%d%d" % (g, s), align_bytes=64)
-            nc.vector.quantize_mx(out=codes[:].bitcast(FP8X4), scales=scales[:], in_=x_in[g, s])
+            nc.vector.quantize_mx(out=codes[:].bitcast(FP8X4), scales=scales[:], in_=x_woven[g, s][:])
             x_codes[g, s] = codes
             x_scales[g, s] = scales
 
-        for g in range(PASSES):
-            rows = xT[g * K_PASS:(g + 1) * K_PASS, :].rearrange("(p j) w -> p j w", j=PACK)
-            for u in range(2):
-                pairs = keep.tile([P, T, 2], BF16, name="pairs%d%d" % (g, u), tag="pairs%d" % ((2 * g + u) % 3), align_bytes=64)
-                c0 = 0
-                for index, (width, share) in enumerate(X_LOADS[2 * g + u]):
-                    tag = "x_raw%d%d%d" % (g, u, index)
-                    raw = keep.tile([P, 2, width], F32, name=tag, tag=tag, align_bytes=64)
-                    nc.sync.dma_start(out=raw[:], in_=rows[:, 2 * u:2 * u + 2, c0:c0 + width])
-                    if (g, u, index) == (0, 0, 0):
-                        nc.sync.dma_start(offs_sb[:], offs)
-                    split = width * share // 16
-                    src = raw[:].rearrange("p v (c e) -> p c v e", e=RUN)
-                    dst = pairs[:, c0:c0 + width, :].rearrange("p (c e) v -> p c v e", e=RUN)
-                    if split > 0:
-                        nc.scalar.activation(dst[:, 0:split // RUN], src[:, 0:split // RUN], COPY)
-                    if split < width:
-                        nc.vector.tensor_copy(dst[:, split // RUN:], src[:, split // RUN:])
-                    c0 += width
-                    if (g, u, index) == (1, 0, 0):
-                        weave(0, NEAR, tag, nc.scalar.copy)
-                window = pairs[:].rearrange("p w v -> p (w v)").bitcast(U32)
-                if u == 0:
-                    gather(g, u, NEAR, FAR, window)
-                else:
-                    gather(g, u, NEAR, NEAR, window)
-                    if g == 0:
-                        gather(g, u, FAR, FAR, window)
-                if (g, u) == (1, 0):
-                    quantise_picked(0, NEAR, "pairs2")
-                    weave(0, FAR, "x_raw102", nc.scalar.copy)
-                    quantise_picked(0, FAR)
+        def pairs_tile(tag):
+            return keep.tile([P, T, 2], BF16, name="pairs", tag=tag, align_bytes=64)
+
+        first_pairs = pairs_tile("pairs0")
+        load_and_round(0, 0, 0, first_pairs)
+        nc.sync.dma_start(offs_sb[:], offs)
+        load_and_round(0, 0, 1, first_pairs)
+        gather(0, 0, NEAR, FAR, first_pairs)
+
+        second_pairs = pairs_tile("pairs1")
+        for index in range(len(X_LOADS[1])):
+            load_and_round(0, 1, index, second_pairs)
+        gather(0, 1, NEAR, NEAR, second_pairs)
+        gather(0, 1, FAR, FAR, second_pairs)
+
+        third_pairs = pairs_tile("pairs2")
+        load_and_round(1, 0, 0, third_pairs)
+        weave(0, NEAR, "x_raw100", nc.scalar.copy)
+        load_and_round(1, 0, 1, third_pairs)
+        quantise_picked(0, NEAR, "x_codes00")
+        load_and_round(1, 0, 2, third_pairs)
+        gather(1, 0, NEAR, FAR, third_pairs)
+        weave(0, FAR, "x_raw102", nc.scalar.copy)
+        quantise_picked(0, FAR, "x_codes01")
+
+        last_pairs = pairs_tile("pairs0")
+        for index in range(len(X_LOADS[3])):
+            load_and_round(1, 1, index, last_pairs)
+        gather(1, 1, NEAR, NEAR, last_pairs)
 
         w_codes = {}
         w_scales = {}
@@ -145,41 +163,42 @@ def tile_picked_bev_max_e_kernel(tc, xT, w1, w2, w3, offs, near, far, out):
         w1_high = [load_pass(w1, g, HALF, HALF, "w1_high%d" % g) for g in range(PASSES)]
         nc.sync.dma_start(far_sb[:], far)
 
-        weave(1, NEAR, "x_in10", nc.vector.tensor_copy)
+        weave(1, NEAR, "x_woven10", nc.vector.tensor_copy)
         first_grouped = keep.tile([P, 2 * K_PASS], BF16, name="first_grouped", tag="first_grouped", align_bytes=64)
         deal(first_grouped[:], w1_low[0])
         quantise_weights(NEAR, [(0, 0), (0, 1)], first_grouped[:])
         quantise_picked(1, NEAR, "first_grouped")
-        low_grouped = got[1][:, 1, V:].bitcast(BF16)
-        deal(low_grouped, w1_low[1])
-        quantise_weights(NEAR, [(1, 0), (1, 1)], low_grouped)
-        gather(1, 1, FAR, FAR, window)
-        high_grouped = keep.tile([P, 2 * K_PASS], BF16, name="high_grouped0", align_bytes=64)
-        deal(high_grouped[:], w1_high[0])
-        quantise_weights(NEAR, [(0, 2), (0, 3)], high_grouped[:])
+        second_grouped = got[1][:, 1, V:].bitcast(BF16)
+        deal(second_grouped, w1_low[1])
+        quantise_weights(NEAR, [(1, 0), (1, 1)], second_grouped)
+        gather(1, 1, FAR, FAR, last_pairs)
+        third_grouped = keep.tile([P, 2 * K_PASS], BF16, name="third_grouped", align_bytes=64)
+        deal(third_grouped[:], w1_high[0])
+        quantise_weights(NEAR, [(0, 2), (0, 3)], third_grouped[:])
+
         near_pairs = keep.tile([P, 2, S, 2], BF16, name="near_pairs", tag="pairs0", align_bytes=64)
         near_halves = {}
 
         def round_near(t):
             h = t // 2
-            if t == 2:
-                near_halves[h] = keep.tile([P, S, 2], BF16, name="near_half%d" % h, tag="w_codes100", align_bytes=64)[:]
             nc.scalar.activation(near_halves[h][:, :, t % 2], windows[NEAR][t][:], COPY)
             if t % 2 == 1:
                 for u in range(2):
-                    nc.sync.dma_start(out=near_pairs[64 * h:64 * (h + 1), u], in_=near_halves[h][64 * u:64 * (u + 1)])
+                    nc.sync.dma_start(out=near_pairs[P // 2 * h:P // 2 * (h + 1), u],
+                                      in_=near_halves[h][P // 2 * u:P // 2 * (u + 1)])
 
         packed0 = keep.tile([P, V], F32, name="packed0", tag="x_raw010", align_bytes=64)
         put(NEAR, 0, layer(NEAR, 0), packed0[:])
-        high_grouped = keep.tile([P, 2 * K_PASS], BF16, name="high_grouped1", tag="w_codes010", align_bytes=64)
-        deal(high_grouped[:], w1_high[1])
-        quantise_weights(NEAR, [(1, 2), (1, 3)], high_grouped[:])
+        fourth_grouped = keep.tile([P, 2 * K_PASS], BF16, name="fourth_grouped", tag="w_codes010", align_bytes=64)
+        deal(fourth_grouped[:], w1_high[1])
+        quantise_weights(NEAR, [(1, 2), (1, 3)], fourth_grouped[:])
         packed1 = keep.tile([P, V], F32, name="packed1", tag="w1_high1", align_bytes=64)
         put(NEAR, 1, layer(NEAR, 1), packed1[:])
         weave(1, FAR, "w_scales010", nc.scalar.copy)
-        quantise_picked(1, FAR)
+        quantise_picked(1, FAR, "x_codes11")
+
         w2_raw = [load_pass(w2, g, 0, H, "w2_raw%d" % g) for g in range(PASSES)]
-        w2_parts = [(g, t) for g in range(PASSES) for t in (0, 2, 1, 3)]
+        w2_parts = [(g, 2 * u + v) for g in range(PASSES) for v in range(2) for u in range(2)]
         w2_grouped = keep.tile([P, len(w2_parts) * K_PASS], BF16, name="w2_grouped", tag="pairs1", align_bytes=64)
         deal(w2_grouped[:, 0:PACK * K_PASS], w2_raw[0])
         after_w2 = keep.tile([P, V + S], F32, name="after_w2", tag="w2_raw0", align_bytes=64)
@@ -192,7 +211,7 @@ def tile_picked_bev_max_e_kernel(tc, xT, w1, w2, w3, offs, near, far, out):
         put(NEAR, 3, last_near, late_packed[:])
 
         w3_raw = keep.tile([P, PACK, N], F32, name="w3_raw", align_bytes=64)
-        w3_rows = w3.rearrange("(c t e) n -> e c t n", t=PACK, e=RUN)
+        w3_rows = w3.rearrange("(c n e) m -> e c n m", n=PACK, e=RUN)
         for e in range(RUN):
             nc.sync.dma_start(out=w3_raw[e:P:RUN], in_=w3_rows[e])
         round_near(0)
@@ -210,6 +229,7 @@ def tile_picked_bev_max_e_kernel(tc, xT, w1, w2, w3, offs, near, far, out):
         nc.vector.quantize_mx(out=w3_codes[:].bitcast(FP8X4), scales=w3_scales[:],
                               in_=w3_grouped[:].rearrange("p w j -> p (w j)"))
 
+        near_halves[1] = keep.tile([P, S, 2], BF16, name="near_half1", tag="w_codes100", align_bytes=64)[:]
         round_near(2)
         round_near(3)
         far_flat = keep.tile([P, PACK * S], BF16, name="far_pairs", tag="win03")

@@ -24,10 +24,10 @@ LIST_COLS = V // 16
 NEAR, FAR = 0, 1
 HALF = H // 2
 ALL, NONE = 16, 0
-SHARE_LAST, SHARE_WIDE, SHARE_END = 6, 7, 8
-X_LOADS = (((1024, ALL), (1024, SHARE_LAST)),
-           ((1024, ALL), (512, NONE), (512, SHARE_LAST)),
-           ((512, ALL), (1024, SHARE_WIDE), (512, SHARE_LAST)),
+SHARE_LAST, SHARE_BESIDE, SHARE_END = 6, 7, 8
+X_LOADS = (((2048, SHARE_LAST),),
+           ((1024, ALL), (1024, SHARE_LAST)),
+           ((1024, SHARE_BESIDE), (1024, SHARE_LAST)),
            ((1024, ALL), (512, NONE), (512, SHARE_END)))
 CELLS = 128
 STEPS = S // CELLS
@@ -102,7 +102,6 @@ def tile_picked_bev_max_e_kernel(tc, xT, w1, w2, w3, offs, near, far, out):
         first_pairs = pairs_tile("pairs0")
         load_and_round(0, 0, 0, first_pairs)
         nc.sync.dma_start(offs_sb[:], offs)
-        load_and_round(0, 0, 1, first_pairs)
         gather(0, 0, NEAR, FAR, first_pairs)
 
         second_pairs = pairs_tile("pairs1")
@@ -112,13 +111,12 @@ def tile_picked_bev_max_e_kernel(tc, xT, w1, w2, w3, offs, near, far, out):
         gather(0, 1, FAR, FAR, second_pairs)
 
         third_pairs = pairs_tile("pairs2")
+        weave(0, NEAR, "x_woven00", nc.scalar.copy)
         load_and_round(1, 0, 0, third_pairs)
-        weave(0, NEAR, "x_raw100", nc.scalar.copy)
-        load_and_round(1, 0, 1, third_pairs)
         quantise_picked(0, NEAR, "x_codes00")
-        load_and_round(1, 0, 2, third_pairs)
+        load_and_round(1, 0, 1, third_pairs)
         gather(1, 0, NEAR, FAR, third_pairs)
-        weave(0, FAR, "x_raw102", nc.scalar.copy)
+        weave(0, FAR, "x_raw101", nc.scalar.copy)
         quantise_picked(0, FAR, "x_codes01")
 
         last_pairs = pairs_tile("pairs0")
@@ -216,7 +214,7 @@ def tile_picked_bev_max_e_kernel(tc, xT, w1, w2, w3, offs, near, far, out):
             nc.sync.dma_start(out=w3_raw[e:P:RUN], in_=w3_rows[e])
         round_near(0)
         round_near(1)
-        far_packed = keep.tile([P, PACK, V], F32, name="far_packed", tag="x_raw101", align_bytes=64)
+        far_packed = keep.tile([P, PACK, V], F32, name="far_packed", tag="x_raw100", align_bytes=64)
         for t in range(PACK):
             put(FAR, t, layer(FAR, t), far_packed[:, t, :])
 
@@ -224,7 +222,7 @@ def tile_picked_bev_max_e_kernel(tc, xT, w1, w2, w3, offs, near, far, out):
         nc.scalar.copy(w3_grouped[:].rearrange("p (c e) (u v) -> p c u v e", e=RUN, u=2),
                        w3_raw[:].rearrange("p (v u) (c e) -> p c u v e", e=RUN, u=2))
 
-        w3_codes = keep.tile([P, N], U32, name="w3_codes", tag="x_raw101", align_bytes=64)
+        w3_codes = keep.tile([P, N], U32, name="w3_codes", tag="x_raw100", align_bytes=64)
         w3_scales = keep.tile([P, N], U8, name="w3_scales", align_bytes=64)
         nc.vector.quantize_mx(out=w3_codes[:].bitcast(FP8X4), scales=w3_scales[:],
                               in_=w3_grouped[:].rearrange("p w j -> p (w j)"))
@@ -245,7 +243,7 @@ def tile_picked_bev_max_e_kernel(tc, xT, w1, w2, w3, offs, near, far, out):
             round_far(PACK - 1, c0, c1)
 
         out_view = out.rearrange("(h p) r -> p h r", p=P)
-        z_all = keep.tile([P, STEPS * CELLS * PACK], BF16, name="z_all", tag="x_raw001", align_bytes=64)
+        z_all = keep.tile([P, STEPS * CELLS * PACK], BF16, name="z_all", tag="x_raw000", align_bytes=64)
         res_all = keep.tile([P, STEPS * 2 * CELLS], F32, name="res_all", tag="x_raw110", align_bytes=64)
 
         def join(c):

@@ -14,6 +14,8 @@ FP8X4 = mybir.dt.float8_e4m3fn_x4
 COPY = mybir.ActivationFunctionType.Copy
 RELU = mybir.ActivationFunctionType.Relu
 MAX = mybir.AluOpType.max
+MULT = mybir.AluOpType.mult
+ADD = mybir.AluOpType.add
 
 P = 128
 PACK = 4
@@ -25,10 +27,10 @@ NEAR, FAR = 0, 1
 HALF = H // 2
 ALL, NONE = 16, 0
 SHARE_LAST, SHARE_BESIDE, SHARE_END = 6, 7, 8
-X_LOADS = (((2048, SHARE_LAST),),
-           ((1024, ALL), (1024, SHARE_LAST)),
-           ((1024, SHARE_BESIDE), (1024, SHARE_LAST)),
-           ((1024, ALL), (512, NONE), (512, SHARE_END)))
+X_LOADS = (((2048, 6, "vector"),),
+           ((1024, 16, None), (1024, 3, "vector")),
+           ((1024, 6, "gpsimd"), (1024, 4, "vector")),
+           ((1024, 8, "gpsimd"), (512, 16, None), (512, 5, "vector")))
 CELLS = 128
 STEPS = S // CELLS
 LAST_PIECES = (1, 2, 4, STEPS)
@@ -49,7 +51,7 @@ def tile_picked_bev_max_e_kernel(tc, xT, w1, w2, w3, offs, near, far, out):
             raw = keep.tile([P, PACK, width], F32, name=tag, tag=tag, align_bytes=64)
             rows = src[g * K_PASS:(g + 1) * K_PASS, c0:c0 + width]
             nc.sync.dma_start(out=raw[:], in_=rows.rearrange("(p j) w -> p j w", j=PACK))
-            return raw
+            return raw[:]
 
         windows = [[keep.tile([P, S], F32, name="win%d%d" % (s, t), tag="win%d%d" % (s, t)) for t in range(PACK)]
                    for s in (NEAR, FAR)]
@@ -57,44 +59,48 @@ def tile_picked_bev_max_e_kernel(tc, xT, w1, w2, w3, offs, near, far, out):
             for t in range(PACK):
                 (nc.vector, nc.gpsimd)[s].memset(windows[s][t][:], 0.0)
 
-        got = [keep.tile([P, 2, S], U32, name="got%d" % g, align_bytes=64) for g in range(PASSES)]
+        got_flat = [keep.tile([P, 2 * S + g * V], U32, name="got%d" % g, align_bytes=64) for g in range(PASSES)]
+        got = [flat[:, 0:2 * S].rearrange("p (u n) -> p u n", u=2) for flat in got_flat]
         x_woven = {}
         x_codes = {}
         x_scales = {}
 
-        def load_and_round(g, u, index, pairs):
+        def load_and_round(g, u, index, pairs, raw=None):
             loads = X_LOADS[2 * g + u]
-            c0 = sum(width for width, share in loads[:index])
-            width, share = loads[index]
+            c0 = sum(load[0] for load in loads[:index])
+            width, share, other = loads[index]
             tag = "x_raw%d%d%d" % (g, u, index)
-            raw = keep.tile([P, 2, width], F32, name=tag, tag=tag, align_bytes=64)
+            if raw is None:
+                raw = keep.tile([P, 2, width], F32, name=tag, tag=tag, align_bytes=64)[:]
             rows = xT[g * K_PASS:(g + 1) * K_PASS, :].rearrange("(p j) w -> p j w", j=PACK)
-            nc.sync.dma_start(out=raw[:], in_=rows[:, 2 * u:2 * u + 2, c0:c0 + width])
+            nc.sync.dma_start(out=raw, in_=rows[:, 2 * u:2 * u + 2, c0:c0 + width])
             split = width * share // ALL // RUN
-            src = raw[:].rearrange("p v (c e) -> p c v e", e=RUN)
+            src = raw.rearrange("p v (c e) -> p c v e", e=RUN)
             dst = pairs[:, c0:c0 + width, :].rearrange("p (c e) v -> p c v e", e=RUN)
             if share != NONE:
                 nc.scalar.activation(dst[:, 0:split], src[:, 0:split], COPY)
-            if share != ALL:
+            if other == "vector":
                 nc.vector.tensor_copy(dst[:, split:], src[:, split:])
+            if other == "gpsimd":
+                nc.gpsimd.tensor_scalar(pairs[:, c0 + split * RUN:c0 + width, :],
+                                        raw[:, :, split * RUN:].rearrange("p v w -> p w v"), 1.0, 0.0, MULT, ADD)
 
         def gather(g, u, first, last, pairs):
             window = pairs[:].rearrange("p w v -> p (w v)").bitcast(U32)
             nc.vector.tensor_copy(got[g][:, u, first * V:(last + 1) * V],
                                   window.indirect(offs_sb[:, LIST_COLS * first:LIST_COLS * (last + 1)]))
 
-        def weave(g, s, tag, copy):
-            woven = keep.tile([P, V * PACK], BF16, name="x_woven%d%d" % (g, s), tag=tag, align_bytes=64)
-            copy(woven[:].bitcast(U32).rearrange("p (c e u) -> p c u e", e=RUN, u=2),
+        def weave(g, s, woven, copy):
+            copy(woven.bitcast(U32).rearrange("p (c e u) -> p c u e", e=RUN, u=2),
                  got[g][:, :, s * V:(s + 1) * V].rearrange("p u (c e) -> p c u e", e=RUN))
             x_woven[g, s] = woven
 
         def quantise_picked(g, s, codes_tag):
             codes = keep.tile([P, V], U32, name="x_codes%d%d" % (g, s), tag=codes_tag, align_bytes=64)
             scales = keep.tile([P, V], U8, name="x_scales%d%d" % (g, s), align_bytes=64)
-            nc.vector.quantize_mx(out=codes[:].bitcast(FP8X4), scales=scales[:], in_=x_woven[g, s][:])
-            x_codes[g, s] = codes
-            x_scales[g, s] = scales
+            nc.vector.quantize_mx(out=codes[:].bitcast(FP8X4), scales=scales[:], in_=x_woven[g, s])
+            x_codes[g, s] = codes[:]
+            x_scales[g, s] = scales[:]
 
         def pairs_tile(tag):
             return keep.tile([P, T, 2], BF16, name="pairs", tag=tag, align_bytes=64)
@@ -111,25 +117,34 @@ def tile_picked_bev_max_e_kernel(tc, xT, w1, w2, w3, offs, near, far, out):
         gather(0, 1, FAR, FAR, second_pairs)
 
         third_pairs = pairs_tile("pairs2")
-        weave(0, NEAR, "x_woven00", nc.scalar.copy)
-        load_and_round(1, 0, 0, third_pairs)
-        quantise_picked(0, NEAR, "x_codes00")
-        load_and_round(1, 0, 1, third_pairs)
+        first_at = 3 * S - S * X_LOADS[2][0][1] // ALL
+        shared = keep.tile([P, first_at + 2 * S], F32, name="shared", tag="x_raw100", align_bytes=64)
+        load_and_round(1, 0, 0, third_pairs, shared[:, first_at:].rearrange("p (v w) -> p v w", v=2))
+        weave(0, NEAR, shared[:, 2 * S:3 * S].bitcast(BF16), nc.scalar.copy)
+        load_and_round(1, 0, 1, third_pairs, shared[:, 0:2 * S].rearrange("p (v w) -> p v w", v=2))
         gather(1, 0, NEAR, FAR, third_pairs)
-        weave(0, FAR, "x_raw101", nc.scalar.copy)
-        quantise_picked(0, FAR, "x_codes01")
+        weave(0, FAR, shared[:, S:2 * S].bitcast(BF16), nc.scalar.copy)
+        codes0 = keep.tile([P, S], U32, name="codes0", align_bytes=64)
+        scales0 = keep.tile([P, S], U8, name="scales0", align_bytes=64)
+        nc.vector.quantize_mx(out=codes0[:].bitcast(FP8X4), scales=scales0[:], in_=shared[:, S:3 * S].bitcast(BF16))
+        for s in (NEAR, FAR):
+            x_codes[0, s] = codes0[:, (1 - s) * V:(2 - s) * V]
+            x_scales[0, s] = scales0[:, (1 - s) * V:(2 - s) * V]
 
         last_pairs = pairs_tile("pairs0")
         for index in range(len(X_LOADS[3])):
             load_and_round(1, 1, index, last_pairs)
-        gather(1, 1, NEAR, NEAR, last_pairs)
+        last_window = last_pairs[:].rearrange("p w v -> p (w v)").bitcast(U32)
+        for half in range(2):
+            nc.vector.tensor_copy(got[1][:, 1, half * V // 2:(half + 1) * V // 2],
+                                  last_window.indirect(offs_sb[:, half * LIST_COLS // 2:(half + 1) * LIST_COLS // 2]))
 
         w_codes = {}
         w_scales = {}
 
         def deal(grouped, raw):
             dst = grouped.rearrange("p (n c e j) -> p n c j e", n=PACK, e=RUN, j=PACK)
-            src = raw[:].rearrange("p j (c n e) -> p n c j e", n=PACK, e=RUN)
+            src = raw.rearrange("p j (c n e) -> p n c j e", n=PACK, e=RUN)
             nc.scalar.copy(dst, src)
 
         def quantise_weights(s, parts, grouped):
@@ -147,7 +162,7 @@ def tile_picked_bev_max_e_kernel(tc, xT, w1, w2, w3, offs, near, far, out):
                 nc.tensor.matmul_mx(
                     out=acc[:],
                     lhsT=w_codes[s, g, t].bitcast(FP8X4), lhsT_scale=w_scales[s, g, t],
-                    rhs=x_codes[g, s][:].bitcast(FP8X4), rhs_scale=x_scales[g, s][:],
+                    rhs=x_codes[g, s].bitcast(FP8X4), rhs_scale=x_scales[g, s],
                     start=(g == 0), stop=(g == PASSES - 1),
                 )
             return acc
@@ -156,17 +171,23 @@ def tile_picked_bev_max_e_kernel(tc, xT, w1, w2, w3, offs, near, far, out):
             nc.scalar.activation(packed, acc[:], RELU)
             nc.vector.tensor_copy(windows[s][t][:].indirect(cell_lists[s][:]), packed)
 
-        w1_low = [load_pass(w1, g, 0, HALF, "w1_low%d" % g) for g in range(PASSES)]
+        w1_low = [load_pass(w1, 0, 0, HALF, "w1_low0"),
+                  got_flat[1][:, S + V:].bitcast(F32).rearrange("p (j w) -> p j w", j=PACK)]
+        nc.sync.dma_start(out=w1_low[1], in_=w1[K_PASS:, 0:HALF].rearrange("(p j) w -> p j w", j=PACK))
         nc.sync.dma_start(near_sb[:], near)
         w1_high = [load_pass(w1, g, HALF, HALF, "w1_high%d" % g) for g in range(PASSES)]
         nc.sync.dma_start(far_sb[:], far)
 
-        weave(1, NEAR, "x_woven10", nc.vector.tensor_copy)
+        x_woven[1, NEAR] = keep.tile([P, V * PACK], BF16, name="x_woven10", align_bytes=64)[:]
+        for half in range(2):
+            words = x_woven[1, NEAR].bitcast(U32)[:, half * V:(half + 1) * V]
+            nc.vector.tensor_copy(words.rearrange("p (c e u) -> p c u e", e=RUN, u=2),
+                                  got[1][:, :, half * V // 2:(half + 1) * V // 2].rearrange("p u (c e) -> p c u e", e=RUN))
         first_grouped = keep.tile([P, 2 * K_PASS], BF16, name="first_grouped", tag="first_grouped", align_bytes=64)
         deal(first_grouped[:], w1_low[0])
         quantise_weights(NEAR, [(0, 0), (0, 1)], first_grouped[:])
-        quantise_picked(1, NEAR, "first_grouped")
-        second_grouped = got[1][:, 1, V:].bitcast(BF16)
+        quantise_picked(1, NEAR, "w1_low0")
+        second_grouped = keep.tile([P, 2 * K_PASS], BF16, name="second_grouped", align_bytes=64)[:]
         deal(second_grouped, w1_low[1])
         quantise_weights(NEAR, [(1, 0), (1, 1)], second_grouped)
         gather(1, 1, FAR, FAR, last_pairs)
@@ -192,7 +213,8 @@ def tile_picked_bev_max_e_kernel(tc, xT, w1, w2, w3, offs, near, far, out):
         quantise_weights(NEAR, [(1, 2), (1, 3)], fourth_grouped[:])
         packed1 = keep.tile([P, V], F32, name="packed1", tag="w1_high1", align_bytes=64)
         put(NEAR, 1, layer(NEAR, 1), packed1[:])
-        weave(1, FAR, "w_scales010", nc.scalar.copy)
+        far_woven = keep.tile([P, V * PACK], BF16, name="far_woven", tag="w_scales010", align_bytes=64)
+        weave(1, FAR, far_woven[:], nc.scalar.copy)
         quantise_picked(1, FAR, "x_codes11")
 
         w2_raw = [load_pass(w2, g, 0, H, "w2_raw%d" % g) for g in range(PASSES)]
@@ -222,7 +244,7 @@ def tile_picked_bev_max_e_kernel(tc, xT, w1, w2, w3, offs, near, far, out):
         nc.scalar.copy(w3_grouped[:].rearrange("p (c e) (u v) -> p c u v e", e=RUN, u=2),
                        w3_raw[:].rearrange("p (v u) (c e) -> p c u v e", e=RUN, u=2))
 
-        w3_codes = keep.tile([P, N], U32, name="w3_codes", tag="x_raw100", align_bytes=64)
+        w3_codes = keep.tile([P, N], U32, name="w3_codes", align_bytes=64)
         w3_scales = keep.tile([P, N], U8, name="w3_scales", align_bytes=64)
         nc.vector.quantize_mx(out=w3_codes[:].bitcast(FP8X4), scales=w3_scales[:],
                               in_=w3_grouped[:].rearrange("p w j -> p (w j)"))

@@ -28,7 +28,7 @@ HALF = H // 2
 ALL, NONE = 16, 0
 SHARE_LAST, SHARE_BESIDE, SHARE_END = 6, 7, 8
 X_LOADS = (((2048, 6, "vector"),),
-           ((1024, 16, None), (1024, 3, "vector")),
+           ((1024, 8, "gpsimd"), (1024, 5, "vector")),
            ((1024, 6, "gpsimd"), (1024, 4, "vector")),
            ((1024, 8, "gpsimd"), (512, 16, None), (512, 5, "vector")))
 CELLS = 128
@@ -142,10 +142,16 @@ def tile_picked_bev_max_e_kernel(tc, xT, w1, w2, w3, offs, near, far, out):
         w_codes = {}
         w_scales = {}
 
-        def deal(grouped, raw):
-            dst = grouped.rearrange("p (n c e j) -> p n c j e", n=PACK, e=RUN, j=PACK)
+        def deal(grouped, raw, n0=0, n1=PACK):
+            dst = grouped.rearrange("p (n c e j) -> p n c j e", n=n1 - n0, e=RUN, j=PACK)
             src = raw.rearrange("p j (c n e) -> p n c j e", n=PACK, e=RUN)
-            nc.scalar.copy(dst, src)
+            nc.scalar.copy(dst, src[:, n0:n1])
+
+        def deal_on_gpsimd(grouped, raw):
+            dst = grouped.rearrange("p (n c e j) -> p n c e j", n=PACK, e=RUN, j=PACK)
+            src = raw.rearrange("p j (c n e) -> p n c e j", n=PACK, e=RUN)
+            for n in range(PACK):
+                nc.gpsimd.tensor_scalar(dst[:, n], src[:, n], 1.0, 0.0, MULT, ADD)
 
         def quantise_weights(s, parts, grouped):
             name = "%d%d%d" % ((s,) + parts[0])
@@ -183,17 +189,20 @@ def tile_picked_bev_max_e_kernel(tc, xT, w1, w2, w3, offs, near, far, out):
             words = x_woven[1, NEAR].bitcast(U32)[:, half * V:(half + 1) * V]
             nc.vector.tensor_copy(words.rearrange("p (c e u) -> p c u e", e=RUN, u=2),
                                   got[1][:, :, half * V // 2:(half + 1) * V // 2].rearrange("p u (c e) -> p c u e", e=RUN))
-        first_grouped = keep.tile([P, 2 * K_PASS], BF16, name="first_grouped", tag="first_grouped", align_bytes=64)
-        deal(first_grouped[:], w1_low[0])
-        quantise_weights(NEAR, [(0, 0), (0, 1)], first_grouped[:])
+        first_grouped = keep.tile([P, K_PASS], BF16, name="first_grouped", align_bytes=64)
+        third_grouped = keep.tile([P, 2 * K_PASS], BF16, name="third_grouped", tag="third_grouped", align_bytes=64)
+        deal(first_grouped[:], w1_low[0], 0, 2)
+        quantise_weights(NEAR, [(0, 0)], first_grouped[:])
+        deal(third_grouped[:, 0:K_PASS], w1_low[0], 2, 4)
         quantise_picked(1, NEAR, "w1_low0")
-        second_grouped = keep.tile([P, 2 * K_PASS], BF16, name="second_grouped", align_bytes=64)[:]
-        deal(second_grouped, w1_low[1])
-        quantise_weights(NEAR, [(1, 0), (1, 1)], second_grouped)
+        second_grouped = keep.tile([P, K_PASS], BF16, name="second_grouped", align_bytes=64)
+        deal(second_grouped[:], w1_low[1], 0, 2)
+        quantise_weights(NEAR, [(1, 0)], second_grouped[:])
+        deal(third_grouped[:, K_PASS:], w1_low[1], 2, 4)
+        quantise_weights(NEAR, [(0, 1), (1, 1)], third_grouped[:])
         gather(1, 1, FAR, FAR, last_pairs)
-        third_grouped = keep.tile([P, 2 * K_PASS], BF16, name="third_grouped", align_bytes=64)
-        deal(third_grouped[:], w1_high[0])
-        quantise_weights(NEAR, [(0, 2), (0, 3)], third_grouped[:])
+        high_grouped = keep.tile([P, 2 * K_PASS], BF16, name="high_grouped", tag="third_grouped", align_bytes=64)
+        deal_on_gpsimd(high_grouped[:], w1_high[0])
 
         near_pairs = keep.tile([P, 2, S, 2], BF16, name="near_pairs", tag="pairs0", align_bytes=64)
         near_halves = {}
@@ -207,13 +216,26 @@ def tile_picked_bev_max_e_kernel(tc, xT, w1, w2, w3, offs, near, far, out):
                                       in_=near_halves[h][P // 2 * u:P // 2 * (u + 1)])
 
         packed0 = keep.tile([P, V], F32, name="packed0", tag="x_raw010", align_bytes=64)
-        put(NEAR, 0, layer(NEAR, 0), packed0[:])
-        fourth_grouped = keep.tile([P, 2 * K_PASS], BF16, name="fourth_grouped", tag="w_codes010", align_bytes=64)
+        halves = [psum.tile([P, V], F32, name="first_acc", tag="first_acc", bufs=2)[:, 0:V // 2] for h in range(2)]
+        for g in range(PASSES):
+            for h in range(2):
+                entries = slice(h * V // 2, (h + 1) * V // 2)
+                nc.tensor.matmul_mx(
+                    out=halves[h],
+                    lhsT=w_codes[NEAR, g, 0].bitcast(FP8X4), lhsT_scale=w_scales[NEAR, g, 0],
+                    rhs=x_codes[g, NEAR][:, entries].bitcast(FP8X4), rhs_scale=x_scales[g, NEAR][:, entries],
+                    start=(g == 0), stop=(g == PASSES - 1),
+                )
+        for h in range(2):
+            nc.scalar.activation(packed0[:, h * V // 2:(h + 1) * V // 2], halves[h], RELU)
+        nc.vector.tensor_copy(windows[NEAR][0][:].indirect(near_sb[:]), packed0[:])
+        quantise_weights(NEAR, [(0, 2), (0, 3)], high_grouped[:])
+        fourth_grouped = keep.tile([P, 2 * K_PASS], BF16, name="fourth_grouped", tag="w_codes001", align_bytes=64)
         deal(fourth_grouped[:], w1_high[1])
         quantise_weights(NEAR, [(1, 2), (1, 3)], fourth_grouped[:])
         packed1 = keep.tile([P, V], F32, name="packed1", tag="w1_high1", align_bytes=64)
         put(NEAR, 1, layer(NEAR, 1), packed1[:])
-        far_woven = keep.tile([P, V * PACK], BF16, name="far_woven", tag="w_scales010", align_bytes=64)
+        far_woven = keep.tile([P, V * PACK], BF16, name="far_woven", tag="w_scales001", align_bytes=64)
         weave(1, FAR, far_woven[:], nc.scalar.copy)
         quantise_picked(1, FAR, "x_codes11")
 

@@ -24,13 +24,7 @@ K_PASS = P * PACK
 PASSES = K // K_PASS
 LIST_COLS = V // 16
 NEAR, FAR = 0, 1
-HALF = H // 2
-ALL, NONE = 16, 0
-SHARE_LAST, SHARE_BESIDE, SHARE_END = 6, 7, 8
-X_LOADS = (((2048, 6, "vector"),),
-           ((1024, 8, "gpsimd"), (1024, 5, "vector")),
-           ((1024, 6, "gpsimd"), (1024, 4, "vector")),
-           ((1024, 8, "gpsimd"), (512, 16, None), (512, 5, "vector")))
+PIECE = V // 2
 CELLS = 128
 STEPS = S // CELLS
 LAST_PIECES = (1, 2, 4, STEPS)
@@ -40,255 +34,198 @@ def tile_picked_bev_max_e_kernel(tc, xT, w1, w2, w3, offs, near, far, out):
     nc = tc.nc
     with ExitStack() as ctx:
         keep = ctx.enter_context(tc.tile_pool(name="keep", bufs=1))
-        psum = ctx.enter_context(tc.psum_pool(name="psum", bufs=2))
+        psum = ctx.enter_context(tc.psum_pool(name="psum", bufs=1))
 
         offs_sb = keep.tile([P, S // 16], U16, name="offs_sb")
         near_sb = keep.tile([P, LIST_COLS], U16, name="near_sb")
         far_sb = keep.tile([P, LIST_COLS], U16, name="far_sb")
         cell_lists = (near_sb, far_sb)
 
-        def load_pass(src, g, c0, width, tag):
-            raw = keep.tile([P, PACK, width], F32, name=tag, tag=tag, align_bytes=64)
-            rows = src[g * K_PASS:(g + 1) * K_PASS, c0:c0 + width]
-            nc.sync.dma_start(out=raw[:], in_=rows.rearrange("(p j) w -> p j w", j=PACK))
+        windows = [[keep.tile([P, S], F32, name="win%d%d" % (s, n)) for n in range(PACK)] for s in (NEAR, FAR)]
+        for s in (NEAR, FAR):
+            for n in range(PACK):
+                (nc.vector, nc.gpsimd)[s].memset(windows[s][n][:], 0.0)
+
+        def quantise(name, grouped):
+            width = grouped.shape[1] // PACK
+            codes = keep.tile([P, width], U32, name="codes_" + name, align_bytes=64)
+            scales = keep.tile([P, width], U8, name="scales_" + name, align_bytes=64)
+            nc.vector.quantize_mx(out=codes[:].bitcast(FP8X4), scales=scales[:], in_=grouped)
+            return codes, scales
+
+        woven = [keep.tile([P, S, PACK], BF16, name="woven%d" % g, align_bytes=64) for g in range(PASSES)]
+        planes = [keep.tile([P, PACK, V], BF16, name="planes%d" % g, align_bytes=64) for g in range(PASSES)]
+        x_ops = {}
+        for g in range(PASSES):
+            rows = xT[g * K_PASS:(g + 1) * K_PASS, :].rearrange("(p j) w -> p j w", j=PACK)
+            for j in range(PACK):
+                tag = "x_row%d%d" % (g, j)
+                row = keep.tile([P, T], F32, name=tag, tag=tag, align_bytes=64)
+                nc.sync.dma_start(out=row[:], in_=rows[:, j, :])
+                if g == 0 and j == 0:
+                    nc.sync.dma_start(offs_sb[:], offs)
+                nc.vector.tensor_copy(woven[g][:, 0:V, j], row[:].indirect(offs_sb[:, 0:LIST_COLS]))
+                nc.scalar.activation(planes[g][:, j, :], row[:].indirect(offs_sb[:, LIST_COLS:]), COPY)
+            if g == 0:
+                nc.gpsimd.tensor_scalar(woven[0][:, V:, :], planes[0][:].rearrange("p j v -> p v j"),
+                                        1.0, 0.0, MULT, ADD)
+                codes, scales = quantise("x0", woven[0][:].rearrange("p v j -> p (v j)"))
+                for s in (NEAR, FAR):
+                    x_ops[0, s] = (codes[:, s * V:(s + 1) * V], scales[:, s * V:(s + 1) * V])
+        codes, scales = quantise("x10", woven[1][:, 0:V, :].rearrange("p v j -> p (v j)"))
+        x_ops[1, NEAR] = (codes[:], scales[:])
+        nc.scalar.copy(woven[1][:, V:, :].rearrange("p (c e) j -> p c j e", e=RUN),
+                       planes[1][:].rearrange("p j (c e) -> p c j e", e=RUN))
+
+        def load_pass(src, g, name):
+            raw = keep.tile([P, PACK, H], F32, name=name, tag=name, align_bytes=64)
+            nc.sync.dma_start(out=raw[:], in_=src[g * K_PASS:(g + 1) * K_PASS, :].rearrange("(p j) w -> p j w", j=PACK))
             return raw[:]
 
-        windows = [[keep.tile([P, S], F32, name="win%d%d" % (s, t), tag="win%d%d" % (s, t)) for t in range(PACK)]
-                   for s in (NEAR, FAR)]
-        for s in (NEAR, FAR):
-            for t in range(PACK):
-                (nc.vector, nc.gpsimd)[s].memset(windows[s][t][:], 0.0)
-
-        got_flat = [keep.tile([P, 2 * S + g * V], U32, name="got%d" % g, align_bytes=64) for g in range(PASSES)]
-        got = [flat[:, 0:2 * S].rearrange("p (u n) -> p u n", u=2) for flat in got_flat]
-        x_woven = {}
-        x_codes = {}
-        x_scales = {}
-
-        def load_and_round(g, u, index, pairs, raw=None):
-            loads = X_LOADS[2 * g + u]
-            c0 = sum(load[0] for load in loads[:index])
-            width, share, other = loads[index]
-            tag = "x_raw%d%d%d" % (g, u, index)
-            if raw is None:
-                raw = keep.tile([P, 2, width], F32, name=tag, tag=tag, align_bytes=64)[:]
-            rows = xT[g * K_PASS:(g + 1) * K_PASS, :].rearrange("(p j) w -> p j w", j=PACK)
-            nc.sync.dma_start(out=raw, in_=rows[:, 2 * u:2 * u + 2, c0:c0 + width])
-            split = width * share // ALL // RUN
-            src = raw.rearrange("p v (c e) -> p c v e", e=RUN)
-            dst = pairs[:, c0:c0 + width, :].rearrange("p (c e) v -> p c v e", e=RUN)
-            if share != NONE:
-                nc.scalar.activation(dst[:, 0:split], src[:, 0:split], COPY)
-            if other == "vector":
-                nc.vector.tensor_copy(dst[:, split:], src[:, split:])
-            if other == "gpsimd":
-                nc.gpsimd.tensor_scalar(pairs[:, c0 + split * RUN:c0 + width, :],
-                                        raw[:, :, split * RUN:].rearrange("p v w -> p w v"), 1.0, 0.0, MULT, ADD)
-
-        def gather(g, u, first, last, pairs):
-            window = pairs[:].rearrange("p w v -> p (w v)").bitcast(U32)
-            nc.vector.tensor_copy(got[g][:, u, first * V:(last + 1) * V],
-                                  window.indirect(offs_sb[:, LIST_COLS * first:LIST_COLS * (last + 1)]))
-
-        def weave(g, s, woven, copy):
-            copy(woven.bitcast(U32).rearrange("p (c e u) -> p c u e", e=RUN, u=2),
-                 got[g][:, :, s * V:(s + 1) * V].rearrange("p u (c e) -> p c u e", e=RUN))
-            x_woven[g, s] = woven
-
-        def quantise_picked(g, s, codes_tag):
-            codes = keep.tile([P, V], U32, name="x_codes%d%d" % (g, s), tag=codes_tag, align_bytes=64)
-            scales = keep.tile([P, V], U8, name="x_scales%d%d" % (g, s), align_bytes=64)
-            nc.vector.quantize_mx(out=codes[:].bitcast(FP8X4), scales=scales[:], in_=x_woven[g, s])
-            x_codes[g, s] = codes[:]
-            x_scales[g, s] = scales[:]
-
-        def pairs_tile(tag):
-            return keep.tile([P, T, 2], BF16, name="pairs", tag=tag, align_bytes=64)
-
-        first_pairs = pairs_tile("pairs0")
-        load_and_round(0, 0, 0, first_pairs)
-        nc.sync.dma_start(offs_sb[:], offs)
-        gather(0, 0, NEAR, FAR, first_pairs)
-
-        second_pairs = pairs_tile("pairs1")
-        for index in range(len(X_LOADS[1])):
-            load_and_round(0, 1, index, second_pairs)
-        gather(0, 1, NEAR, NEAR, second_pairs)
-        gather(0, 1, FAR, FAR, second_pairs)
-
-        third_pairs = pairs_tile("pairs2")
-        first_at = 3 * S - S * X_LOADS[2][0][1] // ALL
-        shared = keep.tile([P, first_at + 2 * S], F32, name="shared", tag="x_raw100", align_bytes=64)
-        load_and_round(1, 0, 0, third_pairs, shared[:, first_at:].rearrange("p (v w) -> p v w", v=2))
-        weave(0, NEAR, shared[:, 2 * S:3 * S].bitcast(BF16), nc.scalar.copy)
-        load_and_round(1, 0, 1, third_pairs, shared[:, 0:2 * S].rearrange("p (v w) -> p v w", v=2))
-        gather(1, 0, NEAR, FAR, third_pairs)
-        weave(0, FAR, shared[:, S:2 * S].bitcast(BF16), nc.scalar.copy)
-        codes0 = keep.tile([P, S], U32, name="codes0", align_bytes=64)
-        scales0 = keep.tile([P, S], U8, name="scales0", align_bytes=64)
-        nc.vector.quantize_mx(out=codes0[:].bitcast(FP8X4), scales=scales0[:], in_=shared[:, S:3 * S].bitcast(BF16))
-        for s in (NEAR, FAR):
-            x_codes[0, s] = codes0[:, (1 - s) * V:(2 - s) * V]
-            x_scales[0, s] = scales0[:, (1 - s) * V:(2 - s) * V]
-
-        last_pairs = pairs_tile("pairs0")
-        for index in range(len(X_LOADS[3])):
-            load_and_round(1, 1, index, last_pairs)
-        last_window = last_pairs[:].rearrange("p w v -> p (w v)").bitcast(U32)
-        for half in range(2):
-            nc.vector.tensor_copy(got[1][:, 1, half * V // 2:(half + 1) * V // 2],
-                                  last_window.indirect(offs_sb[:, half * LIST_COLS // 2:(half + 1) * LIST_COLS // 2]))
-
-        w_codes = {}
-        w_scales = {}
-
-        def deal(grouped, raw, n0=0, n1=PACK):
+        def deal(copy, grouped, raw, n0, n1):
             dst = grouped.rearrange("p (n c e j) -> p n c j e", n=n1 - n0, e=RUN, j=PACK)
             src = raw.rearrange("p j (c n e) -> p n c j e", n=PACK, e=RUN)
-            nc.scalar.copy(dst, src[:, n0:n1])
+            copy(dst, src[:, n0:n1])
 
-        def deal_on_gpsimd(grouped, raw):
-            dst = grouped.rearrange("p (n c e j) -> p n c e j", n=PACK, e=RUN, j=PACK)
+        def deal_on_gpsimd(grouped, raw, n0, n1):
+            dst = grouped.rearrange("p (n c e j) -> p n c e j", n=n1 - n0, e=RUN, j=PACK)
             src = raw.rearrange("p j (c n e) -> p n c e j", n=PACK, e=RUN)
-            for n in range(PACK):
-                nc.gpsimd.tensor_scalar(dst[:, n], src[:, n], 1.0, 0.0, MULT, ADD)
+            for n in range(n0, n1):
+                nc.gpsimd.tensor_scalar(dst[:, n - n0], src[:, n], 1.0, 0.0, MULT, ADD)
 
-        def quantise_weights(s, parts, grouped):
-            name = "%d%d%d" % ((s,) + parts[0])
-            codes = keep.tile([P, len(parts) * P], U32, name="w_codes" + name, tag="w_codes" + name, align_bytes=64)
-            scales = keep.tile([P, len(parts) * P], U8, name="w_scales" + name, tag="w_scales" + name, align_bytes=64)
-            nc.vector.quantize_mx(out=codes[:].bitcast(FP8X4), scales=scales[:], in_=grouped)
-            for n, (g, t) in enumerate(parts):
-                w_codes[s, g, t] = codes[:, n * P:(n + 1) * P]
-                w_scales[s, g, t] = scales[:, n * P:(n + 1) * P]
+        def grouped_tile(name, tiles):
+            return keep.tile([P, tiles * K_PASS], BF16, name=name, tag=name, align_bytes=64)
 
-        def layer(s, t):
-            acc = psum.tile([P, V], F32, name="acc", tag="acc%d" % s, bufs=(2, 4)[s])
-            for g in range(PASSES):
-                nc.tensor.matmul_mx(
-                    out=acc[:],
-                    lhsT=w_codes[s, g, t].bitcast(FP8X4), lhsT_scale=w_scales[s, g, t],
-                    rhs=x_codes[g, s].bitcast(FP8X4), rhs_scale=x_scales[g, s],
-                    start=(g == 0), stop=(g == PASSES - 1),
-                )
-            return acc
+        w_ops = {}
+        banks = {(s, n): psum.tile([P, V], F32, name="acc", tag="bank%d" % (PACK * s + n))
+                 for s in (NEAR, FAR) for n in range(PACK)}
 
-        def put(s, t, acc, packed):
-            nc.scalar.activation(packed, acc[:], RELU)
-            nc.vector.tensor_copy(windows[s][t][:].indirect(cell_lists[s][:]), packed)
+        def quantise_weights(s, g, n0, n1, grouped):
+            codes, scales = quantise("w%d%d%d" % (s, g, n0), grouped)
+            for n in range(n0, n1):
+                cols = slice((n - n0) * P, (n - n0 + 1) * P)
+                w_ops[s, g, n] = (codes[:, cols], scales[:, cols])
 
-        w1_low = [load_pass(w1, 0, 0, HALF, "w1_low0"),
-                  got_flat[1][:, S + V:].bitcast(F32).rearrange("p (j w) -> p j w", j=PACK)]
-        nc.sync.dma_start(out=w1_low[1], in_=w1[K_PASS:, 0:HALF].rearrange("(p j) w -> p j w", j=PACK))
+        def multiply(s, g, n):
+            nc.tensor.matmul_mx(
+                out=banks[s, n][:],
+                lhsT=w_ops[s, g, n][0].bitcast(FP8X4), lhsT_scale=w_ops[s, g, n][1],
+                rhs=x_ops[g, s][0].bitcast(FP8X4), rhs_scale=x_ops[g, s][1],
+                start=(g == 0), stop=(g == PASSES - 1),
+            )
+
+        def leave_on_vector(packed, acc):
+            nc.vector.tensor_scalar_max(packed, acc, 0.0)
+
+        def leave_on_scalar(packed, acc):
+            nc.scalar.activation(packed, acc, RELU)
+
+        def scatter_on_vector(s, n, first, packed):
+            cols = slice(first // 16, (first + packed.shape[1]) // 16)
+            nc.vector.tensor_copy(windows[s][n][:].indirect(cell_lists[s][:, cols]), packed)
+
+        def scatter_on_scalar(s, n, packed):
+            for first in range(0, V, PIECE):
+                cols = slice(first // 16, (first + PIECE) // 16)
+                nc.scalar.activation(windows[s][n][:].indirect(cell_lists[s][:, cols]), packed[:, first:first + PIECE],
+                                     COPY)
+
+        def packed_tile(name, width=V, tag=None):
+            return keep.tile([P, width], F32, name=name, tag=tag or name, align_bytes=64)[:]
+
+        w1_raw = [load_pass(w1, g, "w1_raw%d" % g) for g in range(PASSES)]
         nc.sync.dma_start(near_sb[:], near)
-        w1_high = [load_pass(w1, g, HALF, HALF, "w1_high%d" % g) for g in range(PASSES)]
+        w2_raw = [load_pass(w2, g, "w2_raw%d" % g) for g in range(PASSES)]
         nc.sync.dma_start(far_sb[:], far)
-
-        x_woven[1, NEAR] = keep.tile([P, V * PACK], BF16, name="x_woven10", align_bytes=64)[:]
-        for half in range(2):
-            words = x_woven[1, NEAR].bitcast(U32)[:, half * V:(half + 1) * V]
-            nc.vector.tensor_copy(words.rearrange("p (c e u) -> p c u e", e=RUN, u=2),
-                                  got[1][:, :, half * V // 2:(half + 1) * V // 2].rearrange("p u (c e) -> p c u e", e=RUN))
-        first_grouped = keep.tile([P, K_PASS], BF16, name="first_grouped", align_bytes=64)
-        third_grouped = keep.tile([P, 2 * K_PASS], BF16, name="third_grouped", tag="third_grouped", align_bytes=64)
-        deal(first_grouped[:], w1_low[0], 0, 2)
-        quantise_weights(NEAR, [(0, 0)], first_grouped[:])
-        deal(third_grouped[:, 0:K_PASS], w1_low[0], 2, 4)
-        quantise_picked(1, NEAR, "w1_low0")
-        second_grouped = keep.tile([P, K_PASS], BF16, name="second_grouped", align_bytes=64)
-        deal(second_grouped[:], w1_low[1], 0, 2)
-        quantise_weights(NEAR, [(1, 0)], second_grouped[:])
-        deal(third_grouped[:, K_PASS:], w1_low[1], 2, 4)
-        quantise_weights(NEAR, [(0, 1), (1, 1)], third_grouped[:])
-        gather(1, 1, FAR, FAR, last_pairs)
-        high_grouped = keep.tile([P, 2 * K_PASS], BF16, name="high_grouped", tag="third_grouped", align_bytes=64)
-        deal_on_gpsimd(high_grouped[:], w1_high[0])
-
-        near_pairs = keep.tile([P, 2, S, 2], BF16, name="near_pairs", tag="pairs0", align_bytes=64)
-        near_halves = {}
-
-        def round_near(t):
-            h = t // 2
-            nc.scalar.activation(near_halves[h][:, :, t % 2], windows[NEAR][t][:], COPY)
-            if t % 2 == 1:
-                for u in range(2):
-                    nc.sync.dma_start(out=near_pairs[P // 2 * h:P // 2 * (h + 1), u],
-                                      in_=near_halves[h][P // 2 * u:P // 2 * (u + 1)])
-
-        packed0 = keep.tile([P, V], F32, name="packed0", tag="x_raw010", align_bytes=64)
-        halves = [psum.tile([P, V], F32, name="first_acc", tag="first_acc", bufs=2)[:, 0:V // 2] for h in range(2)]
-        for g in range(PASSES):
-            for h in range(2):
-                entries = slice(h * V // 2, (h + 1) * V // 2)
-                nc.tensor.matmul_mx(
-                    out=halves[h],
-                    lhsT=w_codes[NEAR, g, 0].bitcast(FP8X4), lhsT_scale=w_scales[NEAR, g, 0],
-                    rhs=x_codes[g, NEAR][:, entries].bitcast(FP8X4), rhs_scale=x_scales[g, NEAR][:, entries],
-                    start=(g == 0), stop=(g == PASSES - 1),
-                )
-        for h in range(2):
-            nc.scalar.activation(packed0[:, h * V // 2:(h + 1) * V // 2], halves[h], RELU)
-        nc.vector.tensor_copy(windows[NEAR][0][:].indirect(near_sb[:]), packed0[:])
-        quantise_weights(NEAR, [(0, 2), (0, 3)], high_grouped[:])
-        fourth_grouped = keep.tile([P, 2 * K_PASS], BF16, name="fourth_grouped", tag="w_codes001", align_bytes=64)
-        deal(fourth_grouped[:], w1_high[1])
-        quantise_weights(NEAR, [(1, 2), (1, 3)], fourth_grouped[:])
-        packed1 = keep.tile([P, V], F32, name="packed1", tag="w1_high1", align_bytes=64)
-        put(NEAR, 1, layer(NEAR, 1), packed1[:])
-        far_woven = keep.tile([P, V * PACK], BF16, name="far_woven", tag="w_scales001", align_bytes=64)
-        weave(1, FAR, far_woven[:], nc.scalar.copy)
-        quantise_picked(1, FAR, "x_codes11")
-
-        w2_raw = [load_pass(w2, g, 0, H, "w2_raw%d" % g) for g in range(PASSES)]
-        w2_parts = [(g, 2 * u + v) for g in range(PASSES) for v in range(2) for u in range(2)]
-        w2_grouped = keep.tile([P, len(w2_parts) * K_PASS], BF16, name="w2_grouped", tag="pairs1", align_bytes=64)
-        deal(w2_grouped[:, 0:PACK * K_PASS], w2_raw[0])
-        after_w2 = keep.tile([P, V + S], F32, name="after_w2", tag="w2_raw0", align_bytes=64)
-        near_halves[0] = after_w2[:, V:].bitcast(BF16).rearrange("p (r v) -> p r v", v=2)
-        put(NEAR, 2, layer(NEAR, 2), after_w2[:, 0:V])
-        last_near = layer(NEAR, 3)
-        deal(w2_grouped[:, PACK * K_PASS:], w2_raw[1])
-        quantise_weights(FAR, w2_parts, w2_grouped[:])
-        late_packed = keep.tile([P, V], F32, name="late_packed", tag="w2_raw1", align_bytes=64)
-        put(NEAR, 3, last_near, late_packed[:])
-
         w3_raw = keep.tile([P, PACK, N], F32, name="w3_raw", align_bytes=64)
         w3_rows = w3.rearrange("(c n e) m -> e c n m", n=PACK, e=RUN)
         for e in range(RUN):
             nc.sync.dma_start(out=w3_raw[e:P:RUN], in_=w3_rows[e])
-        round_near(0)
-        round_near(1)
-        far_packed = keep.tile([P, PACK, V], F32, name="far_packed", tag="x_raw100", align_bytes=64)
-        for t in range(PACK):
-            put(FAR, t, layer(FAR, t), far_packed[:, t, :])
 
-        w3_grouped = keep.tile([P, N, PACK], BF16, name="w3_grouped", tag="w_scales100", align_bytes=64)
-        nc.scalar.copy(w3_grouped[:].rearrange("p (c e) (u v) -> p c u v e", e=RUN, u=2),
-                       w3_raw[:].rearrange("p (v u) (c e) -> p c u v e", e=RUN, u=2))
+        low = grouped_tile("w1_00", 2)
+        deal(nc.vector.tensor_copy, low[:], w1_raw[0], 0, 2)
+        high = grouped_tile("w1_02", 2)
+        deal(nc.scalar.copy, high[:], w1_raw[0], 2, 4)
+        quantise_weights(NEAR, 0, 0, 2, low[:])
+        multiply(NEAR, 0, 0)
+        multiply(NEAR, 0, 1)
+        codes, scales = quantise("x11", woven[1][:, V:, :].rearrange("p v j -> p (v j)"))
+        x_ops[1, FAR] = (codes[:], scales[:])
+        first = grouped_tile("w1_10", 1)
+        deal(nc.vector.tensor_copy, first[:], w1_raw[1], 0, 1)
+        second = grouped_tile("w1_11", 1)
+        deal(nc.scalar.copy, second[:], w1_raw[1], 1, 2)
+        quantise_weights(NEAR, 0, 2, 4, high[:])
+        quantise_weights(NEAR, 1, 0, 1, first[:])
+        multiply(NEAR, 1, 0)
+        quantise_weights(NEAR, 1, 1, 2, second[:])
+        multiply(NEAR, 1, 1)
+        rest = grouped_tile("w1_12", 2)
+        deal(nc.vector.tensor_copy, rest[:, 0:K_PASS], w1_raw[1], 2, 3)
+        deal(nc.scalar.copy, rest[:, K_PASS:], w1_raw[1], 3, 4)
+        quantise_weights(NEAR, 1, 2, 4, rest[:])
+        for g in range(PASSES):
+            multiply(NEAR, g, 3)
+        for g in range(PASSES):
+            multiply(NEAR, g, 2)
 
-        w3_codes = keep.tile([P, N], U32, name="w3_codes", align_bytes=64)
-        w3_scales = keep.tile([P, N], U8, name="w3_scales", align_bytes=64)
-        nc.vector.quantize_mx(out=w3_codes[:].bitcast(FP8X4), scales=w3_scales[:],
-                              in_=w3_grouped[:].rearrange("p w j -> p (w j)"))
+        packed = packed_tile("near0")
+        leave_on_vector(packed, banks[NEAR, 0][:])
+        scatter_on_vector(NEAR, 0, 0, packed)
+        for n in (1, 3):
+            packed = packed_tile("near%d" % n)
+            leave_on_scalar(packed, banks[NEAR, n][:])
+            scatter_on_scalar(NEAR, n, packed)
 
-        near_halves[1] = keep.tile([P, S, 2], BF16, name="near_half1", tag="w_codes100", align_bytes=64)[:]
-        round_near(2)
-        round_near(3)
-        far_flat = keep.tile([P, PACK * S], BF16, name="far_pairs", tag="win03")
+        w2_first = grouped_tile("w2_00", PACK)
+        deal_on_gpsimd(w2_first[:], w2_raw[0], 0, PACK)
+        quantise_weights(FAR, 0, 0, PACK, w2_first[:])
+        for n in (1, 0, 2, 3):
+            multiply(FAR, 0, n)
+        for half in range(2):
+            name = "w2_1%d" % half
+            grouped = grouped_tile(name, 2)
+            deal_on_gpsimd(grouped[:], w2_raw[1], 2 * half, 2 * half + 2)
+            quantise_weights(FAR, 1, 2 * half, 2 * half + 2, grouped[:])
+            for n in ((1, 0), (2, 3))[half]:
+                multiply(FAR, 1, n)
+            packed = packed_tile("near2%d" % half, PIECE, name)
+            leave_on_vector(packed, banks[NEAR, 2][:, half * PIECE:(half + 1) * PIECE])
+            scatter_on_vector(NEAR, 2, half * PIECE, packed)
+
+        w3_grouped = keep.tile([P, N, PACK], BF16, name="w3_grouped", align_bytes=64)
+        nc.gpsimd.tensor_scalar(w3_grouped[:], w3_raw[:].rearrange("p n m -> p m n"), 1.0, 0.0, MULT, ADD)
+
+        far_packed = [packed_tile("far%d" % n) for n in range(PACK)]
+        leave_on_vector(far_packed[0], banks[FAR, 0][:])
+        scatter_on_vector(FAR, 0, 0, far_packed[0])
+        leave_on_scalar(far_packed[1], banks[FAR, 1][:])
+        scatter_on_scalar(FAR, 1, far_packed[1])
+        leave_on_scalar(far_packed[2], banks[FAR, 2][:])
+        w3_codes, w3_scales = quantise("w3", w3_grouped[:].rearrange("p m j -> p (m j)"))
+        scatter_on_vector(FAR, 2, 0, far_packed[2])
+        leave_on_scalar(far_packed[3], banks[FAR, 3][:])
+        scatter_on_scalar(FAR, 3, far_packed[3])
+
+        near_pairs = keep.tile([P, 2, S, 2], BF16, name="near_pairs", tag="w2_raw1", align_bytes=64)
+        far_flat = keep.tile([P, PACK * S], BF16, name="far_pairs", tag="x_row01", align_bytes=64)
         far_pairs = far_flat[:].rearrange("p (c u r v) -> p c u r v", u=2, r=CELLS, v=2)
+        for n in (0, 1, 3, 2):
+            nc.gpsimd.tensor_scalar(near_pairs[:, n // 2, :, n % 2], windows[NEAR][n][:], 1.0, 0.0, MULT, ADD)
 
-        def round_far(t, c0, c1):
-            src = windows[FAR][t][:, c0 * CELLS:c1 * CELLS].rearrange("p (c r) -> p c r", r=CELLS)
-            nc.scalar.activation(far_pairs[:, c0:c1, t // 2, :, t % 2], src, COPY)
+        def far_window(n, c0, c1):
+            return (far_pairs[:, c0:c1, n // 2, :, n % 2],
+                    windows[FAR][n][:, c0 * CELLS:c1 * CELLS].rearrange("p (c r) -> p c r", r=CELLS))
 
-        for t in range(PACK - 1):
-            round_far(t, 0, STEPS)
+        for n in (1, 0):
+            nc.gpsimd.tensor_scalar(*far_window(n, 0, STEPS), 1.0, 0.0, MULT, ADD)
+        nc.scalar.activation(*far_window(3, 0, STEPS), COPY)
         for c0, c1 in zip((0,) + LAST_PIECES, LAST_PIECES):
-            round_far(PACK - 1, c0, c1)
+            nc.scalar.activation(*far_window(2, c0, c1), COPY)
 
         out_view = out.rearrange("(h p) r -> p h r", p=P)
-        z_all = keep.tile([P, STEPS * CELLS * PACK], BF16, name="z_all", tag="x_raw000", align_bytes=64)
-        res_all = keep.tile([P, STEPS * 2 * CELLS], F32, name="res_all", tag="x_raw110", align_bytes=64)
+        z_all = keep.tile([P, STEPS * CELLS * PACK], BF16, name="z_all", tag="x_row02", align_bytes=64)
+        res_all = keep.tile([P, STEPS * 2 * CELLS], F32, name="res_all", tag="x_row03", align_bytes=64)
 
         def join(c):
             z = z_all[:, c * CELLS * PACK:(c + 1) * CELLS * PACK]
@@ -297,15 +234,12 @@ def tile_picked_bev_max_e_kernel(tc, xT, w1, w2, w3, offs, near, far, out):
                                     near_pairs[:, :, c * CELLS:(c + 1) * CELLS, :].rearrange("p u r v -> p r u v"), MAX)
 
         def finish(c):
-            z_codes = keep.tile([P, CELLS], U32, name="z_codes%d" % c, align_bytes=64)
-            z_scales = keep.tile([P, CELLS], U8, name="z_scales%d" % c, align_bytes=64)
-            nc.vector.quantize_mx(out=z_codes[:].bitcast(FP8X4), scales=z_scales[:],
-                                  in_=z_all[:, c * CELLS * PACK:(c + 1) * CELLS * PACK])
+            z_codes, z_scales = quantise("z%d" % c, z_all[:, c * CELLS * PACK:(c + 1) * CELLS * PACK])
             last = c == STEPS - 1
             if last:
-                halves = [psum.tile([P, V], F32, name="acc", tag="acc0", bufs=2)[:, 0:CELLS] for h in range(2)]
+                halves = [psum.tile([P, V], F32, name="acc", tag="bank%d" % (PACK + h))[:, 0:CELLS] for h in range(2)]
             else:
-                bank = psum.tile([P, V], F32, name="acc", tag="acc1", bufs=4)
+                bank = psum.tile([P, V], F32, name="acc", tag="bank%d" % (c % PACK))
                 halves = [bank[:, h * CELLS:(h + 1) * CELLS] for h in range(2)]
             for h in range(2):
                 nc.tensor.matmul_mx(

@@ -27,7 +27,7 @@ NEAR, FAR = 0, 1
 PIECE = V // 2
 CELLS = 128
 STEPS = S // CELLS
-LAST_PIECES = (1, 2, 4, STEPS)
+LAST_PIECES = (2, STEPS)
 
 
 def tile_picked_bev_max_e_kernel(tc, xT, w1, w2, w3, offs, near, far, out):
@@ -46,9 +46,9 @@ def tile_picked_bev_max_e_kernel(tc, xT, w1, w2, w3, offs, near, far, out):
             for n in range(PACK):
                 (nc.vector, nc.gpsimd)[s].memset(windows[s][n][:], 0.0)
 
-        def quantise(name, grouped):
+        def quantise(name, grouped, tag=None):
             width = grouped.shape[1] // PACK
-            codes = keep.tile([P, width], U32, name="codes_" + name, align_bytes=64)
+            codes = keep.tile([P, width], U32, name="codes_" + name, tag=tag or "codes_" + name, align_bytes=64)
             scales = keep.tile([P, width], U8, name="scales_" + name, align_bytes=64)
             nc.vector.quantize_mx(out=codes[:].bitcast(FP8X4), scales=scales[:], in_=grouped)
             return codes, scales
@@ -66,6 +66,9 @@ def tile_picked_bev_max_e_kernel(tc, xT, w1, w2, w3, offs, near, far, out):
                     nc.sync.dma_start(offs_sb[:], offs)
                 nc.vector.tensor_copy(woven[g][:, 0:V, j], row[:].indirect(offs_sb[:, 0:LIST_COLS]))
                 nc.scalar.activation(planes[g][:, j, :], row[:].indirect(offs_sb[:, LIST_COLS:]), COPY)
+                if g == 1 and j == 1:
+                    nc.gpsimd.tensor_scalar(woven[1][:, V:, 0:2], planes[1][:, 0:2, :].rearrange("p j v -> p v j"),
+                                            1.0, 0.0, MULT, ADD)
             if g == 0:
                 nc.gpsimd.tensor_scalar(woven[0][:, V:, :], planes[0][:].rearrange("p j v -> p v j"),
                                         1.0, 0.0, MULT, ADD)
@@ -74,8 +77,7 @@ def tile_picked_bev_max_e_kernel(tc, xT, w1, w2, w3, offs, near, far, out):
                     x_ops[0, s] = (codes[:, s * V:(s + 1) * V], scales[:, s * V:(s + 1) * V])
         codes, scales = quantise("x10", woven[1][:, 0:V, :].rearrange("p v j -> p (v j)"))
         x_ops[1, NEAR] = (codes[:], scales[:])
-        nc.scalar.copy(woven[1][:, V:, :].rearrange("p (c e) j -> p c j e", e=RUN),
-                       planes[1][:].rearrange("p j (c e) -> p c j e", e=RUN))
+        nc.scalar.copy(woven[1][:, V:, 2:4], planes[1][:, 2:4, :].rearrange("p j v -> p v j"))
 
         def load_pass(src, g, name):
             raw = keep.tile([P, PACK, H], F32, name=name, tag=name, align_bytes=64)
@@ -144,26 +146,26 @@ def tile_picked_bev_max_e_kernel(tc, xT, w1, w2, w3, offs, near, far, out):
 
         low = grouped_tile("w1_00", 2)
         deal(nc.vector.tensor_copy, low[:], w1_raw[0], 0, 2)
-        high = grouped_tile("w1_02", 2)
-        deal(nc.scalar.copy, high[:], w1_raw[0], 2, 4)
+        high = grouped_tile("w1_high", 4)
+        deal(nc.scalar.copy, high[:, 0:2 * K_PASS], w1_raw[0], 2, 4)
         quantise_weights(NEAR, 0, 0, 2, low[:])
         multiply(NEAR, 0, 0)
         multiply(NEAR, 0, 1)
-        codes, scales = quantise("x11", woven[1][:, V:, :].rearrange("p v j -> p (v j)"))
+        codes, scales = quantise("x11", woven[1][:, V:, :].rearrange("p v j -> p (v j)"), "w1_raw0")
         x_ops[1, FAR] = (codes[:], scales[:])
         first = grouped_tile("w1_10", 1)
         deal(nc.vector.tensor_copy, first[:], w1_raw[1], 0, 1)
         second = grouped_tile("w1_11", 1)
         deal(nc.scalar.copy, second[:], w1_raw[1], 1, 2)
-        quantise_weights(NEAR, 0, 2, 4, high[:])
         quantise_weights(NEAR, 1, 0, 1, first[:])
         multiply(NEAR, 1, 0)
         quantise_weights(NEAR, 1, 1, 2, second[:])
         multiply(NEAR, 1, 1)
-        rest = grouped_tile("w1_12", 2)
-        deal(nc.vector.tensor_copy, rest[:, 0:K_PASS], w1_raw[1], 2, 3)
-        deal(nc.scalar.copy, rest[:, K_PASS:], w1_raw[1], 3, 4)
-        quantise_weights(NEAR, 1, 2, 4, rest[:])
+        deal(nc.vector.tensor_copy, high[:, 2 * K_PASS:3 * K_PASS], w1_raw[1], 2, 3)
+        deal(nc.scalar.copy, high[:, 3 * K_PASS:], w1_raw[1], 3, 4)
+        codes, scales = quantise("w1_high", high[:])
+        for place, (g, n) in enumerate(((0, 2), (0, 3), (1, 2), (1, 3))):
+            w_ops[NEAR, g, n] = (codes[:, place * P:(place + 1) * P], scales[:, place * P:(place + 1) * P])
         for g in range(PASSES):
             multiply(NEAR, g, 3)
         for g in range(PASSES):
@@ -177,51 +179,46 @@ def tile_picked_bev_max_e_kernel(tc, xT, w1, w2, w3, offs, near, far, out):
             leave_on_scalar(packed, banks[NEAR, n][:])
             scatter_on_scalar(NEAR, n, packed)
 
-        w2_first = grouped_tile("w2_00", PACK)
+        w2_first = grouped_tile("w2_grouped", PACK)
         deal_on_gpsimd(w2_first[:], w2_raw[0], 0, PACK)
         quantise_weights(FAR, 0, 0, PACK, w2_first[:])
         for n in (1, 0, 2, 3):
             multiply(FAR, 0, n)
-        for half in range(2):
-            name = "w2_1%d" % half
-            grouped = grouped_tile(name, 2)
-            deal_on_gpsimd(grouped[:], w2_raw[1], 2 * half, 2 * half + 2)
-            quantise_weights(FAR, 1, 2 * half, 2 * half + 2, grouped[:])
-            for n in ((1, 0), (2, 3))[half]:
-                multiply(FAR, 1, n)
-            packed = packed_tile("near2%d" % half, PIECE, name)
-            leave_on_vector(packed, banks[NEAR, 2][:, half * PIECE:(half + 1) * PIECE])
-            scatter_on_vector(NEAR, 2, half * PIECE, packed)
+        w2_second = grouped_tile("w2_grouped", PACK)
+        deal(nc.vector.tensor_copy, w2_second[:], w2_raw[1], 0, PACK)
+        packed = packed_tile("near2", V, "w2_raw1")
+        leave_on_vector(packed, banks[NEAR, 2][:])
+        quantise_weights(FAR, 1, 0, PACK, w2_second[:])
+        for n in (1, 0, 2, 3):
+            multiply(FAR, 1, n)
+        scatter_on_vector(NEAR, 2, 0, packed)
 
-        w3_grouped = keep.tile([P, N, PACK], BF16, name="w3_grouped", align_bytes=64)
-        nc.gpsimd.tensor_scalar(w3_grouped[:], w3_raw[:].rearrange("p n m -> p m n"), 1.0, 0.0, MULT, ADD)
-
-        far_packed = [packed_tile("far%d" % n) for n in range(PACK)]
-        leave_on_vector(far_packed[0], banks[FAR, 0][:])
-        scatter_on_vector(FAR, 0, 0, far_packed[0])
-        leave_on_scalar(far_packed[1], banks[FAR, 1][:])
-        scatter_on_scalar(FAR, 1, far_packed[1])
-        leave_on_scalar(far_packed[2], banks[FAR, 2][:])
-        w3_codes, w3_scales = quantise("w3", w3_grouped[:].rearrange("p m j -> p (m j)"))
-        scatter_on_vector(FAR, 2, 0, far_packed[2])
-        leave_on_scalar(far_packed[3], banks[FAR, 3][:])
-        scatter_on_scalar(FAR, 3, far_packed[3])
-
-        near_pairs = keep.tile([P, 2, S, 2], BF16, name="near_pairs", tag="w2_raw1", align_bytes=64)
         far_flat = keep.tile([P, PACK * S], BF16, name="far_pairs", tag="x_row01", align_bytes=64)
-        far_pairs = far_flat[:].rearrange("p (c u r v) -> p c u r v", u=2, r=CELLS, v=2)
+        far_pairs = far_flat[:].rearrange("p (u r v) -> p u r v", u=2, v=2)
+        far_packed = [packed_tile("far%d" % n) for n in range(PACK)]
+        for pair in ((1, 0), (3, 2)):
+            for n in pair:
+                leave_on_scalar(far_packed[n], banks[FAR, n][:])
+            scatter_on_scalar(FAR, pair[0], far_packed[pair[0]])
+            scatter_on_vector(FAR, pair[1], 0, far_packed[pair[1]])
+
+        w3_grouped = keep.tile([P, N, PACK], BF16, name="w3_grouped", tag="far3", align_bytes=64)
+        nc.scalar.copy(w3_grouped[:].rearrange("p (c e) n -> p c n e", e=RUN),
+                       w3_raw[:].rearrange("p n (c e) -> p c n e", e=RUN))
+
+        near_pairs = keep.tile([P, 2, S, 2], BF16, name="near_pairs", tag="w2_raw0", align_bytes=64)
         for n in (0, 1, 3, 2):
             nc.gpsimd.tensor_scalar(near_pairs[:, n // 2, :, n % 2], windows[NEAR][n][:], 1.0, 0.0, MULT, ADD)
 
         def far_window(n, c0, c1):
-            return (far_pairs[:, c0:c1, n // 2, :, n % 2],
-                    windows[FAR][n][:, c0 * CELLS:c1 * CELLS].rearrange("p (c r) -> p c r", r=CELLS))
+            cells = slice(c0 * CELLS, c1 * CELLS)
+            return far_pairs[:, n // 2, cells, n % 2], windows[FAR][n][:, cells]
 
         for n in (1, 0):
             nc.gpsimd.tensor_scalar(*far_window(n, 0, STEPS), 1.0, 0.0, MULT, ADD)
-        nc.scalar.activation(*far_window(3, 0, STEPS), COPY)
+        nc.vector.tensor_copy(*far_window(2, 0, STEPS))
         for c0, c1 in zip((0,) + LAST_PIECES, LAST_PIECES):
-            nc.scalar.activation(*far_window(2, c0, c1), COPY)
+            nc.vector.tensor_copy(*far_window(3, c0, c1))
 
         out_view = out.rearrange("(h p) r -> p h r", p=P)
         z_all = keep.tile([P, STEPS * CELLS * PACK], BF16, name="z_all", tag="x_row02", align_bytes=64)
@@ -230,7 +227,7 @@ def tile_picked_bev_max_e_kernel(tc, xT, w1, w2, w3, offs, near, far, out):
         def join(c):
             z = z_all[:, c * CELLS * PACK:(c + 1) * CELLS * PACK]
             nc.vector.tensor_tensor(z.rearrange("p (r u v) -> p r u v", u=2, v=2),
-                                    far_pairs[:, c].rearrange("p u r v -> p r u v"),
+                                    far_pairs[:, :, c * CELLS:(c + 1) * CELLS, :].rearrange("p u r v -> p r u v"),
                                     near_pairs[:, :, c * CELLS:(c + 1) * CELLS, :].rearrange("p u r v -> p r u v"), MAX)
 
         def finish(c):
@@ -259,5 +256,7 @@ def tile_picked_bev_max_e_kernel(tc, xT, w1, w2, w3, offs, near, far, out):
         join(0)
         for c in range(1, STEPS):
             join(c)
+            if c == 1:
+                w3_codes, w3_scales = quantise("w3", w3_grouped[:].rearrange("p m j -> p (m j)"))
             finish(c - 1)
         finish(STEPS - 1)

@@ -27,7 +27,8 @@ NEAR, FAR = 0, 1
 PIECE = V // 2
 CELLS = 128
 STEPS = S // CELLS
-LAST_PIECES = (2, STEPS)
+LAST_PIECES = (1, 2, 4, STEPS)
+MOST = 384
 
 
 def tile_picked_bev_max_e_kernel(tc, xT, w1, w2, w3, offs, near, far, out):
@@ -41,7 +42,8 @@ def tile_picked_bev_max_e_kernel(tc, xT, w1, w2, w3, offs, near, far, out):
         far_sb = keep.tile([P, LIST_COLS], U16, name="far_sb")
         cell_lists = (near_sb, far_sb)
 
-        windows = [[keep.tile([P, S], F32, name="win%d%d" % (s, n)) for n in range(PACK)] for s in (NEAR, FAR)]
+        windows = [[keep.tile([P, S], F32, name="win%d%d" % (s, n), tag="win%d%d" % (s, n), align_bytes=64)
+                    for n in range(PACK)] for s in (NEAR, FAR)]
         for s in (NEAR, FAR):
             for n in range(PACK):
                 (nc.vector, nc.gpsimd)[s].memset(windows[s][n][:], 0.0)
@@ -126,18 +128,23 @@ def tile_picked_bev_max_e_kernel(tc, xT, w1, w2, w3, offs, near, far, out):
             cols = slice(first // 16, (first + packed.shape[1]) // 16)
             nc.vector.tensor_copy(windows[s][n][:].indirect(cell_lists[s][:, cols]), packed)
 
+        def piece_on_scalar(s, n, first, packed):
+            cols = slice(first // 16, (first + packed.shape[1]) // 16)
+            nc.scalar.activation(windows[s][n][:].indirect(cell_lists[s][:, cols]), packed, COPY)
+
         def scatter_on_scalar(s, n, packed):
             for first in range(0, V, PIECE):
-                cols = slice(first // 16, (first + PIECE) // 16)
-                nc.scalar.activation(windows[s][n][:].indirect(cell_lists[s][:, cols]), packed[:, first:first + PIECE],
-                                     COPY)
+                piece_on_scalar(s, n, first, packed[:, first:first + PIECE])
 
         def packed_tile(name, width=V, tag=None):
             return keep.tile([P, width], F32, name=name, tag=tag or name, align_bytes=64)[:]
 
         w1_raw = [load_pass(w1, g, "w1_raw%d" % g) for g in range(PASSES)]
         nc.sync.dma_start(near_sb[:], near)
-        w2_raw = [load_pass(w2, g, "w2_raw%d" % g) for g in range(PASSES)]
+        shared = keep.tile([P, 8 * S], BF16, name="shared", align_bytes=64)
+        w2_raw = [shared[:, 0:4 * S].bitcast(F32).rearrange("p (j w) -> p j w", j=PACK)]
+        nc.sync.dma_start(out=w2_raw[0], in_=w2[0:K_PASS, :].rearrange("(p j) w -> p j w", j=PACK))
+        w2_raw.append(load_pass(w2, 1, "w2_raw1"))
         nc.sync.dma_start(far_sb[:], far)
         w3_raw = keep.tile([P, PACK, N], F32, name="w3_raw", align_bytes=64)
         w3_rows = w3.rearrange("(c n e) m -> e c n m", n=PACK, e=RUN)
@@ -146,24 +153,24 @@ def tile_picked_bev_max_e_kernel(tc, xT, w1, w2, w3, offs, near, far, out):
 
         low = grouped_tile("w1_00", 2)
         deal(nc.vector.tensor_copy, low[:], w1_raw[0], 0, 2)
-        high = grouped_tile("w1_high", 4)
+        high = shared[:, 6 * S:]
         deal(nc.scalar.copy, high[:, 0:2 * K_PASS], w1_raw[0], 2, 4)
         quantise_weights(NEAR, 0, 0, 2, low[:])
         multiply(NEAR, 0, 0)
         multiply(NEAR, 0, 1)
-        codes, scales = quantise("x11", woven[1][:, V:, :].rearrange("p v j -> p (v j)"), "w1_raw0")
+        codes, scales = quantise("x11", woven[1][:, V:, :].rearrange("p v j -> p (v j)"), "w1_00")
         x_ops[1, FAR] = (codes[:], scales[:])
         first = grouped_tile("w1_10", 1)
-        deal(nc.vector.tensor_copy, first[:], w1_raw[1], 0, 1)
+        deal(nc.vector.tensor_copy, first[:], w1_raw[1], 1, 2)
         second = grouped_tile("w1_11", 1)
-        deal(nc.scalar.copy, second[:], w1_raw[1], 1, 2)
-        quantise_weights(NEAR, 1, 0, 1, first[:])
-        multiply(NEAR, 1, 0)
-        quantise_weights(NEAR, 1, 1, 2, second[:])
+        deal(nc.scalar.copy, second[:], w1_raw[1], 0, 1)
+        quantise_weights(NEAR, 1, 1, 2, first[:])
         multiply(NEAR, 1, 1)
+        quantise_weights(NEAR, 1, 0, 1, second[:])
+        multiply(NEAR, 1, 0)
         deal(nc.vector.tensor_copy, high[:, 2 * K_PASS:3 * K_PASS], w1_raw[1], 2, 3)
         deal(nc.scalar.copy, high[:, 3 * K_PASS:], w1_raw[1], 3, 4)
-        codes, scales = quantise("w1_high", high[:])
+        codes, scales = quantise("w1_high", high)
         for place, (g, n) in enumerate(((0, 2), (0, 3), (1, 2), (1, 3))):
             w_ops[NEAR, g, n] = (codes[:, place * P:(place + 1) * P], scales[:, place * P:(place + 1) * P])
         for g in range(PASSES):
@@ -174,51 +181,62 @@ def tile_picked_bev_max_e_kernel(tc, xT, w1, w2, w3, offs, near, far, out):
         packed = packed_tile("near0")
         leave_on_vector(packed, banks[NEAR, 0][:])
         scatter_on_vector(NEAR, 0, 0, packed)
-        for n in (1, 3):
-            packed = packed_tile("near%d" % n)
-            leave_on_scalar(packed, banks[NEAR, n][:])
-            scatter_on_scalar(NEAR, n, packed)
-
-        w2_first = grouped_tile("w2_grouped", PACK)
-        deal_on_gpsimd(w2_first[:], w2_raw[0], 0, PACK)
-        quantise_weights(FAR, 0, 0, PACK, w2_first[:])
-        for n in (1, 0, 2, 3):
-            multiply(FAR, 0, n)
-        w2_second = grouped_tile("w2_grouped", PACK)
-        deal(nc.vector.tensor_copy, w2_second[:], w2_raw[1], 0, PACK)
-        packed = packed_tile("near2", V, "w2_raw1")
-        leave_on_vector(packed, banks[NEAR, 2][:])
-        quantise_weights(FAR, 1, 0, PACK, w2_second[:])
-        for n in (1, 0, 2, 3):
-            multiply(FAR, 1, n)
+        packed = packed_tile("near1")
+        leave_on_scalar(packed, banks[NEAR, 1][:])
+        scatter_on_scalar(NEAR, 1, packed)
+        packed = packed_tile("near2", PIECE)
+        leave_on_scalar(packed, banks[NEAR, 2][:, 0:PIECE])
         scatter_on_vector(NEAR, 2, 0, packed)
+
+        near_pairs = shared[:, 2 * S:6 * S].rearrange("p (u r v) -> p u r v", u=2, v=2)
+        w2_grouped = (shared[:, 6 * S:], shared[:, 4 * S:6 * S])
+        deal_on_gpsimd(w2_grouped[0], w2_raw[0], 0, PACK)
+        deal(nc.scalar.copy, w2_grouped[1], w2_raw[1], 0, PACK)
+        w3_grouped = keep.tile([P, N, PACK], BF16, name="w3_grouped", align_bytes=64)
+        nc.vector.tensor_copy(w3_grouped[:].rearrange("p (c e) (u v) -> p c u v e", e=RUN, u=2),
+                              w3_raw[:].rearrange("p (v u) (c e) -> p c u v e", e=RUN, u=2))
+        quantise_weights(FAR, 0, 0, PACK, w2_grouped[0])
+        for n in range(PACK):
+            multiply(FAR, 0, n)
+        late = packed_tile("late", V + PIECE, "w2_raw1")
+        leave_on_vector(late[:, V:], banks[NEAR, 2][:, PIECE:])
+        w3_codes, w3_scales = quantise("w3", w3_grouped[:].rearrange("p m j -> p (m j)"))
+        quantise_weights(FAR, 1, 0, PACK, w2_grouped[1])
+        for n in range(PACK):
+            multiply(FAR, 1, n)
+        scatter_on_vector(NEAR, 2, PIECE, late[:, V:])
+        leave_on_scalar(late[:, 0:V], banks[NEAR, 3][:])
+        scatter_on_scalar(NEAR, 3, late[:, 0:V])
 
         far_flat = keep.tile([P, PACK * S], BF16, name="far_pairs", tag="x_row01", align_bytes=64)
         far_pairs = far_flat[:].rearrange("p (u r v) -> p u r v", u=2, v=2)
-        far_packed = [packed_tile("far%d" % n) for n in range(PACK)]
-        for pair in ((1, 0), (3, 2)):
-            for n in pair:
-                leave_on_scalar(far_packed[n], banks[FAR, n][:])
-            scatter_on_scalar(FAR, pair[0], far_packed[pair[0]])
-            scatter_on_vector(FAR, pair[1], 0, far_packed[pair[1]])
+        both = packed_tile("far13", MOST + PIECE)
+        far_packed = [packed_tile("far0"), both[:, MOST - PIECE:], packed_tile("far2"), both[:, 0:MOST]]
+        for n in (0, 2):
+            leave_on_vector(far_packed[n], banks[FAR, n][:])
+        leave_on_scalar(far_packed[1], banks[FAR, 1][:])
+        for n in (0, 2):
+            scatter_on_vector(FAR, n, 0, far_packed[n])
+        piece_on_scalar(FAR, 1, 0, far_packed[1][:, 0:PIECE])
+        leave_on_scalar(far_packed[3], banks[FAR, 3][:, 0:MOST])
+        piece_on_scalar(FAR, 1, PIECE, far_packed[1][:, PIECE:])
+        piece_on_scalar(FAR, 3, 0, far_packed[3])
 
-        w3_grouped = keep.tile([P, N, PACK], BF16, name="w3_grouped", tag="far3", align_bytes=64)
-        nc.scalar.copy(w3_grouped[:].rearrange("p (c e) n -> p c n e", e=RUN),
-                       w3_raw[:].rearrange("p n (c e) -> p c n e", e=RUN))
-
-        near_pairs = keep.tile([P, 2, S, 2], BF16, name="near_pairs", tag="w2_raw0", align_bytes=64)
-        for n in (0, 1, 3, 2):
-            nc.gpsimd.tensor_scalar(near_pairs[:, n // 2, :, n % 2], windows[NEAR][n][:], 1.0, 0.0, MULT, ADD)
+        for n in (0, 1, 2, 3):
+            nc.gpsimd.tensor_scalar(near_pairs[:, n % 2, :, n // 2], windows[NEAR][n][:], 1.0, 0.0, MULT, ADD)
 
         def far_window(n, c0, c1):
             cells = slice(c0 * CELLS, c1 * CELLS)
-            return far_pairs[:, n // 2, cells, n % 2], windows[FAR][n][:, cells]
+            return far_pairs[:, n % 2, cells, n // 2], windows[FAR][n][:, cells]
 
-        for n in (1, 0):
-            nc.gpsimd.tensor_scalar(*far_window(n, 0, STEPS), 1.0, 0.0, MULT, ADD)
-        nc.vector.tensor_copy(*far_window(2, 0, STEPS))
+        nc.gpsimd.tensor_scalar(*far_window(1, 0, STEPS), 1.0, 0.0, MULT, ADD)
+        packed = packed_tile("far_last", V - MOST, "win11")
+        leave_on_scalar(packed, banks[FAR, 3][:, MOST:])
+        piece_on_scalar(FAR, 3, MOST, packed)
+        for n in (0, 2):
+            nc.vector.tensor_copy(*far_window(n, 0, STEPS))
         for c0, c1 in zip((0,) + LAST_PIECES, LAST_PIECES):
-            nc.vector.tensor_copy(*far_window(3, c0, c1))
+            nc.scalar.activation(*far_window(3, c0, c1), COPY)
 
         out_view = out.rearrange("(h p) r -> p h r", p=P)
         z_all = keep.tile([P, STEPS * CELLS * PACK], BF16, name="z_all", tag="x_row02", align_bytes=64)
@@ -256,7 +274,5 @@ def tile_picked_bev_max_e_kernel(tc, xT, w1, w2, w3, offs, near, far, out):
         join(0)
         for c in range(1, STEPS):
             join(c)
-            if c == 1:
-                w3_codes, w3_scales = quantise("w3", w3_grouped[:].rearrange("p m j -> p (m j)"))
             finish(c - 1)
         finish(STEPS - 1)

@@ -141,10 +141,8 @@ def tile_picked_bev_max_e_kernel(tc, xT, w1, w2, w3, offs, near, far, out):
 
         w1_raw = [load_pass(w1, g, "w1_raw%d" % g) for g in range(PASSES)]
         nc.sync.dma_start(near_sb[:], near)
-        shared = keep.tile([P, 8 * S], BF16, name="shared", align_bytes=64)
-        w2_raw = [shared[:, 0:4 * S].bitcast(F32).rearrange("p (j w) -> p j w", j=PACK)]
-        nc.sync.dma_start(out=w2_raw[0], in_=w2[0:K_PASS, :].rearrange("(p j) w -> p j w", j=PACK))
-        w2_raw.append(load_pass(w2, 1, "w2_raw1"))
+        shared = keep.tile([P, 6 * S], BF16, name="shared", align_bytes=64)
+        w2_raw = [load_pass(w2, g, "w2_raw%d" % g) for g in range(PASSES)]
         nc.sync.dma_start(far_sb[:], far)
         w3_raw = keep.tile([P, PACK, N], F32, name="w3_raw", align_bytes=64)
         w3_rows = w3.rearrange("(c n e) m -> e c n m", n=PACK, e=RUN)
@@ -153,7 +151,7 @@ def tile_picked_bev_max_e_kernel(tc, xT, w1, w2, w3, offs, near, far, out):
 
         low = grouped_tile("w1_00", 2)
         deal(nc.vector.tensor_copy, low[:], w1_raw[0], 0, 2)
-        high = shared[:, 6 * S:]
+        high = shared[:, 4 * S:]
         deal(nc.scalar.copy, high[:, 0:2 * K_PASS], w1_raw[0], 2, 4)
         quantise_weights(NEAR, 0, 0, 2, low[:])
         multiply(NEAR, 0, 0)
@@ -188,8 +186,8 @@ def tile_picked_bev_max_e_kernel(tc, xT, w1, w2, w3, offs, near, far, out):
         leave_on_scalar(packed, banks[NEAR, 2][:, 0:PIECE])
         scatter_on_vector(NEAR, 2, 0, packed)
 
-        near_pairs = shared[:, 2 * S:6 * S].rearrange("p (u r v) -> p u r v", u=2, v=2)
-        w2_grouped = (shared[:, 6 * S:], shared[:, 4 * S:6 * S])
+        near_pairs = shared[:, 0:4 * S].rearrange("p (u r v) -> p u r v", u=2, v=2)
+        w2_grouped = (shared[:, 4 * S:], shared[:, S:3 * S])
         deal_on_gpsimd(w2_grouped[0], w2_raw[0], 0, PACK)
         deal(nc.scalar.copy, w2_grouped[1], w2_raw[1], 0, PACK)
         w3_grouped = keep.tile([P, N, PACK], BF16, name="w3_grouped", align_bytes=64)
@@ -206,19 +204,20 @@ def tile_picked_bev_max_e_kernel(tc, xT, w1, w2, w3, offs, near, far, out):
             multiply(FAR, 1, n)
         scatter_on_vector(NEAR, 2, PIECE, late[:, V:])
         leave_on_scalar(late[:, 0:V], banks[NEAR, 3][:])
-        scatter_on_scalar(NEAR, 3, late[:, 0:V])
+        piece_on_scalar(NEAR, 3, 0, late[:, 0:MOST])
+        scatter_on_vector(NEAR, 3, MOST, late[:, MOST:V])
 
         far_flat = keep.tile([P, PACK * S], BF16, name="far_pairs", tag="x_row01", align_bytes=64)
         far_pairs = far_flat[:].rearrange("p (u r v) -> p u r v", u=2, v=2)
-        both = packed_tile("far13", MOST + PIECE)
-        far_packed = [packed_tile("far0"), both[:, MOST - PIECE:], packed_tile("far2"), both[:, 0:MOST]]
+        both = packed_tile("far13")
+        far_packed = [packed_tile("far0"), both, packed_tile("far2"), both[:, 0:PIECE]]
         for n in (0, 2):
             leave_on_vector(far_packed[n], banks[FAR, n][:])
         leave_on_scalar(far_packed[1], banks[FAR, 1][:])
         for n in (0, 2):
             scatter_on_vector(FAR, n, 0, far_packed[n])
         piece_on_scalar(FAR, 1, 0, far_packed[1][:, 0:PIECE])
-        leave_on_scalar(far_packed[3], banks[FAR, 3][:, 0:MOST])
+        leave_on_scalar(far_packed[3], banks[FAR, 3][:, 0:PIECE])
         piece_on_scalar(FAR, 1, PIECE, far_packed[1][:, PIECE:])
         piece_on_scalar(FAR, 3, 0, far_packed[3])
 
@@ -229,10 +228,10 @@ def tile_picked_bev_max_e_kernel(tc, xT, w1, w2, w3, offs, near, far, out):
             cells = slice(c0 * CELLS, c1 * CELLS)
             return far_pairs[:, n % 2, cells, n // 2], windows[FAR][n][:, cells]
 
-        nc.gpsimd.tensor_scalar(*far_window(1, 0, STEPS), 1.0, 0.0, MULT, ADD)
-        packed = packed_tile("far_last", V - MOST, "win11")
-        leave_on_scalar(packed, banks[FAR, 3][:, MOST:])
-        piece_on_scalar(FAR, 3, MOST, packed)
+        nc.scalar.activation(*far_window(1, 0, STEPS), COPY)
+        packed = packed_tile("far_last", PIECE, "win11")
+        leave_on_scalar(packed, banks[FAR, 3][:, PIECE:])
+        piece_on_scalar(FAR, 3, PIECE, packed)
         for n in (0, 2):
             nc.vector.tensor_copy(*far_window(n, 0, STEPS))
         for c0, c1 in zip((0,) + LAST_PIECES, LAST_PIECES):

@@ -101,11 +101,14 @@ def tile_picked_bev_max_e_kernel(tc, xT, w1, w2, w3, offs, near, far, out):
             return keep.tile([P, tiles * K_PASS], BF16, name=name, tag=name, align_bytes=64)
 
         w_ops = {}
-        banks = {(s, n): psum.tile([P, V], F32, name="acc", tag="bank%d" % (PACK * s + n))
-                 for s in (NEAR, FAR) for n in range(PACK)}
+        def bank(b):
+            return psum.tile([P, V], F32, name="acc", tag="bank%d" % b)
 
-        def quantise_weights(s, g, n0, n1, grouped):
-            codes, scales = quantise("w%d%d%d" % (s, g, n0), grouped)
+        half_banks = {(n, h): bank(2 * n + h)[:, 0:PIECE] for n in range(2) for h in range(2)}
+        banks = {(NEAR, 2): bank(4), (NEAR, 3): bank(5), (FAR, 0): bank(6), (FAR, 1): bank(7)}
+
+        def quantise_weights(s, g, n0, n1, grouped, tag=None):
+            codes, scales = quantise("w%d%d%d" % (s, g, n0), grouped, tag)
             for n in range(n0, n1):
                 cols = slice((n - n0) * P, (n - n0 + 1) * P)
                 w_ops[s, g, n] = (codes[:, cols], scales[:, cols])
@@ -117,6 +120,16 @@ def tile_picked_bev_max_e_kernel(tc, xT, w1, w2, w3, offs, near, far, out):
                 rhs=x_ops[g, s][0].bitcast(FP8X4), rhs_scale=x_ops[g, s][1],
                 start=(g == 0), stop=(g == PASSES - 1),
             )
+
+        def multiply_in_halves(g, n):
+            for h in range(2):
+                entries = slice(h * PIECE, (h + 1) * PIECE)
+                nc.tensor.matmul_mx(
+                    out=half_banks[n, h],
+                    lhsT=w_ops[NEAR, g, n][0].bitcast(FP8X4), lhsT_scale=w_ops[NEAR, g, n][1],
+                    rhs=x_ops[g, NEAR][0][:, entries].bitcast(FP8X4), rhs_scale=x_ops[g, NEAR][1][:, entries],
+                    start=(g == 0), stop=(g == PASSES - 1),
+                )
 
         def leave_on_vector(packed, acc):
             nc.vector.tensor_scalar_max(packed, acc, 0.0)
@@ -141,21 +154,20 @@ def tile_picked_bev_max_e_kernel(tc, xT, w1, w2, w3, offs, near, far, out):
 
         w1_raw = [load_pass(w1, g, "w1_raw%d" % g) for g in range(PASSES)]
         nc.sync.dma_start(near_sb[:], near)
-        shared = keep.tile([P, 6 * S], BF16, name="shared", align_bytes=64)
         w2_raw = [load_pass(w2, g, "w2_raw%d" % g) for g in range(PASSES)]
         nc.sync.dma_start(far_sb[:], far)
-        w3_raw = keep.tile([P, PACK, N], F32, name="w3_raw", align_bytes=64)
+        w3_raw = keep.tile([P, PACK, N], F32, name="w3_raw", tag="w3_raw", align_bytes=64)[:]
         w3_rows = w3.rearrange("(c n e) m -> e c n m", n=PACK, e=RUN)
         for e in range(RUN):
             nc.sync.dma_start(out=w3_raw[e:P:RUN], in_=w3_rows[e])
 
         low = grouped_tile("w1_00", 2)
         deal(nc.vector.tensor_copy, low[:], w1_raw[0], 0, 2)
-        high = shared[:, 4 * S:]
+        high = grouped_tile("w1_high", PACK)[:]
         deal(nc.scalar.copy, high[:, 0:2 * K_PASS], w1_raw[0], 2, 4)
         quantise_weights(NEAR, 0, 0, 2, low[:])
-        multiply(NEAR, 0, 0)
-        multiply(NEAR, 0, 1)
+        multiply_in_halves(0, 1)
+        multiply_in_halves(0, 0)
         codes, scales = quantise("x11", woven[1][:, V:, :].rearrange("p v j -> p (v j)"), "w1_00")
         x_ops[1, FAR] = (codes[:], scales[:])
         first = grouped_tile("w1_10", 1)
@@ -163,54 +175,56 @@ def tile_picked_bev_max_e_kernel(tc, xT, w1, w2, w3, offs, near, far, out):
         second = grouped_tile("w1_11", 1)
         deal(nc.scalar.copy, second[:], w1_raw[1], 0, 1)
         quantise_weights(NEAR, 1, 1, 2, first[:])
-        multiply(NEAR, 1, 1)
+        multiply_in_halves(1, 1)
         quantise_weights(NEAR, 1, 0, 1, second[:])
-        multiply(NEAR, 1, 0)
+        multiply_in_halves(1, 0)
         deal(nc.vector.tensor_copy, high[:, 2 * K_PASS:3 * K_PASS], w1_raw[1], 2, 3)
         deal(nc.scalar.copy, high[:, 3 * K_PASS:], w1_raw[1], 3, 4)
         codes, scales = quantise("w1_high", high)
         for place, (g, n) in enumerate(((0, 2), (0, 3), (1, 2), (1, 3))):
             w_ops[NEAR, g, n] = (codes[:, place * P:(place + 1) * P], scales[:, place * P:(place + 1) * P])
-        for g in range(PASSES):
-            multiply(NEAR, g, 3)
-        for g in range(PASSES):
-            multiply(NEAR, g, 2)
+        for n in (2, 3):
+            for g in range(PASSES):
+                multiply(NEAR, g, n)
 
-        packed = packed_tile("near0")
-        leave_on_vector(packed, banks[NEAR, 0][:])
-        scatter_on_vector(NEAR, 0, 0, packed)
-        packed = packed_tile("near1")
-        leave_on_scalar(packed, banks[NEAR, 1][:])
-        scatter_on_scalar(NEAR, 1, packed)
-        packed = packed_tile("near2", PIECE)
-        leave_on_scalar(packed, banks[NEAR, 2][:, 0:PIECE])
-        scatter_on_vector(NEAR, 2, 0, packed)
+        packed = [packed_tile("near%d" % n) for n in range(2)]
+        for h in range(2):
+            leave_on_vector(packed[0][:, h * PIECE:(h + 1) * PIECE], half_banks[0, h])
+            leave_on_scalar(packed[1][:, h * PIECE:(h + 1) * PIECE], half_banks[1, h])
+        scatter_on_vector(NEAR, 0, 0, packed[0])
+        scatter_on_scalar(NEAR, 1, packed[1])
+        banks[FAR, 2] = bank(2)
+        banks[FAR, 3] = bank(3)
+        near2 = packed_tile("near2", PIECE)
+        leave_on_scalar(near2, banks[NEAR, 2][:, 0:PIECE])
+        scatter_on_vector(NEAR, 2, 0, near2)
 
-        near_pairs = shared[:, 0:4 * S].rearrange("p (u r v) -> p u r v", u=2, v=2)
-        w2_grouped = (shared[:, 4 * S:], shared[:, S:3 * S])
+        w2_grouped = [grouped_tile("w1_high", PACK)[:], grouped_tile("w2_second", PACK)[:]]
         deal_on_gpsimd(w2_grouped[0], w2_raw[0], 0, PACK)
         deal(nc.scalar.copy, w2_grouped[1], w2_raw[1], 0, PACK)
-        w3_grouped = keep.tile([P, N, PACK], BF16, name="w3_grouped", align_bytes=64)
-        nc.vector.tensor_copy(w3_grouped[:].rearrange("p (c e) (u v) -> p c u v e", e=RUN, u=2),
-                              w3_raw[:].rearrange("p (v u) (c e) -> p c u v e", e=RUN, u=2))
+        near3 = packed_tile("near3", MOST, "w2_raw1")
+        leave_on_scalar(near3, banks[NEAR, 3][:, 0:MOST])
+        piece_on_scalar(NEAR, 3, 0, near3)
         quantise_weights(FAR, 0, 0, PACK, w2_grouped[0])
         for n in range(PACK):
             multiply(FAR, 0, n)
-        late = packed_tile("late", V + PIECE, "w2_raw1")
-        leave_on_vector(late[:, V:], banks[NEAR, 2][:, PIECE:])
-        w3_codes, w3_scales = quantise("w3", w3_grouped[:].rearrange("p m j -> p (m j)"))
-        quantise_weights(FAR, 1, 0, PACK, w2_grouped[1])
+        w3_grouped = keep.tile([P, N * PACK], BF16, name="w3_grouped", tag="w3_grouped", align_bytes=64)
+        nc.vector.tensor_copy(w3_grouped[:].rearrange("p (c e u v) -> p c u v e", e=RUN, u=2, v=2),
+                              w3_raw.rearrange("p (v u) (c e) -> p c u v e", e=RUN, u=2))
+        w3_codes, w3_scales = quantise("w3", w3_grouped[:])
+        late = packed_tile("late", PIECE + V - MOST, "w3_raw")
+        leave_on_vector(late[:, 0:PIECE], banks[NEAR, 2][:, PIECE:])
+        quantise_weights(FAR, 1, 0, PACK, w2_grouped[1], "w3_grouped")
         for n in range(PACK):
             multiply(FAR, 1, n)
-        scatter_on_vector(NEAR, 2, PIECE, late[:, V:])
-        leave_on_scalar(late[:, 0:V], banks[NEAR, 3][:])
-        piece_on_scalar(NEAR, 3, 0, late[:, 0:MOST])
-        scatter_on_vector(NEAR, 3, MOST, late[:, MOST:V])
+        leave_on_vector(late[:, PIECE:], banks[NEAR, 3][:, MOST:])
+        scatter_on_vector(NEAR, 2, PIECE, late[:, 0:PIECE])
+        scatter_on_vector(NEAR, 3, MOST, late[:, PIECE:])
 
         far_flat = keep.tile([P, PACK * S], BF16, name="far_pairs", tag="x_row01", align_bytes=64)
         far_pairs = far_flat[:].rearrange("p (u r v) -> p u r v", u=2, v=2)
         both = packed_tile("far13")
-        far_packed = [packed_tile("far0"), both, packed_tile("far2"), both[:, 0:PIECE]]
+        far_packed = [packed_tile("far0"), both, far_flat[:].bitcast(F32)[:, 0:V], both[:, 0:PIECE]]
         for n in (0, 2):
             leave_on_vector(far_packed[n], banks[FAR, n][:])
         leave_on_scalar(far_packed[1], banks[FAR, 1][:])
@@ -221,7 +235,8 @@ def tile_picked_bev_max_e_kernel(tc, xT, w1, w2, w3, offs, near, far, out):
         piece_on_scalar(FAR, 1, PIECE, far_packed[1][:, PIECE:])
         piece_on_scalar(FAR, 3, 0, far_packed[3])
 
-        for n in (0, 1, 2, 3):
+        near_pairs = keep.tile([P, 2, S, 2], BF16, name="near_pairs", tag="w2_second", align_bytes=64)
+        for n in range(PACK):
             nc.gpsimd.tensor_scalar(near_pairs[:, n % 2, :, n // 2], windows[NEAR][n][:], 1.0, 0.0, MULT, ADD)
 
         def far_window(n, c0, c1):
@@ -251,10 +266,10 @@ def tile_picked_bev_max_e_kernel(tc, xT, w1, w2, w3, offs, near, far, out):
             z_codes, z_scales = quantise("z%d" % c, z_all[:, c * CELLS * PACK:(c + 1) * CELLS * PACK])
             last = c == STEPS - 1
             if last:
-                halves = [psum.tile([P, V], F32, name="acc", tag="bank%d" % (PACK + h))[:, 0:CELLS] for h in range(2)]
+                halves = [bank(6 + h)[:, 0:CELLS] for h in range(2)]
             else:
-                bank = psum.tile([P, V], F32, name="acc", tag="bank%d" % (c % PACK))
-                halves = [bank[:, h * CELLS:(h + 1) * CELLS] for h in range(2)]
+                acc = bank((0, 1, 4, 5)[c % PACK])
+                halves = [acc[:, h * CELLS:(h + 1) * CELLS] for h in range(2)]
             for h in range(2):
                 nc.tensor.matmul_mx(
                     out=halves[h],
@@ -267,7 +282,7 @@ def tile_picked_bev_max_e_kernel(tc, xT, w1, w2, w3, offs, near, far, out):
                 nc.scalar.activation(res[:, 0:CELLS], halves[0], COPY)
                 nc.vector.tensor_copy(res[:, CELLS:2 * CELLS], halves[1])
             else:
-                nc.scalar.activation(res, bank[:, 0:2 * CELLS], COPY)
+                nc.scalar.activation(res, acc[:, 0:2 * CELLS], COPY)
             nc.sync.dma_start(out=out_view[:, :, c * CELLS:(c + 1) * CELLS], in_=res.rearrange("p (h r) -> p h r", h=2))
 
         join(0)

@@ -94,8 +94,7 @@ def tile_picked_bev_max_e_kernel(tc, xT, w1, w2, w3, offs, near, far, out):
         def deal_on_gpsimd(grouped, raw, n0, n1):
             dst = grouped.rearrange("p (n c e j) -> p n c e j", n=n1 - n0, e=RUN, j=PACK)
             src = raw.rearrange("p j (c n e) -> p n c e j", n=PACK, e=RUN)
-            for n in range(n0, n1):
-                nc.gpsimd.tensor_scalar(dst[:, n - n0], src[:, n], 1.0, 0.0, MULT, ADD)
+            nc.gpsimd.tensor_copy(dst, src[:, n0:n1])
 
         def grouped_tile(name, tiles):
             return keep.tile([P, tiles * K_PASS], BF16, name=name, tag=name, align_bytes=64)
@@ -199,32 +198,35 @@ def tile_picked_bev_max_e_kernel(tc, xT, w1, w2, w3, offs, near, far, out):
         leave_on_scalar(near2, banks[NEAR, 2][:, 0:PIECE])
         scatter_on_vector(NEAR, 2, 0, near2)
 
-        w2_grouped = [grouped_tile("w1_high", PACK)[:], grouped_tile("w2_second", PACK)[:]]
-        deal_on_gpsimd(w2_grouped[0], w2_raw[0], 0, PACK)
-        deal(nc.scalar.copy, w2_grouped[1], w2_raw[1], 0, PACK)
-        near3 = packed_tile("near3", MOST, "w2_raw1")
-        leave_on_scalar(near3, banks[NEAR, 3][:, 0:MOST])
-        piece_on_scalar(NEAR, 3, 0, near3)
-        quantise_weights(FAR, 0, 0, PACK, w2_grouped[0])
-        for n in range(PACK):
-            multiply(FAR, 0, n)
-        w3_grouped = keep.tile([P, N * PACK], BF16, name="w3_grouped", tag="w3_grouped", align_bytes=64)
-        nc.vector.tensor_copy(w3_grouped[:].rearrange("p (c e u v) -> p c u v e", e=RUN, u=2, v=2),
+        near3 = packed_tile("near3")
+        leave_on_scalar(near3, banks[NEAR, 3][:])
+        scatter_on_scalar(NEAR, 3, near3)
+
+        with_w3 = grouped_tile("w1_high", PACK + 2)
+        w2_second = grouped_tile("w2_second", PACK)
+        deal_on_gpsimd(with_w3[:, 0:PACK * K_PASS], w2_raw[0], 0, PACK)
+        deal_on_gpsimd(w2_second[:], w2_raw[1], 0, PACK)
+        quantise_weights(FAR, 0, 0, 2, with_w3[:, 0:2 * K_PASS])
+        quantise_weights(FAR, 1, 0, PACK, w2_second[:])
+        for g in range(PASSES):
+            for n in (1, 0):
+                multiply(FAR, g, n)
+        nc.vector.tensor_copy(with_w3[:, PACK * K_PASS:].rearrange("p (c e u v) -> p c u v e", e=RUN, u=2, v=2),
                               w3_raw.rearrange("p (v u) (c e) -> p c u v e", e=RUN, u=2))
-        w3_codes, w3_scales = quantise("w3", w3_grouped[:])
-        late = packed_tile("late", PIECE + V - MOST, "w3_raw")
+        late = packed_tile("late", PIECE + V, "w3_raw")
         leave_on_vector(late[:, 0:PIECE], banks[NEAR, 2][:, PIECE:])
-        quantise_weights(FAR, 1, 0, PACK, w2_grouped[1], "w3_grouped")
-        for n in range(PACK):
-            multiply(FAR, 1, n)
-        leave_on_vector(late[:, PIECE:], banks[NEAR, 3][:, MOST:])
+        codes, scales = quantise("w2_w3", with_w3[:, 2 * K_PASS:])
+        for n in (2, 3):
+            w_ops[FAR, 0, n] = (codes[:, (n - 2) * P:(n - 1) * P], scales[:, (n - 2) * P:(n - 1) * P])
+            for g in range(PASSES):
+                multiply(FAR, g, n)
+        w3_codes, w3_scales = codes[:, 2 * P:], scales[:, 2 * P:]
         scatter_on_vector(NEAR, 2, PIECE, late[:, 0:PIECE])
-        scatter_on_vector(NEAR, 3, MOST, late[:, PIECE:])
 
         far_flat = keep.tile([P, PACK * S], BF16, name="far_pairs", tag="x_row01", align_bytes=64)
         far_pairs = far_flat[:].rearrange("p (u r v) -> p u r v", u=2, v=2)
         both = packed_tile("far13")
-        far_packed = [packed_tile("far0"), both, far_flat[:].bitcast(F32)[:, 0:V], both[:, 0:PIECE]]
+        far_packed = [late[:, PIECE:], both, far_flat[:].bitcast(F32)[:, 0:V], both[:, 0:PIECE]]
         for n in (0, 2):
             leave_on_vector(far_packed[n], banks[FAR, n][:])
         leave_on_scalar(far_packed[1], banks[FAR, 1][:])
@@ -235,7 +237,7 @@ def tile_picked_bev_max_e_kernel(tc, xT, w1, w2, w3, offs, near, far, out):
         piece_on_scalar(FAR, 1, PIECE, far_packed[1][:, PIECE:])
         piece_on_scalar(FAR, 3, 0, far_packed[3])
 
-        near_pairs = keep.tile([P, 2, S, 2], BF16, name="near_pairs", tag="w2_second", align_bytes=64)
+        near_pairs = keep.tile([P, 2, S, 2], BF16, name="near_pairs", tag="w1_high", align_bytes=64)
         for n in range(PACK):
             nc.gpsimd.tensor_scalar(near_pairs[:, n % 2, :, n // 2], windows[NEAR][n][:], 1.0, 0.0, MULT, ADD)
 

@@ -42,11 +42,11 @@ def tile_picked_bev_max_e_kernel(tc, xT, w1, w2, w3, offs, near, far, out):
         far_sb = keep.tile([P, LIST_COLS], U16, name="far_sb")
         cell_lists = (near_sb, far_sb)
 
-        windows = [[keep.tile([P, S], F32, name="win%d%d" % (s, n), tag="win%d%d" % (s, n), align_bytes=64)
-                    for n in range(PACK)] for s in (NEAR, FAR)]
+        windows = [[keep.tile([P, 2 * S if (s, n) == (NEAR, 0) else S], F32, name="win%d%d" % (s, n),
+                              tag="win%d%d" % (s, n), align_bytes=64) for n in range(PACK)] for s in (NEAR, FAR)]
         for s in (NEAR, FAR):
             for n in range(PACK):
-                (nc.vector, nc.gpsimd)[s].memset(windows[s][n][:], 0.0)
+                (nc.vector, nc.gpsimd)[s].memset(windows[s][n][:, 0:S], 0.0)
 
         def quantise(name, grouped, tag=None):
             width = grouped.shape[1] // PACK
@@ -86,10 +86,10 @@ def tile_picked_bev_max_e_kernel(tc, xT, w1, w2, w3, offs, near, far, out):
             nc.sync.dma_start(out=raw[:], in_=src[g * K_PASS:(g + 1) * K_PASS, :].rearrange("(p j) w -> p j w", j=PACK))
             return raw[:]
 
-        def deal(copy, grouped, raw, n0, n1):
-            dst = grouped.rearrange("p (n c e j) -> p n c j e", n=n1 - n0, e=RUN, j=PACK)
+        def deal(copy, grouped, raw, tiles):
+            dst = grouped.rearrange("p (n c e j) -> p n c j e", c=H // 16, e=RUN, j=PACK)
             src = raw.rearrange("p j (c n e) -> p n c j e", n=PACK, e=RUN)
-            copy(dst, src[:, n0:n1])
+            copy(dst, src[:, tiles])
 
         def deal_on_gpsimd(grouped, raw, n0, n1):
             dst = grouped.rearrange("p (n c e j) -> p n c e j", n=n1 - n0, e=RUN, j=PACK)
@@ -103,8 +103,8 @@ def tile_picked_bev_max_e_kernel(tc, xT, w1, w2, w3, offs, near, far, out):
         def bank(b):
             return psum.tile([P, V], F32, name="acc", tag="bank%d" % b)
 
-        half_banks = {(n, h): bank(2 * n + h)[:, 0:PIECE] for n in range(2) for h in range(2)}
-        banks = {(NEAR, 2): bank(4), (NEAR, 3): bank(5), (FAR, 0): bank(6), (FAR, 1): bank(7)}
+        half_banks = {(n, h): bank(n + h)[:, 0:PIECE] for n in (0, 2) for h in range(2)}
+        banks = {(NEAR, 1): bank(4), (NEAR, 3): bank(5), (FAR, 0): bank(6), (FAR, 1): bank(7)}
 
         def quantise_weights(s, g, n0, n1, grouped, tag=None):
             codes, scales = quantise("w%d%d%d" % (s, g, n0), grouped, tag)
@@ -161,42 +161,44 @@ def tile_picked_bev_max_e_kernel(tc, xT, w1, w2, w3, offs, near, far, out):
             nc.sync.dma_start(out=w3_raw[e:P:RUN], in_=w3_rows[e])
 
         low = grouped_tile("w1_00", 2)
-        deal(nc.vector.tensor_copy, low[:], w1_raw[0], 0, 2)
+        deal(nc.vector.tensor_copy, low[:], w1_raw[0], slice(0, PACK, 2))
         high = grouped_tile("w1_high", PACK)[:]
-        deal(nc.scalar.copy, high[:, 0:2 * K_PASS], w1_raw[0], 2, 4)
-        quantise_weights(NEAR, 0, 0, 2, low[:])
-        multiply_in_halves(0, 1)
+        deal(nc.scalar.copy, high[:, 0:2 * K_PASS], w1_raw[0], slice(1, PACK, 2))
+        codes, scales = quantise("w1_low", low[:])
+        for place, n in enumerate((0, 2)):
+            w_ops[NEAR, 0, n] = (codes[:, place * P:(place + 1) * P], scales[:, place * P:(place + 1) * P])
+        multiply_in_halves(0, 2)
         multiply_in_halves(0, 0)
         codes, scales = quantise("x11", woven[1][:, V:, :].rearrange("p v j -> p (v j)"), "w1_00")
         x_ops[1, FAR] = (codes[:], scales[:])
         first = grouped_tile("w1_10", 1)
-        deal(nc.vector.tensor_copy, first[:], w1_raw[1], 1, 2)
+        deal(nc.vector.tensor_copy, first[:], w1_raw[1], slice(2, 3))
         second = grouped_tile("w1_11", 1)
-        deal(nc.scalar.copy, second[:], w1_raw[1], 0, 1)
-        quantise_weights(NEAR, 1, 1, 2, first[:])
-        multiply_in_halves(1, 1)
+        deal(nc.scalar.copy, second[:], w1_raw[1], slice(0, 1))
+        quantise_weights(NEAR, 1, 2, 3, first[:])
+        multiply_in_halves(1, 2)
         quantise_weights(NEAR, 1, 0, 1, second[:])
         multiply_in_halves(1, 0)
-        deal(nc.vector.tensor_copy, high[:, 2 * K_PASS:3 * K_PASS], w1_raw[1], 2, 3)
-        deal(nc.scalar.copy, high[:, 3 * K_PASS:], w1_raw[1], 3, 4)
+        deal(nc.vector.tensor_copy, high[:, 2 * K_PASS:3 * K_PASS], w1_raw[1], slice(1, 2))
+        deal(nc.scalar.copy, high[:, 3 * K_PASS:], w1_raw[1], slice(3, 4))
         codes, scales = quantise("w1_high", high)
-        for place, (g, n) in enumerate(((0, 2), (0, 3), (1, 2), (1, 3))):
+        for place, (g, n) in enumerate(((0, 1), (0, 3), (1, 1), (1, 3))):
             w_ops[NEAR, g, n] = (codes[:, place * P:(place + 1) * P], scales[:, place * P:(place + 1) * P])
-        for n in (2, 3):
+        for n in (1, 3):
             for g in range(PASSES):
                 multiply(NEAR, g, n)
 
-        packed = [packed_tile("near%d" % n) for n in range(2)]
+        packed = {n: packed_tile("near%d" % n) for n in (0, 2)}
         for h in range(2):
             leave_on_vector(packed[0][:, h * PIECE:(h + 1) * PIECE], half_banks[0, h])
-            leave_on_scalar(packed[1][:, h * PIECE:(h + 1) * PIECE], half_banks[1, h])
+            leave_on_scalar(packed[2][:, h * PIECE:(h + 1) * PIECE], half_banks[2, h])
         scatter_on_vector(NEAR, 0, 0, packed[0])
-        scatter_on_scalar(NEAR, 1, packed[1])
+        scatter_on_scalar(NEAR, 2, packed[2])
         banks[FAR, 2] = bank(2)
         banks[FAR, 3] = bank(3)
-        near2 = packed_tile("near2", PIECE)
-        leave_on_scalar(near2, banks[NEAR, 2][:, 0:PIECE])
-        scatter_on_vector(NEAR, 2, 0, near2)
+        near1 = packed_tile("near1", PIECE)
+        leave_on_scalar(near1, banks[NEAR, 1][:, 0:PIECE])
+        scatter_on_vector(NEAR, 1, 0, near1)
 
         near3 = packed_tile("near3")
         leave_on_scalar(near3, banks[NEAR, 3][:])
@@ -209,46 +211,47 @@ def tile_picked_bev_max_e_kernel(tc, xT, w1, w2, w3, offs, near, far, out):
         quantise_weights(FAR, 0, 0, 2, with_w3[:, 0:2 * K_PASS])
         quantise_weights(FAR, 1, 0, PACK, w2_second[:])
         for g in range(PASSES):
-            for n in (1, 0):
+            for n in range(2):
                 multiply(FAR, g, n)
         nc.vector.tensor_copy(with_w3[:, PACK * K_PASS:].rearrange("p (c e u v) -> p c u v e", e=RUN, u=2, v=2),
                               w3_raw.rearrange("p (v u) (c e) -> p c u v e", e=RUN, u=2))
-        late = packed_tile("late", PIECE + V, "w3_raw")
-        leave_on_vector(late[:, 0:PIECE], banks[NEAR, 2][:, PIECE:])
+        late = packed_tile("late", MOST + 2 * V, "w3_raw")
+        leave_on_vector(late[:, 0:PIECE], banks[NEAR, 1][:, PIECE:])
         codes, scales = quantise("w2_w3", with_w3[:, 2 * K_PASS:])
         for n in (2, 3):
             w_ops[FAR, 0, n] = (codes[:, (n - 2) * P:(n - 1) * P], scales[:, (n - 2) * P:(n - 1) * P])
             for g in range(PASSES):
                 multiply(FAR, g, n)
         w3_codes, w3_scales = codes[:, 2 * P:], scales[:, 2 * P:]
-        scatter_on_vector(NEAR, 2, PIECE, late[:, 0:PIECE])
+        scatter_on_vector(NEAR, 1, PIECE, late[:, 0:PIECE])
 
         far_flat = keep.tile([P, PACK * S], BF16, name="far_pairs", tag="x_row01", align_bytes=64)
         far_pairs = far_flat[:].rearrange("p (u r v) -> p u r v", u=2, v=2)
-        both = packed_tile("far13")
-        far_packed = [late[:, PIECE:], both, far_flat[:].bitcast(F32)[:, 0:V], both[:, 0:PIECE]]
-        for n in (0, 2):
-            leave_on_vector(far_packed[n], banks[FAR, n][:])
-        leave_on_scalar(far_packed[1], banks[FAR, 1][:])
+        both = late[:, PIECE + V:]
+        far_packed = [late[:, PIECE:PIECE + V], both[:, MOST - PIECE:], far_flat[:].bitcast(F32)[:, 0:V], both[:, 0:MOST]]
+        for n in range(3):
+            leave_on_scalar(far_packed[n], banks[FAR, n][:])
         for n in (0, 2):
             scatter_on_vector(FAR, n, 0, far_packed[n])
         piece_on_scalar(FAR, 1, 0, far_packed[1][:, 0:PIECE])
-        leave_on_scalar(far_packed[3], banks[FAR, 3][:, 0:PIECE])
+        leave_on_scalar(far_packed[3], banks[FAR, 3][:, 0:MOST])
         piece_on_scalar(FAR, 1, PIECE, far_packed[1][:, PIECE:])
         piece_on_scalar(FAR, 3, 0, far_packed[3])
 
         near_pairs = keep.tile([P, 2, S, 2], BF16, name="near_pairs", tag="w1_high", align_bytes=64)
-        for n in range(PACK):
-            nc.gpsimd.tensor_scalar(near_pairs[:, n % 2, :, n // 2], windows[NEAR][n][:], 1.0, 0.0, MULT, ADD)
+        nc.sync.dma_start(out=windows[NEAR][0][:, S:], in_=windows[NEAR][2][:])
+        nc.gpsimd.tensor_copy(near_pairs[:, 0], windows[NEAR][0][:].rearrange("p (v r) -> p r v", v=2))
+        for n in (3, 1):
+            nc.gpsimd.tensor_scalar(near_pairs[:, 1, :, n // 2], windows[NEAR][n][:], 1.0, 0.0, MULT, ADD)
 
         def far_window(n, c0, c1):
             cells = slice(c0 * CELLS, c1 * CELLS)
             return far_pairs[:, n % 2, cells, n // 2], windows[FAR][n][:, cells]
 
-        nc.scalar.activation(*far_window(1, 0, STEPS), COPY)
-        packed = packed_tile("far_last", PIECE, "win11")
-        leave_on_scalar(packed, banks[FAR, 3][:, PIECE:])
-        piece_on_scalar(FAR, 3, PIECE, packed)
+        nc.gpsimd.tensor_scalar(*far_window(1, 0, STEPS), 1.0, 0.0, MULT, ADD)
+        packed = packed_tile("far_last", V - MOST, "win11")
+        leave_on_scalar(packed, banks[FAR, 3][:, MOST:])
+        piece_on_scalar(FAR, 3, MOST, packed)
         for n in (0, 2):
             nc.vector.tensor_copy(*far_window(n, 0, STEPS))
         for c0, c1 in zip((0,) + LAST_PIECES, LAST_PIECES):

@@ -46,7 +46,7 @@ def tile_picked_bev_max_e_kernel(tc, xT, w1, w2, w3, offs, near, far, out):
                               tag="win%d%d" % (s, n), align_bytes=64) for n in range(PACK)] for s in (NEAR, FAR)]
         for s in (NEAR, FAR):
             for n in range(PACK):
-                (nc.vector, nc.gpsimd)[s].memset(windows[s][n][:, 0:S], 0.0)
+                nc.gpsimd.memset(windows[s][n][:, 0:S], 0.0)
 
         def quantise(name, grouped, tag=None):
             width = grouped.shape[1] // PACK

@@ -103,8 +103,10 @@ def tile_picked_bev_max_e_kernel(tc, xT, w1, w2, w3, offs, near, far, out):
         def bank(b):
             return psum.tile([P, V], F32, name="acc", tag="bank%d" % b)
 
-        half_banks = {(n, h): bank(n + h)[:, 0:PIECE] for n in (0, 2) for h in range(2)}
-        banks = {(NEAR, 1): bank(4), (NEAR, 3): bank(5), (FAR, 0): bank(6), (FAR, 1): bank(7)}
+        half_banks = {(n, h): bank(n + h)[:, 0:PIECE] for n, h in ((0, 0), (0, 1), (2, 0))}
+        joint = bank(3)
+        half_banks[2, 1], half_banks[1, 0], half_banks[1, 1] = joint[:, 0:PIECE], joint[:, PIECE:], bank(4)[:, 0:PIECE]
+        banks = {(NEAR, 3): bank(5), (FAR, 0): bank(6), (FAR, 1): bank(7)}
 
         def quantise_weights(s, g, n0, n1, grouped, tag=None):
             codes, scales = quantise("w%d%d%d" % (s, g, n0), grouped, tag)
@@ -120,8 +122,8 @@ def tile_picked_bev_max_e_kernel(tc, xT, w1, w2, w3, offs, near, far, out):
                 start=(g == 0), stop=(g == PASSES - 1),
             )
 
-        def multiply_in_halves(g, n):
-            for h in range(2):
+        def multiply_in_halves(g, n, halves=(0, 1)):
+            for h in halves:
                 entries = slice(h * PIECE, (h + 1) * PIECE)
                 nc.tensor.matmul_mx(
                     out=half_banks[n, h],
@@ -184,24 +186,29 @@ def tile_picked_bev_max_e_kernel(tc, xT, w1, w2, w3, offs, near, far, out):
         codes, scales = quantise("w1_high", high)
         for place, (g, n) in enumerate(((0, 1), (0, 3), (1, 1), (1, 3))):
             w_ops[NEAR, g, n] = (codes[:, place * P:(place + 1) * P], scales[:, place * P:(place + 1) * P])
-        for n in (1, 3):
-            for g in range(PASSES):
-                multiply(NEAR, g, n)
+        for g in range(PASSES):
+            multiply_in_halves(g, 1, (0,))
+        for g in range(PASSES):
+            multiply(NEAR, g, 3)
+        for g in range(PASSES):
+            multiply_in_halves(g, 1, (1,))
 
-        packed = {n: packed_tile("near%d" % n) for n in (0, 2)}
+        near0 = packed_tile("near0")
         for h in range(2):
-            leave_on_vector(packed[0][:, h * PIECE:(h + 1) * PIECE], half_banks[0, h])
-            leave_on_scalar(packed[2][:, h * PIECE:(h + 1) * PIECE], half_banks[2, h])
-        scatter_on_vector(NEAR, 0, 0, packed[0])
-        scatter_on_scalar(NEAR, 2, packed[2])
-        banks[FAR, 2] = bank(2)
-        banks[FAR, 3] = bank(3)
-        near1 = packed_tile("near1", PIECE)
-        leave_on_scalar(near1, banks[NEAR, 1][:, 0:PIECE])
-        scatter_on_vector(NEAR, 1, 0, near1)
-
+            leave_on_vector(near0[:, h * PIECE:(h + 1) * PIECE], half_banks[0, h])
+        for h in range(2):
+            scatter_on_vector(NEAR, 0, h * PIECE, near0[:, h * PIECE:(h + 1) * PIECE])
+        near2 = packed_tile("near2", PIECE)
+        leave_on_scalar(near2, half_banks[2, 0])
+        piece_on_scalar(NEAR, 2, 0, near2)
+        two = packed_tile("two")
+        leave_on_scalar(two, joint[:])
         near3 = packed_tile("near3")
         leave_on_scalar(near3, banks[NEAR, 3][:])
+        piece_on_scalar(NEAR, 2, PIECE, two[:, 0:PIECE])
+        banks[FAR, 2] = bank(2)
+        banks[FAR, 3] = bank(3)
+        scatter_on_vector(NEAR, 1, 0, two[:, PIECE:])
         scatter_on_scalar(NEAR, 3, near3)
 
         with_w3 = grouped_tile("w1_high", PACK + 2)
@@ -216,7 +223,7 @@ def tile_picked_bev_max_e_kernel(tc, xT, w1, w2, w3, offs, near, far, out):
         nc.vector.tensor_copy(with_w3[:, PACK * K_PASS:].rearrange("p (c e u v) -> p c u v e", e=RUN, u=2, v=2),
                               w3_raw.rearrange("p (v u) (c e) -> p c u v e", e=RUN, u=2))
         late = packed_tile("late", MOST + 2 * V, "w3_raw")
-        leave_on_vector(late[:, 0:PIECE], banks[NEAR, 1][:, PIECE:])
+        leave_on_vector(late[:, 0:PIECE], half_banks[1, 1])
         codes, scales = quantise("w2_w3", with_w3[:, 2 * K_PASS:])
         for n in (2, 3):
             w_ops[FAR, 0, n] = (codes[:, (n - 2) * P:(n - 1) * P], scales[:, (n - 2) * P:(n - 1) * P])
@@ -252,8 +259,9 @@ def tile_picked_bev_max_e_kernel(tc, xT, w1, w2, w3, offs, near, far, out):
         packed = packed_tile("far_last", V - MOST, "win11")
         leave_on_scalar(packed, banks[FAR, 3][:, MOST:])
         piece_on_scalar(FAR, 3, MOST, packed)
-        for n in (0, 2):
-            nc.vector.tensor_copy(*far_window(n, 0, STEPS))
+        nc.vector.tensor_copy(*far_window(0, 0, STEPS))
+        for c0 in (0, STEPS // 2):
+            nc.vector.tensor_copy(*far_window(2, c0, c0 + STEPS // 2))
         for c0, c1 in zip((0,) + LAST_PIECES, LAST_PIECES):
             nc.scalar.activation(*far_window(3, c0, c1), COPY)
 

from contextlib import ExitStack

import concourse.mybir as mybir

K, T, S, H, N, V = 1024, 2048, 1024, 512, 256, 512
FLOPS = 2 * K * H * V * 2 + 2 * H * N * S

F32 = mybir.dt.float32
BF16 = mybir.dt.bfloat16
U32 = mybir.dt.uint32
U16 = mybir.dt.uint16
U8 = mybir.dt.uint8
FP8X4 = mybir.dt.float8_e4m3fn_x4
COPY = mybir.ActivationFunctionType.Copy
RELU = mybir.ActivationFunctionType.Relu
MAX = mybir.AluOpType.max
MULT = mybir.AluOpType.mult
ADD = mybir.AluOpType.add

P = 128
PACK = 4
RUN = 4
K_PASS = P * PACK
PASSES = K // K_PASS
LIST_COLS = V // 16
NEAR, FAR = 0, 1
PIECE = V // 2
CELLS = 128
STEPS = S // CELLS
LAST_PIECES = (1, 2, 4, STEPS)
MOST = 384


def tile_picked_bev_max_e_kernel(tc, xT, w1, w2, w3, offs, near, far, out):
    nc = tc.nc
    with ExitStack() as ctx:
        keep = ctx.enter_context(tc.tile_pool(name="keep", bufs=1))
        psum = ctx.enter_context(tc.psum_pool(name="psum", bufs=1))

        offs_sb = keep.tile([P, S // 16], U16, name="offs_sb")
        near_sb = keep.tile([P, LIST_COLS], U16, name="near_sb")
        far_sb = keep.tile([P, LIST_COLS], U16, name="far_sb")
        cell_lists = (near_sb, far_sb)

        windows = [[keep.tile([P, 2 * S if (s, n) == (NEAR, 0) else S], F32, name="win%d%d" % (s, n),
                              tag="win%d%d" % (s, n), align_bytes=64) for n in range(PACK)] for s in (NEAR, FAR)]
        for s in (NEAR, FAR):
            for n in range(PACK):
                nc.gpsimd.memset(windows[s][n][:, 0:S], 0.0)

        def quantise(name, grouped, tag=None):
            width = grouped.shape[1] // PACK
            codes = keep.tile([P, width], U32, name="codes_" + name, tag=tag or "codes_" + name, align_bytes=64)
            scales = keep.tile([P, width], U8, name="scales_" + name, align_bytes=64)
            nc.vector.quantize_mx(out=codes[:].bitcast(FP8X4), scales=scales[:], in_=grouped)
            return codes, scales

        woven = [keep.tile([P, S, PACK], BF16, name="woven%d" % g, align_bytes=64) for g in range(PASSES)]
        planes = [keep.tile([P, PACK, V], BF16, name="planes%d" % g, align_bytes=64) for g in range(PASSES)]
        x_ops = {}
        for g in range(PASSES):
            rows = xT[g * K_PASS:(g + 1) * K_PASS, :].rearrange("(p j) w -> p j w", j=PACK)
            for j in range(PACK):
                tag = "x_row%d%d" % (g, j)
                row = keep.tile([P, T], F32, name=tag, tag=tag, align_bytes=64)
                nc.sync.dma_start(out=row[:], in_=rows[:, j, :])
                if g == 0 and j == 0:
                    nc.sync.dma_start(offs_sb[:], offs)
                nc.vector.tensor_copy(woven[g][:, 0:V, j], row[:].indirect(offs_sb[:, 0:LIST_COLS]))
                nc.scalar.activation(planes[g][:, j, :], row[:].indirect(offs_sb[:, LIST_COLS:]), COPY)
                if g == 1 and j == 1:
                    nc.gpsimd.tensor_scalar(woven[1][:, V:, 0:2], planes[1][:, 0:2, :].rearrange("p j v -> p v j"),
                                            1.0, 0.0, MULT, ADD)
            if g == 0:
                nc.gpsimd.tensor_scalar(woven[0][:, V:, :], planes[0][:].rearrange("p j v -> p v j"),
                                        1.0, 0.0, MULT, ADD)
                codes, scales = quantise("x0", woven[0][:].rearrange("p v j -> p (v j)"))
                for s in (NEAR, FAR):
                    x_ops[0, s] = (codes[:, s * V:(s + 1) * V], scales[:, s * V:(s + 1) * V])
        codes, scales = quantise("x10", woven[1][:, 0:V, :].rearrange("p v j -> p (v j)"))
        x_ops[1, NEAR] = (codes[:], scales[:])
        nc.scalar.copy(woven[1][:, V:, 2:4], planes[1][:, 2:4, :].rearrange("p j v -> p v j"))

        def load_pass(src, g, name):
            raw = keep.tile([P, PACK, H], F32, name=name, tag=name, align_bytes=64)
            nc.sync.dma_start(out=raw[:], in_=src[g * K_PASS:(g + 1) * K_PASS, :].rearrange("(p j) w -> p j w", j=PACK))
            return raw[:]

        def deal(copy, grouped, raw, tiles):
            dst = grouped.rearrange("p (n c e j) -> p n c j e", c=H // 16, e=RUN, j=PACK)
            src = raw.rearrange("p j (c n e) -> p n c j e", n=PACK, e=RUN)
            copy(dst, src[:, tiles])

        def deal_on_gpsimd(grouped, raw, n0, n1):
            dst = grouped.rearrange("p (n c e j) -> p n c e j", n=n1 - n0, e=RUN, j=PACK)
            src = raw.rearrange("p j (c n e) -> p n c e j", n=PACK, e=RUN)
            nc.gpsimd.tensor_copy(dst, src[:, n0:n1])

        def grouped_tile(name, tiles):
            return keep.tile([P, tiles * K_PASS], BF16, name=name, tag=name, align_bytes=64)

        w_ops = {}
        def bank(b):
            return psum.tile([P, V], F32, name="acc", tag="bank%d" % b)

        half_banks = {(n, h): bank(n + h)[:, 0:PIECE] for n, h in ((0, 0), (0, 1), (2, 0))}
        joint = bank(3)
        half_banks[2, 1], half_banks[1, 0], half_banks[1, 1] = joint[:, 0:PIECE], joint[:, PIECE:], bank(4)[:, 0:PIECE]
        banks = {(NEAR, 3): bank(5), (FAR, 0): bank(6), (FAR, 1): bank(7)}

        def quantise_weights(s, g, n0, n1, grouped, tag=None):
            codes, scales = quantise("w%d%d%d" % (s, g, n0), grouped, tag)
            for n in range(n0, n1):
                cols = slice((n - n0) * P, (n - n0 + 1) * P)
                w_ops[s, g, n] = (codes[:, cols], scales[:, cols])

        def multiply(s, g, n):
            nc.tensor.matmul_mx(
                out=banks[s, n][:],
                lhsT=w_ops[s, g, n][0].bitcast(FP8X4), lhsT_scale=w_ops[s, g, n][1],
                rhs=x_ops[g, s][0].bitcast(FP8X4), rhs_scale=x_ops[g, s][1],
                start=(g == 0), stop=(g == PASSES - 1),
            )

        def multiply_in_halves(g, n, halves=(0, 1)):
            for h in halves:
                entries = slice(h * PIECE, (h + 1) * PIECE)
                nc.tensor.matmul_mx(
                    out=half_banks[n, h],
                    lhsT=w_ops[NEAR, g, n][0].bitcast(FP8X4), lhsT_scale=w_ops[NEAR, g, n][1],
                    rhs=x_ops[g, NEAR][0][:, entries].bitcast(FP8X4), rhs_scale=x_ops[g, NEAR][1][:, entries],
                    start=(g == 0), stop=(g == PASSES - 1),
                )

        def leave_on_vector(packed, acc):
            nc.vector.tensor_scalar_max(packed, acc, 0.0)

        def leave_on_scalar(packed, acc):
            nc.scalar.activation(packed, acc, RELU)

        def scatter_on_vector(s, n, first, packed):
            cols = slice(first // 16, (first + packed.shape[1]) // 16)
            nc.vector.tensor_copy(windows[s][n][:].indirect(cell_lists[s][:, cols]), packed)

        def piece_on_scalar(s, n, first, packed):
            cols = slice(first // 16, (first + packed.shape[1]) // 16)
            nc.scalar.activation(windows[s][n][:].indirect(cell_lists[s][:, cols]), packed, COPY)

        def scatter_on_scalar(s, n, packed):
            for first in range(0, V, PIECE):
                piece_on_scalar(s, n, first, packed[:, first:first + PIECE])

        def packed_tile(name, width=V, tag=None):
            return keep.tile([P, width], F32, name=name, tag=tag or name, align_bytes=64)[:]

        w1_raw = [load_pass(w1, g, "w1_raw%d" % g) for g in range(PASSES)]
        nc.sync.dma_start(near_sb[:], near)
        w2_raw = [load_pass(w2, g, "w2_raw%d" % g) for g in range(PASSES)]
        nc.sync.dma_start(far_sb[:], far)
        w3_raw = keep.tile([P, PACK, N], F32, name="w3_raw", tag="w3_raw", align_bytes=64)[:]
        w3_rows = w3.rearrange("(c n e) m -> e c n m", n=PACK, e=RUN)
        for e in range(RUN):
            nc.sync.dma_start(out=w3_raw[e:P:RUN], in_=w3_rows[e])

        low = grouped_tile("w1_00", 2)
        deal(nc.vector.tensor_copy, low[:], w1_raw[0], slice(0, PACK, 2))
        high = grouped_tile("w1_high", PACK)[:]
        deal(nc.scalar.copy, high[:, 0:2 * K_PASS], w1_raw[0], slice(1, PACK, 2))
        codes, scales = quantise("w1_low", low[:])
        for place, n in enumerate((0, 2)):
            w_ops[NEAR, 0, n] = (codes[:, place * P:(place + 1) * P], scales[:, place * P:(place + 1) * P])
        multiply_in_halves(0, 2)
        multiply_in_halves(0, 0)
        codes, scales = quantise("x11", woven[1][:, V:, :].rearrange("p v j -> p (v j)"), "w1_00")
        x_ops[1, FAR] = (codes[:], scales[:])
        first = grouped_tile("w1_10", 1)
        deal(nc.vector.tensor_copy, first[:], w1_raw[1], slice(2, 3))
        second = grouped_tile("w1_11", 1)
        deal(nc.scalar.copy, second[:], w1_raw[1], slice(0, 1))
        quantise_weights(NEAR, 1, 2, 3, first[:])
        multiply_in_halves(1, 2)
        quantise_weights(NEAR, 1, 0, 1, second[:])
        multiply_in_halves(1, 0)
        deal(nc.vector.tensor_copy, high[:, 2 * K_PASS:3 * K_PASS], w1_raw[1], slice(1, 2))
        deal(nc.scalar.copy, high[:, 3 * K_PASS:], w1_raw[1], slice(3, 4))
        codes, scales = quantise("w1_high", high)
        for place, (g, n) in enumerate(((0, 1), (0, 3), (1, 1), (1, 3))):
            w_ops[NEAR, g, n] = (codes[:, place * P:(place + 1) * P], scales[:, place * P:(place + 1) * P])
        for g in range(PASSES):
            multiply_in_halves(g, 1, (0,))
        for g in range(PASSES):
            multiply(NEAR, g, 3)
        for g in range(PASSES):
            multiply_in_halves(g, 1, (1,))

        near0 = packed_tile("near0")
        for h in range(2):
            leave_on_vector(near0[:, h * PIECE:(h + 1) * PIECE], half_banks[0, h])
        for h in range(2):
            scatter_on_vector(NEAR, 0, h * PIECE, near0[:, h * PIECE:(h + 1) * PIECE])
        near2 = packed_tile("near2", PIECE)
        leave_on_scalar(near2, half_banks[2, 0])
        piece_on_scalar(NEAR, 2, 0, near2)
        two = packed_tile("two")
        leave_on_scalar(two, joint[:])
        near3 = packed_tile("near3")
        leave_on_scalar(near3, banks[NEAR, 3][:])
        piece_on_scalar(NEAR, 2, PIECE, two[:, 0:PIECE])
        banks[FAR, 2] = bank(2)
        banks[FAR, 3] = bank(3)
        scatter_on_vector(NEAR, 1, 0, two[:, PIECE:])
        scatter_on_scalar(NEAR, 3, near3)

        with_w3 = grouped_tile("w1_high", PACK + 2)
        w2_second = grouped_tile("w2_second", PACK)
        deal_on_gpsimd(with_w3[:, 0:PACK * K_PASS], w2_raw[0], 0, PACK)
        deal_on_gpsimd(w2_second[:], w2_raw[1], 0, PACK)
        quantise_weights(FAR, 0, 0, 2, with_w3[:, 0:2 * K_PASS])
        quantise_weights(FAR, 1, 0, PACK, w2_second[:])
        for g in range(PASSES):
            for n in range(2):
                multiply(FAR, g, n)
        nc.vector.tensor_copy(with_w3[:, PACK * K_PASS:].rearrange("p (c e u v) -> p c u v e", e=RUN, u=2, v=2),
                              w3_raw.rearrange("p (v u) (c e) -> p c u v e", e=RUN, u=2))
        late = packed_tile("late", MOST + 2 * V, "w3_raw")
        leave_on_vector(late[:, 0:PIECE], half_banks[1, 1])
        codes, scales = quantise("w2_w3", with_w3[:, 2 * K_PASS:])
        for n in (2, 3):
            w_ops[FAR, 0, n] = (codes[:, (n - 2) * P:(n - 1) * P], scales[:, (n - 2) * P:(n - 1) * P])
            for g in range(PASSES):
                multiply(FAR, g, n)
        w3_codes, w3_scales = codes[:, 2 * P:], scales[:, 2 * P:]
        scatter_on_vector(NEAR, 1, PIECE, late[:, 0:PIECE])

        far_flat = keep.tile([P, PACK * S], BF16, name="far_pairs", tag="x_row01", align_bytes=64)
        far_pairs = far_flat[:].rearrange("p (u r v) -> p u r v", u=2, v=2)
        both = late[:, PIECE + V:]
        far_packed = [late[:, PIECE:PIECE + V], both[:, MOST - PIECE:], far_flat[:].bitcast(F32)[:, 0:V], both[:, 0:MOST]]
        for n in range(3):
            leave_on_scalar(far_packed[n], banks[FAR, n][:])
        for n in (0, 2):
            scatter_on_vector(FAR, n, 0, far_packed[n])
        piece_on_scalar(FAR, 1, 0, far_packed[1][:, 0:PIECE])
        leave_on_scalar(far_packed[3], banks[FAR, 3][:, 0:MOST])
        piece_on_scalar(FAR, 1, PIECE, far_packed[1][:, PIECE:])
        piece_on_scalar(FAR, 3, 0, far_packed[3])

        near_pairs = keep.tile([P, 2, S, 2], BF16, name="near_pairs", tag="w1_high", align_bytes=64)
        nc.sync.dma_start(out=windows[NEAR][0][:, S:], in_=windows[NEAR][2][:])
        nc.gpsimd.tensor_copy(near_pairs[:, 0], windows[NEAR][0][:].rearrange("p (v r) -> p r v", v=2))
        for n in (3, 1):
            nc.gpsimd.tensor_scalar(near_pairs[:, 1, :, n // 2], windows[NEAR][n][:], 1.0, 0.0, MULT, ADD)

        def far_window(n, c0, c1):
            cells = slice(c0 * CELLS, c1 * CELLS)
            return far_pairs[:, n % 2, cells, n // 2], windows[FAR][n][:, cells]

        nc.gpsimd.tensor_scalar(*far_window(1, 0, STEPS), 1.0, 0.0, MULT, ADD)
        packed = packed_tile("far_last", V - MOST, "win11")
        leave_on_scalar(packed, banks[FAR, 3][:, MOST:])
        piece_on_scalar(FAR, 3, MOST, packed)
        nc.vector.tensor_copy(*far_window(0, 0, STEPS))
        for c0 in (0, STEPS // 2):
            nc.vector.tensor_copy(*far_window(2, c0, c0 + STEPS // 2))
        for c0, c1 in zip((0,) + LAST_PIECES, LAST_PIECES):
            nc.scalar.activation(*far_window(3, c0, c1), COPY)

        out_view = out.rearrange("(h p) r -> p h r", p=P)
        z_all = keep.tile([P, STEPS * CELLS * PACK], BF16, name="z_all", tag="x_row02", align_bytes=64)
        res_all = keep.tile([P, STEPS * 2 * CELLS], F32, name="res_all", tag="x_row03", align_bytes=64)

        def join(c):
            z = z_all[:, c * CELLS * PACK:(c + 1) * CELLS * PACK]
            nc.vector.tensor_tensor(z.rearrange("p (r u v) -> p r u v", u=2, v=2),
                                    far_pairs[:, :, c * CELLS:(c + 1) * CELLS, :].rearrange("p u r v -> p r u v"),
                                    near_pairs[:, :, c * CELLS:(c + 1) * CELLS, :].rearrange("p u r v -> p r u v"), MAX)

        def finish(c):
            z_codes, z_scales = quantise("z%d" % c, z_all[:, c * CELLS * PACK:(c + 1) * CELLS * PACK])
            last = c == STEPS - 1
            if last:
                halves = [bank(6 + h)[:, 0:CELLS] for h in range(2)]
            else:
                acc = bank((0, 1, 4, 5)[c % PACK])
                halves = [acc[:, h * CELLS:(h + 1) * CELLS] for h in range(2)]
            for h in range(2):
                nc.tensor.matmul_mx(
                    out=halves[h],
                    lhsT=w3_codes[:, h * P:(h + 1) * P].bitcast(FP8X4), lhsT_scale=w3_scales[:, h * P:(h + 1) * P],
                    rhs=z_codes[:].bitcast(FP8X4), rhs_scale=z_scales[:],
                    start=True, stop=True,
                )
            res = res_all[:, c * 2 * CELLS:(c + 1) * 2 * CELLS]
            if last:
                nc.scalar.activation(res[:, 0:CELLS], halves[0], COPY)
                nc.vector.tensor_copy(res[:, CELLS:2 * CELLS], halves[1])
            else:
                nc.scalar.activation(res, acc[:, 0:2 * CELLS], COPY)
            nc.sync.dma_start(out=out_view[:, :, c * CELLS:(c + 1) * CELLS], in_=res.rearrange("p (h r) -> p h r", h=2))

        join(0)
        for c in range(1, STEPS):
            join(c)
            finish(c - 1)
        finish(STEPS - 1)
